import numpy as np, ml_dtypes
CORES = [3,11,19,27,35,43,51,59]
N = 8
import mx_ref
BF = ml_dtypes.bfloat16
def gcols(t, e):
    v = np.concatenate([t.reshape(8, 16, -1, 4), np.zeros((8, 16, 1, 4), BF)], axis=2)
    return np.ascontiguousarray(np.stack([v[g][:, e[g]] for g in range(8)])).reshape(128, -1)
def tile(rs):
    return np.stack(rs, axis=2).reshape(128, -1).astype(BF)
def cut(t, i, w=512):
    return t[:, w * i:w * i + w]
def pick(q, e):
    c = np.concatenate([q[0].reshape(128, -1, 4), np.zeros((128, 1, 4), np.uint8)], axis=1); s = np.concatenate([q[1], np.ones((16, 1), np.uint8)], axis=1)
    return (np.ascontiguousarray(c[:, e].reshape(128, -1)), np.ascontiguousarray(s[:, e]))
def join(*qs):
    return (np.concatenate([q[0] for q in qs], axis=1), np.concatenate([q[1] for q in qs], axis=1))
def put(q, e, v):
    c, s = q[0].reshape(128, -1, 4).copy(), q[1].copy(); c[:, e] = v[0].reshape(128, -1, 4); s[:, e] = v[1]
    return (c.reshape(128, -1), s)
def pk(c, s):
    return (np.ascontiguousarray(c), mx_ref.live(s))
def emit(q):
    return q[0], q[1]
def packed(v, rng):
    q = [mx_ref.quantize(np.ascontiguousarray(v[r])) for r in range(N)]
    return np.stack([a for a, b in q]), np.stack([mx_ref.plane(b, rng) for a, b in q])
def values_of_codes():
    e, c = np.zeros((128, 128, 4), np.float32), np.zeros((128, 2, 4), np.uint8)
    e[np.arange(128), np.arange(128), 0] = 1
    c[:127, :, 0] = np.arange(256).reshape(2, 128).T[:127]
    return mx_ref.matmul(mx_ref.quantize(e.reshape(128, 512).astype(BF)), (c.reshape(128, 8), np.full((16, 2), 127, np.uint8))).T.reshape(-1).astype(np.float64)
CODE_VALUE, SCALE_VALUE = values_of_codes(), 2.0 ** (np.arange(256) - 127.0)
def decode(q):
    return (CODE_VALUE[q[0]].reshape(16, 8, -1, 4) * SCALE_VALUE[q[1]][:, None, :, None] + 0.0).reshape(128, -1).astype(np.float32)
def f(rng, *shape):
    return mx_ref.flush((rng.standard_normal(shape, dtype=np.float32) * np.exp2(rng.integers(-2, 3, shape[:-1] + (1,)))).astype(BF))
def wide(rng, *shape, cols=0):
    v = rng.standard_normal(shape, dtype=np.float32) * np.exp2(rng.integers(-12, 13, shape)).astype(np.float32)
    if cols: v *= np.repeat(np.exp2(rng.integers(-cols, cols + 1, shape[:-2] + (1, shape[-1] // 4))) * (rng.random(shape[:-2] + (1, shape[-1] // 4)) > 0.0625), 4, axis=-1).astype(np.float32)
    return mx_ref.flush(v.astype(BF))
C, K, R = 448, 64, 3
def order(p):
    return np.argsort(-(p[::16] + np.float32(0.0)), axis=1, kind="stable")
def numbers_of(rng):
    return {"x": np.array(f(rng, N, 128, 4 * C)), "u": np.array(f(rng, N, 128, 512)), "v": np.array(f(rng, N, 128, 512))}
def weights(rng, w):
    c, p = packed(w, rng)
    return {"wc": c, "ws": p}
def still(rng):
    w = np.zeros((N, 128, 4, 128, 4), np.float32)
    i = np.arange(128)
    for b in range(4): w[:, i, b, i, b] = 32
    return weights(rng, w.reshape(N, 128, 2048).astype(BF))
def signs(rng):
    return np.stack([rng.permutation(8) % 2 * 2.0 - 1.0 for r in range(N)])
def setup_inputs(rng):
    return {**numbers_of(rng), **weights(rng, f(rng, N, 128, 2048))}
def setup_inputs_ties(rng):
    d = numbers_of(rng)
    e = rng.permutation(N)
    x = d["x"].reshape(N, 8, 16, C, 4)
    for r in range(N):
        k = np.zeros(C, int) if r == e[0] else rng.permutation(C) % 3
        a = x[r][:, :8, :3].copy()
        a[:, :, 2] = 0
        x[r][:, :8] = a[:, :, k]
    x[e[1]] = 0
    u = d["u"].reshape(N, 8, 16, 128, 4)
    u[:, :, 8:, ::16] = 0
    w = np.array(f(rng, N, 128, 2048)).reshape(N, 8, 16, 4, 8, 16, 4)
    w[:, :, 8:, :, :, :8] = 0
    return {"x": x.reshape(N, 128, 4 * C), "u": u.reshape(N, 128, 512), "v": d["v"], **weights(rng, w.reshape(N, 128, 2048))}
def setup_inputs_near(rng):
    d = numbers_of(rng)
    x = d["x"].astype(np.float32).reshape(N, 8, 16, C, 4)
    s = np.arange(C) // 2
    g = ((s[:, None] >> np.arange(8)) & 1) * np.exp2(np.arange(8) - 23.0)
    x[:, :, 0] = 0
    x[:, :, 0, :, 0] = signs(rng)[:, :, None]
    x[:, :, 8] = g[:, :4]
    x[:, :, 9] = g[:, 4:]
    x[:, :, 10:] = rng.integers(4, 8, (N, 8, 6, C, 4)) * rng.choice([-1.0, 1.0], (N, 8, 6, C, 4)) * 2.0 ** -20
    u = d["u"].reshape(N, 128, 128, 4)
    k = np.where(rng.permutation(N) < N // 2, 2.0 ** -30, 1.0).astype(np.float32).astype(BF)
    u[:, :, ::16] = 0
    for h in range(0, 128, 16):
        u[:, h, h, 0] = k
        u[:, h + 8:h + 10, h] = k[:, None, None]
    return {"x": x.reshape(N, 128, 4 * C).astype(BF), "u": u.reshape(N, 128, 512), "v": d["v"], **still(rng)}
def setup_inputs_huge(rng):
    d = numbers_of(rng)
    x = 2.0 ** 30 * (0.6 + 0.4 * rng.random((N, 128, C, 4)))
    c = np.stack([rng.permutation(C) % 2 * 2.0 - 1.0 for r in range(N)])
    c[rng.permutation(N) < N // 2] = 1
    x *= c[:, None, :, None]
    u = d["u"].reshape(N, 128, 128, 4)
    a = 2.0 ** 30 * (1 - 0.25 * rng.random((N, 128, 8, 4))) * signs(rng)[:, None, :, None]
    u[:, :, ::16] = a.astype(np.float32).astype(BF)
    return {"x": x.astype(np.float32).reshape(N, 128, 4 * C).astype(BF), "u": u.reshape(N, 128, 512), "v": d["v"], **still(rng)}
def setup_inputs_spread(rng):
    d = setup_inputs(rng)
    d["x"] = wide(rng, N, 128, 4 * C, cols=6)
    return d
def check_inputs(d):
    b = []
    for k in ("x", "u", "v"):
        a = np.abs(d[k].astype(np.float32))
        if not (np.isfinite(a).all() and ((a == 0) | (a >= 2.0 ** -30) & (a <= 2.0 ** 30)).all()): b.append("a value of " + k)
    return b
def reference(x, u, v, wc, ws):
    qu = [mx_ref.quantize(u[r]) for r in range(N)]
    lay = [pk(wc[r], ws[r]) for r in range(N)]
    now = [x[r] for r in range(N)]
    place = np.tile(C + np.arange(K), (8, 1))
    for t in range(R):
        made, o, border = [], [], []
        for r in range(N):
            q = mx_ref.quantize(now[r])
            made.append(tile([mx_ref.matmul(pick(lay[r], np.arange(128 * b, 128 * b + 128)), q) * np.float32(0.03125) for b in range(4)]))
            o.append(order(mx_ref.matmul(qu[r], mx_ref.quantize(made[r]))))
            border.append(mx_ref.quantize(gcols(made[r], o[r][:, :K])))
        came = decode(join(*border)).astype(BF)
        for r in range(N):
            e = np.concatenate([o[r], place], axis=1)
            i = np.argsort(o[r], axis=1)
            now[r] = gcols(np.concatenate([made[r], cut(came, (r + 1) % N, 4 * K)], axis=1), np.take_along_axis(e, i + K, axis=1))
    y, ol = np.zeros((N, 128, C), np.float32), np.zeros((N, 8, C), np.float32)
    oc, osc = np.zeros((N, 128, 4 * C), np.uint8), np.zeros((N, 16, C), np.uint8)
    for r in range(N):
        q = mx_ref.quantize(now[r])
        y[r] = mx_ref.matmul(mx_ref.quantize(v[r]), q)
        ol[r] = o[r]
        oc[r], osc[r] = emit(q)
    return {"y": y, "ol": ol, "oc": oc, "osc": osc}

@@ -1,0 +1,390 @@
+from concourse.mybir import dt, AluOpType as A, ActivationFunctionType as F
+
+C, K, R, H = 448, 64, 3, 224
+NB = C // 16
+HB = NB // 2
+BIG = 2.0 ** 90
+CH = 112
+CW = 8 * CH + 8
+
+SCRATCH = {
+    "ps": ("psum", [128, 4096], "float32"),
+    "X": ("sbuf", [128, 4 * C], "bfloat16"), "Y": ("sbuf", [128, 4 * C], "bfloat16"),
+    "qx": ("sbuf", [128, C], "float8_e4m3fn_x4"), "sx": ("sbuf", [128, C], "uint8"),
+    "qw": ("sbuf", [128, 512], "float8_e4m3fn_x4"), "sw": ("sbuf", [128, 512], "uint8"),
+    "ut": ("sbuf", [128, 512], "bfloat16"), "vt": ("sbuf", [128, 512], "bfloat16"),
+    "qu": ("sbuf", [128, 128], "float8_e4m3fn_x4"), "su": ("sbuf", [128, 128], "uint8"),
+    "qu2": ("sbuf", [128, 128], "float8_e4m3fn_x4"), "su2": ("sbuf", [128, 128], "uint8"),
+    "qv": ("sbuf", [128, 128], "float8_e4m3fn_x4"), "sv": ("sbuf", [128, 128], "uint8"),
+    "et": ("sbuf", [128, 516], "bfloat16"),
+    "qe": ("sbuf", [128, 512], "float8_e4m3fn_x4"), "se": ("sbuf", [128, 512], "uint8"),
+    "pi": ("sbuf", [128, 8], "int32"), "pf": ("sbuf", [128, 8], "float32"),
+    "ui": ("sbuf", [128, 8], "int32"), "uo": ("sbuf", [128, 8], "uint16"),
+    "rr": ("sbuf", [128, C], "float32"), "idn": ("sbuf", [128, 128], "float32"), "hh": ("sbuf", [128, 32], "float32"),
+    "jc": ("sbuf", [128, C], "bfloat16"), "m01": ("sbuf", [128, C], "bfloat16"), "rs01": ("sbuf", [128, C], "bfloat16"),
+    "mpm": ("sbuf", [128, C], "float32"), "mrs": ("sbuf", [128, C], "float32"), "zm": ("sbuf", [128, 928], "bfloat16"),
+    "d1": ("sbuf", [128, C], "float32"), "S": ("sbuf", [128, C], "float32"), "pc": ("sbuf", [128, C + 208], "float32"),
+    "fa": ("sbuf", [128, 8 * C], "bfloat16"), "fb": ("sbuf", [128, 8 * C], "bfloat16"),
+    "sg": ("sbuf", [128, HB * 208], "bfloat16"), "rj": ("sbuf", [128, HB * 112], "bfloat16"),
+    "fr": ("sbuf", [128, C], "bfloat16"), "ra": ("sbuf", [128, 16], "float32"), "rb": ("sbuf", [128, 16], "float32"),
+    "cum": ("sbuf", [128, 4 * CW], "float16"), "cs": ("sbuf", [128, C + 32], "bfloat16"),
+    "tt": ("sbuf", [128, 928], "bfloat16"), "zz": ("sbuf", [128, 928], "bfloat16"),
+    "base": ("sbuf", [128, 32], "float32"), "col": ("sbuf", [128, 32], "float32"), "rk": ("sbuf", [128, 32], "float32"),
+    "oi": ("sbuf", [128, 32], "uint16"), "oi64": ("sbuf", [128, 32], "uint16"),
+    "o": ("sbuf", [128, 512], "bfloat16"),
+    "t1": ("sbuf", [128, K], "bfloat16"), "t2": ("sbuf", [128, K], "bfloat16"),
+    "b1": ("sbuf", [128, K], "bfloat16"), "b2": ("sbuf", [128, K], "bfloat16"),
+    "e1": ("sbuf", [128, C], "bfloat16"), "e2": ("sbuf", [128, C], "bfloat16"),
+    "ox": ("sbuf", [128, 4 * NB], "uint16"), "ob": ("sbuf", [128, 16], "uint16"),
+    "dall": ("sbuf", [128, 4 * C], "bfloat16"), "dsel": ("sbuf", [128, 4 * K], "bfloat16"),
+    "of": ("sbuf", [128, C], "float32"), "yo": ("sbuf", [128, C], "float32"),
+}
+for _t in range(R):
+    SCRATCH["qy%d" % _t] = ("sbuf", [128, C], "float8_e4m3fn_x4")
+    SCRATCH["sy%d" % _t] = ("sbuf", [128, C], "uint8")
+    SCRATCH["qn%d" % _t] = ("sbuf", [128, C], "float8_e4m3fn_x4")
+    SCRATCH["sn%d" % _t] = ("sbuf", [128, C], "uint8")
+    SCRATCH["ls%d" % _t] = ("sbuf", [128, 8], "uint16")
+    SCRATCH["ln%d" % _t] = ("sbuf", [128, 8], "uint16")
+
+SEMAPHORES = (["cv", "ca", "cp", "cg", "sent"] + ["d%d" % i for i in range(16)]
+              + ["aq%d" % t for t in range(R)] + ["al%d" % t for t in range(R)])
+
+
+def rank_program(g, core, T, topo):
+    rank = T.rank_of(core)
+    if rank is None:
+        return
+    n = len(T.cores)
+    dst = T.cores[(rank - 1) % n]
+    rid, pid, _se = topo.addr(dst)
+    mask = topo.mask(core, dst)
+    neng = len(topo.engines(core, dst))
+    back = len(topo.engines(T.cores[(rank + 1) % n], core))
+
+    Q = {"v": g.vector, "a": g.scalar, "p": g.tensor, "g": g, "s": g.sync}
+    csem = {"v": "cv", "a": "ca", "p": "cp", "g": "cg"}
+    cnt = {"v": 0, "a": 0, "p": 0, "g": 0}
+    waited = {q: {} for q in Q}
+    wr, rd = {}, {}
+    ndma, dmas, sent = [0], [], [0]
+
+    def wait(q, h):
+        if waited[q].get(h[0], 0) < h[1]:
+            Q[q].wait_ge(T.sem[h[0]], h[1])
+            waited[q][h[0]] = h[1]
+
+    def order(q, r, w, x):
+        need = {}
+        hs = [wr[k] for k in list(r) + list(w) + list(x) if k in wr]
+        hs += [h for k in w for h in rd.get(k, [])]
+        hs += [h for k in x for h in rd.get(k, []) if h[0] != csem.get(q)]
+        for s, c in hs:
+            need[s] = max(need.get(s, 0), c)
+        for s in need:
+            wait(q, (s, need[s]))
+
+    def note(h, r, w, x):
+        for k in list(r) + list(x):
+            rd.setdefault(k, []).append(h)
+        for k in w:
+            wr[k] = h
+            rd[k] = []
+
+    def op(q, fn, r=(), w=(), x=()):
+        order(q, r, w, x)
+        cnt[q] += 1
+        fn().then_inc(T.sem[csem[q]], 1)
+        note((csem[q], cnt[q]), r, w, x)
+
+    def dma(q, out, in_, r=(), w=()):
+        order(q, r, w, ())
+        s = "d%d" % ndma[0]
+        ndma[0] += 1
+        Q[q].dma_start(out, in_).then_inc(T.sem[s], 16)
+        dmas.append((s, 16))
+        note((s, 16), r, w, ())
+
+    def send(out, in_, sem, r):
+        order("g", r, (), ())
+        g.remote_dma(out, in_, T.sem[sem], T.sem.sent, pid, rid, mask)
+        sent[0] += neng
+
+    V, S = g.vector, g.scalar
+    u8, u32 = dt.uint8, dt.uint32
+
+    def bank(b, m):
+        return T.ps[:, 512 * b:512 * b + m]
+
+    def slot(c, lo, hi):
+        s = c % HB
+        buf = T.fa if s < 7 else T.fb
+        return buf[:, 8 * lo + s % 7:8 * hi:8]
+
+    dma("s", T.X[:, 0:4 * H], T.x[:, 0:4 * H], w=["X0"])
+    dma("a", T.sw[:], T.ws[:], w=["sw"])
+    dma("a", T.qw[:, 0:256].bitcast(u8), T.wc[:, 0:1024], w=["w0", "w1"])
+    dma("s", T.X[:, 4 * H:4 * C], T.x[:, 4 * H:4 * C], w=["X1"])
+    dma("a", T.qw[:, 256:512].bitcast(u8), T.wc[:, 1024:2048], w=["w2", "w3"])
+    dma("s", T.ut[:], T.u[:], w=["ut"])
+    dma("s", T.vt[:], T.v[:], w=["vt"])
+
+    op("g", lambda: g.iota(T.pi[:, 0:1], [[1, 1]], 0, 1), w=["pi0"])
+    op("g", lambda: g.iota(T.rr[:], [[0, NB], [1, 16]], 0, 0, allow_small_or_imprecise_dtypes=True), w=["rr"])
+    op("g", lambda: g.iota(T.idn[:], [[1, 128]], 0, -1, allow_small_or_imprecise_dtypes=True), w=["idn"])
+    op("g", lambda: g.iota(T.hh[:], [[1, 2], [0, 16]], 0, 0, allow_small_or_imprecise_dtypes=True), w=["hh"])
+    op("g", lambda: g.iota(T.ui[:], [[16, 8]], 0, 0), w=["ui"])
+    op("g", lambda: g.iota(T.jc[:], [[1, C]], -256, 0, allow_small_or_imprecise_dtypes=True), w=["jc"])
+    op("v", lambda: V.memset(T.et[:], 0.0), w=["et"])
+    op("v", lambda: V.memset(T.fa[:, 0:8 * 112], 0.0), w=["fz"])
+    op("v", lambda: V.tensor_scalar(T.pi[:, 1:2], T.pi[:, 0:1], 15, None, A.bitwise_and), r=["pi0"], w=["pi1"])
+    op("v", lambda: V.tensor_scalar(T.pi[:, 2:3], T.pi[:, 0:1], 4, 1, A.logical_shift_right, A.bitwise_and), r=["pi0"], w=["pi2"])
+    op("v", lambda: V.memset(T.fb[:, 8 * 112:8 * 224], 0.0), w=["fz2"])
+    op("v", lambda: V.tensor_copy(T.pf[:, 0:2], T.pi[:, 1:3]), r=["pi1", "pi2"], w=["pf"])
+    op("v", lambda: V.memset(T.fb[:, 7:8 * 112:8], 0.0), w=["fz3"])
+    op("v", lambda: V.memset(T.fb[:, 8 * 224 + 7:8 * C:8], 0.0), w=["fz4"])
+    op("v", lambda: V.tensor_scalar(T.pf[:, 2:3], T.pf[:, 0:1], 224.0, None, A.add), r=["pf"], w=["cr"])
+    op("v", lambda: V.tensor_scalar(T.m01[:], T.rr[:], T.pf[:, 0:1], None, A.is_equal), r=["rr", "pf"], w=["m01"])
+    op("v", lambda: V.tensor_scalar(T.et[:, 3:515:4], T.idn[:], 0.0, None, A.is_equal), r=["idn"], w=["et"])
+    op("v", lambda: V.tensor_scalar(T.zm[:, 0:32], T.hh[:], T.pf[:, 1:2], None, A.is_equal), r=["hh", "pf"], w=["zm"])
+    op("v", lambda: V.tensor_copy(T.uo[:], T.ui[:]), r=["ui"], w=["uo"])
+    op("a", lambda: S.activation(T.mrs[:], T.rr[:], F.Identity, bias=BIG, scale=-2 * BIG), r=["rr"], w=["mrs"])
+    op("a", lambda: S.activation(T.mpm[:], T.m01[:], F.Identity, bias=BIG, scale=-2 * BIG), r=["m01"], w=["mpm"])
+    have = 32
+    while have < 928:
+        m = min(have, 928 - have)
+        op("a", lambda: S.activation(T.zm[:, have:have + m], T.zm[:, 0:m], F.Copy), r=["zm"], w=["zm"])
+        have += m
+    for b in range(4):
+        op("v", lambda: V.quantize_mx(T.qe[:, 128 * b:128 * b + 128], T.se[:, 128 * b:128 * b + 128], T.et[:, 3 - b:515 - b]),
+           r=["et"], w=["e%d" % b])
+
+    def late_constants():
+        op("v", lambda: V.quantize_mx(T.qu[:], T.su[:], T.ut[:]), r=["ut"], w=["qu"])
+        op("v", lambda: V.tensor_scalar(T.rs01[:], T.rr[:], 1.0, None, A.min), r=["rr"], w=["rs01"])
+        op("v", lambda: V.tensor_copy(T.qu2[:].bitcast(u32), T.qu[:].bitcast(u32).indirect(T.uo[:])), r=["qu", "uo"], w=["qu2"])
+        op("v", lambda: V.tensor_copy(T.su2[:], T.su[:].indirect(T.uo[:])), r=["qu", "uo"], w=["su2"])
+
+    def small_fills():
+        op("v", lambda: V.memset(T.cum[:, 7:4 * CW:CW], 16.0), w=["cum_i"])
+        op("v", lambda: V.memset(T.cs[:, 0:16], 0.0), w=["cs_a"])
+        op("v", lambda: V.memset(T.cs[:, C + 16:C + 32], 0.0), w=["cs_b"])
+        op("v", lambda: V.memset(T.ra[:], 0.0), w=["ra%d" % c for c in range(HB, NB)])
+        op("v", lambda: V.memset(T.rb[:], 0.0), w=["rb%d" % c for c in range(HB, NB)])
+        op("v", lambda: V.memset(T.o[:, C:512], -256.0), w=["o_x"])
+
+    small_fills()
+
+    def quant_x(h):
+        op("v", lambda: V.quantize_mx(T.qx[:, H * h:H * h + H], T.sx[:, H * h:H * h + H], T.X[:, 4 * H * h:4 * H * (h + 1)]),
+           r=["X%d" % h, "Xs"] + ["Xg%d" % b for b in range(4)], w=["qx%d" % h])
+
+    def mm(b, lq, ls, rq, rs, m, r):
+        op("p", lambda: g.tensor.matmul_mx(bank(b, m), lq, ls, rq, rs, True, True), r=r, w=["bk%d" % b])
+
+    for t in range(R):
+        qy, sy, qn, sn, ls, ln = (T[k + str(t)] for k in ("qy", "sy", "qn", "sn", "ls", "ln"))
+
+        def layer(b, h):
+            mm(2 * b + h, T.qw[:, 128 * b:128 * b + 128], T.sw[:, 128 * b:128 * b + 128],
+               T.qx[:, H * h:H * h + H], T.sx[:, H * h:H * h + H], H, ["w%d" % b, "sw", "qx%d" % h])
+
+        def to_y(q, b, h):
+            out = T.Y[:, 4 * H * h + b:4 * H * (h + 1):4]
+            if q == "a":
+                op("a", lambda: S.activation(out, bank(2 * b + h, H), F.Copy, scale=0.03125), x=["bk%d" % (2 * b + h)], w=["Y%d%d" % (b, h)])
+            else:
+                op("v", lambda: V.tensor_scalar(out, bank(2 * b + h, H), 0.03125, None, A.mult), x=["bk%d" % (2 * b + h)], w=["Y%d%d" % (b, h)])
+
+        def quant_y(h):
+            op("v", lambda: V.quantize_mx(qy[:, H * h:H * h + H], sy[:, H * h:H * h + H], T.Y[:, 4 * H * h:4 * H * (h + 1)]),
+               r=["Y%d%d" % (b, h) for b in range(4)], w=["qy%d%d" % (t, h)])
+
+        def scores(h):
+            mm(2 * h, T.qu2[:], T.su2[:], qy[:, H * h:H * h + H], sy[:, H * h:H * h + H], H, ["qu2", "su2", "qy%d%d" % (t, h)])
+
+        def own_mask(h):
+            op("v", lambda: V.tensor_tensor(T.d1[:, H * h:H * h + H], bank(2 * h, H), T.mpm[:, 0:H], A.max), r=["mpm"], x=["bk%d" % (2 * h)], w=["d1%d" % h])
+
+        def own_scan(h):
+            op("v", lambda: V.tensor_tensor_scan(T.S[:, H * h:H * h + H], T.mrs[:, 0:H], T.d1[:, H * h:H * h + H], BIG, A.max, A.min),
+               r=["mrs", "d1%d" % h], w=["S%d" % h])
+
+        def diag(h):
+            op("v", lambda: V.tensor_tensor(T.fa[:, 8 * H * h + 7:8 * H * (h + 1):8], bank(2 * h, H), T.S[:, H * h:H * h + H], A.is_gt),
+               r=["S%d" % h, "fz"], x=["bk%d" % (2 * h)], w=["fd%d" % h])
+
+        quant_x(0)
+        quant_x(1)
+        for b in range(4):
+            layer(b, 0)
+        layer(0, 1)
+        layer(1, 1)
+        if t == 0:
+            late_constants()
+        to_y("a", 0, 0)
+        to_y("v", 1, 0)
+        to_y("a", 2, 0)
+        to_y("v", 3, 0)
+        quant_y(0)
+        scores(0)
+        layer(2, 1)
+        layer(3, 1)
+        to_y("a", 0, 1)
+        to_y("a", 1, 1)
+        own_mask(0)
+        to_y("a", 2, 1)
+        own_scan(0)
+        to_y("v", 3, 1)
+        op("a", lambda: S.activation(T.pc[:, 0:H], bank(0, H), F.Copy), x=["bk0"], w=["pc0"])
+        op("a", lambda: S.activation(T.pc[:, C:C + 208], bank(0, 208), F.Copy), x=["bk0"], w=["pcx"])
+        quant_y(1)
+        scores(1)
+        send(qn[:].bitcast(u8), qy[:].bitcast(u8), "aq%d" % t, ["qy%d0" % t, "qy%d1" % t])
+        send(sn[:], sy[:], "aq%d" % t, [])
+        diag(0)
+        own_mask(1)
+        op("a", lambda: S.activation(T.pc[:, H:C], bank(2, H), F.Copy), x=["bk2"], w=["pc1"])
+        own_scan(1)
+        wr["qn%d" % t] = ("aq%d" % t, 2 * back)
+        for b in range(4):
+            mm(4 + b, T.qe[:, 128 * b:128 * b + 128], T.se[:, 128 * b:128 * b + 128], qn[:], sn[:], C, ["e%d" % b, "qn%d" % t])
+
+        zs = ["fz", "fz2", "fz3", "fz4"]
+
+        def sign(c):
+            op("a", lambda: S.activation(T.sg[:, 208 * (c - HB):208 * (c - HB + 1)], T.pc[:, 16 * (c + 1):16 * (c + HB)], F.Sign,
+                                         bias=T.S[:, 16 * c + 15:16 * c + 16], scale=-1.0),
+               r=["pc1", "pcx", "S1"], w=["sg%d" % c])
+
+        def later(c):
+            m = C - 16 * (c + 1)
+            op("a", lambda: S.activation(slot(c, 16 * (c + 1), C), T.sg[:, 208 * (c - HB):208 * (c - HB) + m], F.Relu, scale=-1.0,
+                                         accum_out=T.ra[:, c - HB:c - HB + 1]), r=["sg%d" % c] + zs, w=["f%da" % c, "ra%d" % c])
+
+        def earlier(c):
+            m = 16 * (c - HB)
+            op("a", lambda: S.activation(slot(c, 0, m), T.sg[:, 208 * (c - HB + 1) - m:208 * (c - HB + 1)], F.Sign, bias=1.0, scale=-1.0,
+                                         accum_out=T.rb[:, c - HB:c - HB + 1]), r=["sg%d" % c] + zs, w=["f%db" % c, "rb%d" % c])
+
+        sign(HB)
+        for c in range(HB, NB - 1):
+            sign(c + 1)
+            later(c)
+        for c in range(NB - 1, HB, -1):
+            earlier(c)
+
+        def flags(c):
+            op("v", lambda: V.tensor_scalar(slot(c, 16 * (c + 1), 16 * (c + 15)), T.pc[:, 16 * (c + 1):16 * (c + 15)],
+                                            T.S[:, 16 * c + 15:16 * c + 16], None, A.is_gt),
+               r=["pc0", "pc1", "S0"] + zs, w=["f%d" % c])
+
+        def rowsum(c):
+            op("v", lambda: V.tensor_tensor_scan(T.rj[:, 112 * c:112 * c + 112], slot(c, 16 * (c + 1), 16 * (c + 8)),
+                                                 slot(c, 16 * (c + 8), 16 * (c + 15)), -16.0, A.add, A.add),
+               r=["f%d" % c], w=["rj%d" % c])
+
+        flags(0)
+        for c in range(1, HB):
+            flags(c)
+            rowsum(c - 1)
+        diag(1)
+        rowsum(HB - 1)
+        op("v", lambda: V.tensor_tensor_scan(T.fr[:], T.rs01[:], T.fa[:, 7:8 * C:8], 0.0, A.mult, A.add), r=["rs01", "fd0", "fd1"], w=["fr"])
+
+        def colscan(i):
+            lo, hi = 7 * i, 7 * i + 6
+            r = ["f%d" % c for c in range(HB) if c + 1 <= hi and c + HB >= lo]
+            r += ["f%da" % c for c in range(HB, NB - 1) if c + 1 <= hi]
+            r += ["f%db" % c for c in range(HB + 1, NB) if c - HB - 1 >= lo]
+            op("v", lambda: V.tensor_tensor_scan(T.cum[:, CW * i + 8:CW * (i + 1)], T.fa[:, 8 * CH * i:8 * CH * (i + 1)],
+                                                 T.fb[:, 8 * CH * i:8 * CH * (i + 1)], 16.0, A.add, A.add),
+               r=r + zs + ["fd%d" % (i // 2)], w=["cum%d" % i])
+
+        def coldiff(i):
+            op("v", lambda: V.tensor_tensor_scan(T.cs[:, 16 + CH * i:16 + CH * (i + 1)], T.cum[:, CW * i + 15:CW * (i + 1):8],
+                                                 T.cum[:, CW * i + 7:CW * (i + 1) - 8:8], 0.0, A.max, A.subtract),
+               r=["cum%d" % i, "cum_i"], w=["cs%d" % i])
+
+        colscan(2)
+        op("v", lambda: V.tensor_tensor(T.base[:, 0:HB], T.rj[:, 111:112 * HB:112], T.fr[:, 15:H:16], A.add),
+           r=["fr"] + ["rj%d" % c for c in range(HB)], w=["base0"])
+        colscan(3)
+        coldiff(2)
+        op("v", lambda: V.tensor_tensor(T.rk[:, HB:NB], T.ra[:, 0:HB], T.fr[:, H + 15:C:16], A.add),
+           r=["fr"] + ["ra%d" % c for c in range(HB, NB)], w=["rk"])
+        colscan(1)
+        coldiff(3)
+        colscan(0)
+        coldiff(1)
+        op("v", lambda: V.tensor_tensor(T.base[:, HB:NB], T.rk[:, HB:NB], T.rb[:, 0:HB], A.add),
+           r=["rk"] + ["rb%d" % c for c in range(HB, NB)], w=["base1"])
+        coldiff(0)
+        css = ["cs%d" % i for i in range(4)] + ["cs_a", "cs_b"]
+        op("v", lambda: V.transpose(T.tt[:, 0:C], T.cs[:, 16:16 + C]), r=css, w=["tt0"])
+        op("v", lambda: V.transpose(T.tt[:, C:928], T.cs[:, 0:480]), r=css, w=["tt1"])
+        op("v", lambda: V.tensor_tensor_scan(T.zz[:], T.tt[:], T.zm[:], 0.0, A.add, A.mult), r=["tt0", "tt1", "zm"], w=["zz"])
+        op("v", lambda: V.tensor_tensor(T.col[:, 0:NB:2], T.zz[:, 15:C:32], T.zz[:, C + 31:C + 448:32], A.add), r=["zz"], w=["col0"])
+        op("v", lambda: V.tensor_tensor(T.col[:, 1:NB:2], T.zz[:, 31:C:32], T.zz[:, C + 47:928:32], A.add), r=["zz"], w=["col1"])
+        op("v", lambda: V.tensor_tensor(T.rk[:, 0:NB], T.base[:, 0:NB], T.col[:, 0:NB], A.subtract), r=["base0", "base1", "col0", "col1"], w=["rk"])
+        op("v", lambda: V.tensor_scalar(T.oi[:, 0:NB], T.rk[:, 0:NB], T.pf[:, 2:3], None, A.add), r=["rk", "cr"], w=["oi"])
+        op("v", lambda: V.tensor_scalar(T.oi64[:, 0:NB], T.rk[:, 0:NB], T.pf[:, 2:3], float(K), A.add, A.add), r=["rk", "cr"], w=["oi64"])
+
+        op("v", lambda: V.tensor_copy(T.o[:, 0:C].indirect(T.oi[:, 0:NB]), T.jc[:]), r=["oi", "jc"], w=["o"])
+        op("v", lambda: V.tensor_tensor(T.t1[:], T.o[:, 0:K], T.m01[:, 0:K], A.mult), r=["o", "m01"], w=["t1"])
+        op("v", lambda: V.tensor_tensor(T.b1[:], T.o[:, C - K:C], T.m01[:, 0:K], A.mult), r=["o", "m01"], w=["b1"])
+        op("v", lambda: V.tensor_tensor_scan(T.t2[:], T.rs01[:, 0:K], T.t1[:], 0.0, A.mult, A.add), r=["t1", "rs01"], w=["t2"])
+        op("v", lambda: V.tensor_tensor_scan(T.b2[:], T.rs01[:, 0:K], T.b1[:], 0.0, A.mult, A.add), r=["b1", "rs01"], w=["b2"])
+        op("v", lambda: V.tensor_scalar(ls[:, 0:4], T.t2[:, 15:K:16], 256.0, None, A.add), r=["t2"], w=["ls%d" % t])
+        send(ln[:, 0:4], ls[:, 0:4], "al%d" % t, ["ls%d" % t])
+        wr["ln%d" % t] = ("al%d" % t, back)
+        for b in range(4):
+            op("a", lambda: S.activation(T.dall[:, C * b:C * b + C], bank(4 + b, C), F.Copy), x=["bk%d" % (4 + b)], w=["dall%d" % b])
+
+        op("v", lambda: V.tensor_tensor(T.e1[:], T.o[:].indirect(T.oi64[:, 0:NB]), T.m01[:], A.mult), r=["o", "o_x", "oi64", "m01"], w=["e1"])
+        op("v", lambda: V.tensor_tensor_scan(T.e2[:], T.rs01[:], T.e1[:], 0.0, A.mult, A.add), r=["e1", "rs01"], w=["e2"])
+        ys = ["Y%d%d" % (b, h) for b in range(4) for h in range(2)]
+        for b in (2, 0, 3, 1):
+            op("v", lambda: V.tensor_scalar(T.ox[:, NB * b:NB * b + NB], T.e2[:, 15:C:16], 4.0, 1024.0 + b, A.mult, A.add), r=["e2"], w=["ox%d" % b])
+        for b in range(4):
+            out, src = T.X[:, b:4 * C:4], T.Y[:].indirect(T.ox[:, NB * b:NB * b + NB])
+            w = ["Xg%d" % b]
+            if b < 2:
+                order("v", (), ["X0", "X1", "Xs"], ())
+                op("v", lambda: V.tensor_copy(out, src), r=ys + ["ox%d" % b], w=w)
+            else:
+                order("a", (), ["X0", "X1", "Xs"], ())
+                op("a", lambda: S.activation(out, src, F.Copy), r=ys + ["ox%d" % b], w=w)
+        for b in range(4):
+            op("v", lambda: V.tensor_scalar(T.ob[:, 4 * b:4 * b + 4], T.b2[:, 15:K:16], 4.0, 1024.0 + b, A.mult, A.add), r=["b2"], w=["ob%d" % b])
+        if t == 0:
+            op("v", lambda: V.quantize_mx(T.qv[:], T.sv[:], T.vt[:]), r=["vt"], w=["qv"])
+        if t == R - 1:
+            op("a", lambda: S.activation(T.of[:], T.o[:, 0:C], F.Identity, bias=256.0), r=["o"], w=["of"])
+            dma("s", T.ol[:], T.of[0:128:16, :], r=["of"])
+        for b in (0, 2, 1, 3):
+            out, src = T.dsel[:, K * b:K * b + K], T.dall[:, C * b:C * b + C].indirect(ln[:, 0:4])
+            r = ["dall%d" % b, "ln%d" % t]
+            if b < 2:
+                op("v", lambda: V.tensor_copy(out, src), r=r, w=["ds%d" % b])
+            else:
+                op("a", lambda: S.activation(out, src, F.Copy), r=r, w=["ds%d" % b])
+        op("v", lambda: V.tensor_copy(T.X[:].indirect(T.ob[:]), T.dsel[:]),
+           r=["ds%d" % b for b in range(4)] + ["ob%d" % b for b in range(4)] + ["Xg%d" % b for b in range(4)], w=["Xs"])
+
+    quant_x(0)
+    quant_x(1)
+    for h in range(2):
+        mm(h, T.qv[:], T.sv[:], T.qx[:, H * h:H * h + H], T.sx[:, H * h:H * h + H], H, ["qv", "qx%d" % h])
+    dma("s", T.oc[:], T.qx[:].bitcast(u8), r=["qx0", "qx1"])
+    for k in range(4):
+        dma("a" if k < 2 else "s", T.osc[4 * k:4 * k + 4, :], T.sx[32 * k:32 * k + 4, :], r=["qx0", "qx1"])
+    for h in range(2):
+        op("v", lambda: V.tensor_copy(T.yo[:, H * h:H * h + H], bank(h, H)), x=["bk%d" % h], w=["yo%d" % h])
+    dma("a", T.y[:], T.yo[:], r=["yo0", "yo1"])
+
+    for q in cnt:
+        wait("g", (csem[q], cnt[q]))
+    for h in dmas:
+        wait("g", h)
+    wait("g", ("sent", sent[0]))

@@ -1,11 +1,12 @@
 from concourse.mybir import dt, AluOpType as A, ActivationFunctionType as F
 
-C, K, R, H = 448, 64, 3, 224
+C, K, R = 448, 64, 3
+PART = ((0, 288), (288, 448))
 NB = C // 16
 HB = NB // 2
 BIG = 2.0 ** 90
-CH = 112
-CW = 8 * CH + 8
+RUNS = ((14, 21), (21, 28), (5, 14), (0, 5))
+CW = 8 * 144 + 8
 
 SCRATCH = {
     "ps": ("psum", [128, 4096], "float32"),
@@ -22,7 +23,7 @@ SCRATCH = {
     "ui": ("sbuf", [128, 8], "int32"), "uo": ("sbuf", [128, 8], "uint16"),
     "rr": ("sbuf", [128, C], "float32"), "idn": ("sbuf", [128, 128], "float32"), "hh": ("sbuf", [128, 32], "float32"),
     "jc": ("sbuf", [128, C], "bfloat16"), "m01": ("sbuf", [128, C], "bfloat16"), "rs01": ("sbuf", [128, C], "bfloat16"),
-    "mpm": ("sbuf", [128, C], "float32"), "mrs": ("sbuf", [128, C], "float32"), "zm": ("sbuf", [128, 928], "bfloat16"),
+    "mpm": ("sbuf", [128, 288], "float32"), "mrs": ("sbuf", [128, 288], "float32"), "zm": ("sbuf", [128, 928], "bfloat16"),
     "d1": ("sbuf", [128, C], "float32"), "S": ("sbuf", [128, C], "float32"), "pc": ("sbuf", [128, C + 208], "float32"),
     "fa": ("sbuf", [128, 8 * C], "bfloat16"), "fb": ("sbuf", [128, 8 * C], "bfloat16"),
     "sg": ("sbuf", [128, HB * 208], "bfloat16"), "rj": ("sbuf", [128, HB * 112], "bfloat16"),
@@ -30,7 +31,7 @@ SCRATCH = {
     "cum": ("sbuf", [128, 4 * CW], "float16"), "cs": ("sbuf", [128, C + 32], "bfloat16"),
     "tt": ("sbuf", [128, 928], "bfloat16"), "zz": ("sbuf", [128, 928], "bfloat16"),
     "base": ("sbuf", [128, 32], "float32"), "col": ("sbuf", [128, 32], "float32"), "rk": ("sbuf", [128, 32], "float32"),
-    "oi": ("sbuf", [128, 32], "uint16"), "oi64": ("sbuf", [128, 32], "uint16"),
+    "oi": ("sbuf", [128, 32], "uint16"),
     "o": ("sbuf", [128, 512], "bfloat16"),
     "t1": ("sbuf", [128, K], "bfloat16"), "t2": ("sbuf", [128, K], "bfloat16"),
     "b1": ("sbuf", [128, K], "bfloat16"), "b2": ("sbuf", [128, K], "bfloat16"),
@@ -121,62 +122,65 @@ def rank_program(g, core, T, topo):
         buf = T.fa if s < 7 else T.fb
         return buf[:, 8 * lo + s % 7:8 * hi:8]
 
-    dma("s", T.X[:, 0:4 * H], T.x[:, 0:4 * H], w=["X0"])
+    (l0, h0), (l1, h1) = PART
+
+    dma("s", T.X[:, 0:4 * h0], T.x[:, 0:4 * h0], w=["X0"])
     dma("a", T.sw[:], T.ws[:], w=["sw"])
     dma("a", T.qw[:, 0:256].bitcast(u8), T.wc[:, 0:1024], w=["w0", "w1"])
-    dma("s", T.X[:, 4 * H:4 * C], T.x[:, 4 * H:4 * C], w=["X1"])
-    dma("a", T.qw[:, 256:512].bitcast(u8), T.wc[:, 1024:2048], w=["w2", "w3"])
+    dma("s", T.qw[:, 256:512].bitcast(u8), T.wc[:, 1024:2048], w=["w2", "w3"])
+    dma("a", T.X[:, 4 * h0:4 * C], T.x[:, 4 * h0:4 * C], w=["X1"])
     dma("s", T.ut[:], T.u[:], w=["ut"])
-    dma("s", T.vt[:], T.v[:], w=["vt"])
+    dma("s", T.vt[:], T.v[:], r=["ut"], w=["vt"])
+
+    def count(out, pattern, base, step, key):
+        op("g", lambda: g.iota(out, pattern, base, step, allow_small_or_imprecise_dtypes=True), w=[key])
 
     op("g", lambda: g.iota(T.pi[:, 0:1], [[1, 1]], 0, 1), w=["pi0"])
-    op("g", lambda: g.iota(T.rr[:], [[0, NB], [1, 16]], 0, 0, allow_small_or_imprecise_dtypes=True), w=["rr"])
-    op("g", lambda: g.iota(T.idn[:], [[1, 128]], 0, -1, allow_small_or_imprecise_dtypes=True), w=["idn"])
-    op("g", lambda: g.iota(T.hh[:], [[1, 2], [0, 16]], 0, 0, allow_small_or_imprecise_dtypes=True), w=["hh"])
+    count(T.idn[:], [[1, 128]], 0, -1, "idn")
+    count(T.rr[:], [[0, NB], [1, 16]], 0, 0, "rr")
     op("g", lambda: g.iota(T.ui[:], [[16, 8]], 0, 0), w=["ui"])
-    op("g", lambda: g.iota(T.jc[:], [[1, C]], -256, 0, allow_small_or_imprecise_dtypes=True), w=["jc"])
+    count(T.hh[:], [[1, 2], [0, 16]], 0, 0, "hh")
+    count(T.fa[:, 0:8 * 112], [[0, 8 * 112]], 0, 0, "fz")
+    count(T.fb[:, 8 * 112:8 * 224], [[0, 8 * 112]], 0, 0, "fz2")
     op("v", lambda: V.memset(T.et[:], 0.0), w=["et"])
-    op("v", lambda: V.memset(T.fa[:, 0:8 * 112], 0.0), w=["fz"])
     op("v", lambda: V.tensor_scalar(T.pi[:, 1:2], T.pi[:, 0:1], 15, None, A.bitwise_and), r=["pi0"], w=["pi1"])
     op("v", lambda: V.tensor_scalar(T.pi[:, 2:3], T.pi[:, 0:1], 4, 1, A.logical_shift_right, A.bitwise_and), r=["pi0"], w=["pi2"])
-    op("v", lambda: V.memset(T.fb[:, 8 * 112:8 * 224], 0.0), w=["fz2"])
-    op("v", lambda: V.tensor_copy(T.pf[:, 0:2], T.pi[:, 1:3]), r=["pi1", "pi2"], w=["pf"])
     op("v", lambda: V.memset(T.fb[:, 7:8 * 112:8], 0.0), w=["fz3"])
+    op("v", lambda: V.tensor_copy(T.pf[:, 0:2], T.pi[:, 1:3]), r=["pi1", "pi2"], w=["pf"])
+    op("v", lambda: V.tensor_scalar(T.et[:, 3:515:4], T.idn[:], 0.0, None, A.is_equal), r=["idn"], w=["et"])
     op("v", lambda: V.memset(T.fb[:, 8 * 224 + 7:8 * C:8], 0.0), w=["fz4"])
     op("v", lambda: V.tensor_scalar(T.pf[:, 2:3], T.pf[:, 0:1], 224.0, None, A.add), r=["pf"], w=["cr"])
-    op("v", lambda: V.tensor_scalar(T.m01[:], T.rr[:], T.pf[:, 0:1], None, A.is_equal), r=["rr", "pf"], w=["m01"])
-    op("v", lambda: V.tensor_scalar(T.et[:, 3:515:4], T.idn[:], 0.0, None, A.is_equal), r=["idn"], w=["et"])
-    op("v", lambda: V.tensor_scalar(T.zm[:, 0:32], T.hh[:], T.pf[:, 1:2], None, A.is_equal), r=["hh", "pf"], w=["zm"])
-    op("v", lambda: V.tensor_copy(T.uo[:], T.ui[:]), r=["ui"], w=["uo"])
-    op("a", lambda: S.activation(T.mrs[:], T.rr[:], F.Identity, bias=BIG, scale=-2 * BIG), r=["rr"], w=["mrs"])
-    op("a", lambda: S.activation(T.mpm[:], T.m01[:], F.Identity, bias=BIG, scale=-2 * BIG), r=["m01"], w=["mpm"])
-    have = 32
-    while have < 928:
-        m = min(have, 928 - have)
-        op("a", lambda: S.activation(T.zm[:, have:have + m], T.zm[:, 0:m], F.Copy), r=["zm"], w=["zm"])
-        have += m
     for b in range(4):
         op("v", lambda: V.quantize_mx(T.qe[:, 128 * b:128 * b + 128], T.se[:, 128 * b:128 * b + 128], T.et[:, 3 - b:515 - b]),
            r=["et"], w=["e%d" % b])
+    op("v", lambda: V.tensor_scalar(T.m01[:], T.rr[:], T.pf[:, 0:1], None, A.is_equal), r=["rr", "pf"], w=["m01"])
+    op("v", lambda: V.memset(T.cum[:, 7:4 * CW:CW], 16.0), w=["cum_i"])
+    op("v", lambda: V.memset(T.cs[:, 0:16], 0.0), w=["cs_a"])
+    op("v", lambda: V.memset(T.cs[:, C + 16:C + 32], 0.0), w=["cs_b"])
+    op("v", lambda: V.memset(T.ra[:], 0.0), w=["ra%d" % c for c in range(HB, NB)])
+    op("v", lambda: V.memset(T.rb[:], 0.0), w=["rb%d" % c for c in range(HB, NB)])
+    op("v", lambda: V.memset(T.o[:, C:512], -256.0), w=["o_x"])
+    op("v", lambda: V.tensor_copy(T.uo[:], T.ui[:]), r=["ui"], w=["uo"])
+    op("v", lambda: V.tensor_scalar(T.zm[:, 0:32], T.hh[:], T.pf[:, 1:2], None, A.is_equal), r=["hh", "pf"], w=["zm"])
+    op("a", lambda: S.activation(T.mrs[:], T.rr[:, 0:h0], F.Identity, bias=BIG, scale=-2 * BIG), r=["rr"], w=["mrs"])
+    op("a", lambda: S.activation(T.mpm[:], T.m01[:, 0:h0], F.Identity, bias=BIG, scale=-2 * BIG), r=["m01"], w=["mpm"])
+    op("a", lambda: S.activation(T.rs01[:], T.rr[:], F.Sign), r=["rr"], w=["rs01"])
 
-    def late_constants():
+    def widen_zm():
+        have = 32
+        while have < 928:
+            m = min(have, 928 - have)
+            op("a", lambda: S.activation(T.zm[:, have:have + m], T.zm[:, 0:m], F.Copy), r=["zm"], w=["zm"])
+            have += m
+
+    def pick_u():
         op("v", lambda: V.quantize_mx(T.qu[:], T.su[:], T.ut[:]), r=["ut"], w=["qu"])
-        op("v", lambda: V.tensor_scalar(T.rs01[:], T.rr[:], 1.0, None, A.min), r=["rr"], w=["rs01"])
         op("v", lambda: V.tensor_copy(T.qu2[:].bitcast(u32), T.qu[:].bitcast(u32).indirect(T.uo[:])), r=["qu", "uo"], w=["qu2"])
-        op("v", lambda: V.tensor_copy(T.su2[:], T.su[:].indirect(T.uo[:])), r=["qu", "uo"], w=["su2"])
-
-    def small_fills():
-        op("v", lambda: V.memset(T.cum[:, 7:4 * CW:CW], 16.0), w=["cum_i"])
-        op("v", lambda: V.memset(T.cs[:, 0:16], 0.0), w=["cs_a"])
-        op("v", lambda: V.memset(T.cs[:, C + 16:C + 32], 0.0), w=["cs_b"])
-        op("v", lambda: V.memset(T.ra[:], 0.0), w=["ra%d" % c for c in range(HB, NB)])
-        op("v", lambda: V.memset(T.rb[:], 0.0), w=["rb%d" % c for c in range(HB, NB)])
-        op("v", lambda: V.memset(T.o[:, C:512], -256.0), w=["o_x"])
-
-    small_fills()
+        op("a", lambda: S.activation(T.su2[:], T.su[:].indirect(T.uo[:]), F.Copy), r=["qu", "uo"], w=["su2"])
 
     def quant_x(h):
-        op("v", lambda: V.quantize_mx(T.qx[:, H * h:H * h + H], T.sx[:, H * h:H * h + H], T.X[:, 4 * H * h:4 * H * (h + 1)]),
+        lo, hi = PART[h]
+        op("v", lambda: V.quantize_mx(T.qx[:, lo:hi], T.sx[:, lo:hi], T.X[:, 4 * lo:4 * hi]),
            r=["X%d" % h, "Xs"] + ["Xg%d" % b for b in range(4)], w=["qx%d" % h])
 
     def mm(b, lq, ls, rq, rs, m, r):
@@ -186,76 +190,97 @@ def rank_program(g, core, T, topo):
         qy, sy, qn, sn, ls, ln = (T[k + str(t)] for k in ("qy", "sy", "qn", "sn", "ls", "ln"))
 
         def layer(b, h):
+            lo, hi = PART[h]
             mm(2 * b + h, T.qw[:, 128 * b:128 * b + 128], T.sw[:, 128 * b:128 * b + 128],
-               T.qx[:, H * h:H * h + H], T.sx[:, H * h:H * h + H], H, ["w%d" % b, "sw", "qx%d" % h])
+               T.qx[:, lo:hi], T.sx[:, lo:hi], hi - lo, ["w%d" % b, "sw", "qx%d" % h])
 
         def to_y(q, b, h):
-            out = T.Y[:, 4 * H * h + b:4 * H * (h + 1):4]
+            lo, hi = PART[h]
+            out, src = T.Y[:, 4 * lo + b:4 * hi:4], bank(2 * b + h, hi - lo)
             if q == "a":
-                op("a", lambda: S.activation(out, bank(2 * b + h, H), F.Copy, scale=0.03125), x=["bk%d" % (2 * b + h)], w=["Y%d%d" % (b, h)])
+                op("a", lambda: S.activation(out, src, F.Copy, scale=0.03125), x=["bk%d" % (2 * b + h)], w=["Y%d%d" % (b, h)])
             else:
-                op("v", lambda: V.tensor_scalar(out, bank(2 * b + h, H), 0.03125, None, A.mult), x=["bk%d" % (2 * b + h)], w=["Y%d%d" % (b, h)])
+                op("v", lambda: V.tensor_scalar(out, src, 0.03125, None, A.mult), x=["bk%d" % (2 * b + h)], w=["Y%d%d" % (b, h)])
 
         def quant_y(h):
-            op("v", lambda: V.quantize_mx(qy[:, H * h:H * h + H], sy[:, H * h:H * h + H], T.Y[:, 4 * H * h:4 * H * (h + 1)]),
+            lo, hi = PART[h]
+            op("v", lambda: V.quantize_mx(qy[:, lo:hi], sy[:, lo:hi], T.Y[:, 4 * lo:4 * hi]),
                r=["Y%d%d" % (b, h) for b in range(4)], w=["qy%d%d" % (t, h)])
 
-        def scores(h):
-            mm(2 * h, T.qu2[:], T.su2[:], qy[:, H * h:H * h + H], sy[:, H * h:H * h + H], H, ["qu2", "su2", "qy%d%d" % (t, h)])
+        def scores(h, b):
+            lo, hi = PART[h]
+            mm(b, T.qu2[:], T.su2[:], qy[:, lo:hi], sy[:, lo:hi], hi - lo, ["qu2", "su2", "qy%d%d" % (t, h)])
 
         def own_mask(h):
-            op("v", lambda: V.tensor_tensor(T.d1[:, H * h:H * h + H], bank(2 * h, H), T.mpm[:, 0:H], A.max), r=["mpm"], x=["bk%d" % (2 * h)], w=["d1%d" % h])
+            lo, hi = PART[h]
+            op("v", lambda: V.tensor_tensor(T.d1[:, lo:hi], bank(2 * h, hi - lo), T.mpm[:, 0:hi - lo], A.max),
+               r=["mpm"], x=["bk%d" % (2 * h)], w=["d1%d" % h])
 
         def own_scan(h):
-            op("v", lambda: V.tensor_tensor_scan(T.S[:, H * h:H * h + H], T.mrs[:, 0:H], T.d1[:, H * h:H * h + H], BIG, A.max, A.min),
+            lo, hi = PART[h]
+            op("v", lambda: V.tensor_tensor_scan(T.S[:, lo:hi], T.mrs[:, 0:hi - lo], T.d1[:, lo:hi], BIG, A.max, A.min),
                r=["mrs", "d1%d" % h], w=["S%d" % h])
 
         def diag(h):
-            op("v", lambda: V.tensor_tensor(T.fa[:, 8 * H * h + 7:8 * H * (h + 1):8], bank(2 * h, H), T.S[:, H * h:H * h + H], A.is_gt),
+            lo, hi = PART[h]
+            op("v", lambda: V.tensor_tensor(T.fa[:, 8 * lo + 7:8 * hi:8], bank(2 * h, hi - lo), T.S[:, lo:hi], A.is_gt),
                r=["S%d" % h, "fz"], x=["bk%d" % (2 * h)], w=["fd%d" % h])
 
         quant_x(0)
         quant_x(1)
-        for b in range(4):
-            layer(b, 0)
-        layer(0, 1)
-        layer(1, 1)
-        if t == 0:
-            late_constants()
+        for h in range(2):
+            for b in range(4):
+                layer(b, h)
         to_y("a", 0, 0)
         to_y("v", 1, 0)
         to_y("a", 2, 0)
+        if t == 0:
+            pick_u()
         to_y("v", 3, 0)
         quant_y(0)
-        scores(0)
-        layer(2, 1)
-        layer(3, 1)
+        scores(0, 0)
+        scores(0, 4)
+        send(qn[:, l0:h0].bitcast(u8), qy[:, l0:h0].bitcast(u8), "aq%d" % t, ["qy%d0" % t])
         to_y("a", 0, 1)
         to_y("a", 1, 1)
-        own_mask(0)
         to_y("a", 2, 1)
-        own_scan(0)
         to_y("v", 3, 1)
-        op("a", lambda: S.activation(T.pc[:, 0:H], bank(0, H), F.Copy), x=["bk0"], w=["pc0"])
-        op("a", lambda: S.activation(T.pc[:, C:C + 208], bank(0, 208), F.Copy), x=["bk0"], w=["pcx"])
         quant_y(1)
-        scores(1)
-        send(qn[:].bitcast(u8), qy[:].bitcast(u8), "aq%d" % t, ["qy%d0" % t, "qy%d1" % t])
+        scores(1, 2)
+        send(qn[:, l1:h1].bitcast(u8), qy[:, l1:h1].bitcast(u8), "aq%d" % t, ["qy%d1" % t])
         send(sn[:], sy[:], "aq%d" % t, [])
-        diag(0)
-        own_mask(1)
-        op("a", lambda: S.activation(T.pc[:, H:C], bank(2, H), F.Copy), x=["bk2"], w=["pc1"])
-        own_scan(1)
-        wr["qn%d" % t] = ("aq%d" % t, 2 * back)
+        if t == 0:
+            count(T.jc[:], [[1, C]], -256, 0, "jc")
+        op("a", lambda: S.activation(T.pc[:, 0:h0], bank(4, h0), F.Copy), x=["bk4"], w=["pc0"])
+        op("a", lambda: S.activation(T.pc[:, l1:h1], bank(2, h1 - l1), F.Copy), x=["bk2"], w=["pc1"])
+        op("a", lambda: S.activation(T.pc[:, C:C + 208], bank(4, 208), F.Copy), x=["bk4"], w=["pcx"])
+        own_mask(0)
+        own_scan(0)
+        wr["qn%d" % t] = ("aq%d" % t, 3 * back)
         for b in range(4):
             mm(4 + b, T.qe[:, 128 * b:128 * b + 128], T.se[:, 128 * b:128 * b + 128], qn[:], sn[:], C, ["e%d" % b, "qn%d" % t])
 
         zs = ["fz", "fz2", "fz3", "fz4"]
 
+        def flags(c):
+            op("v", lambda: V.tensor_scalar(slot(c, 16 * (c + 1), 16 * (c + 15)), T.pc[:, 16 * (c + 1):16 * (c + 15)],
+                                            T.S[:, 16 * c + 15:16 * c + 16], None, A.is_gt),
+               r=["pc0", "S0"] + (["pc1"] if 16 * (c + 15) > h0 else []) + zs, w=["f%d" % c])
+
+        def rowsum(c):
+            op("v", lambda: V.tensor_tensor_scan(T.rj[:, 112 * c:112 * c + 112], slot(c, 16 * (c + 1), 16 * (c + 8)),
+                                                 slot(c, 16 * (c + 8), 16 * (c + 15)), -16.0, A.add, A.add),
+               r=["f%d" % c], w=["rj%d" % c])
+
+        diag(0)
+        own_mask(1)
+        flags(0)
+        own_scan(1)
+
         def sign(c):
             op("a", lambda: S.activation(T.sg[:, 208 * (c - HB):208 * (c - HB + 1)], T.pc[:, 16 * (c + 1):16 * (c + HB)], F.Sign,
                                          bias=T.S[:, 16 * c + 15:16 * c + 16], scale=-1.0),
-               r=["pc1", "pcx", "S1"], w=["sg%d" % c])
+               r=["pc0", "pc1", "pcx", "S0" if 16 * c < h0 else "S1"], w=["sg%d" % c])
 
         def later(c):
             m = C - 16 * (c + 1)
@@ -273,18 +298,9 @@ def rank_program(g, core, T, topo):
             later(c)
         for c in range(NB - 1, HB, -1):
             earlier(c)
+        if t == 0:
+            widen_zm()
 
-        def flags(c):
-            op("v", lambda: V.tensor_scalar(slot(c, 16 * (c + 1), 16 * (c + 15)), T.pc[:, 16 * (c + 1):16 * (c + 15)],
-                                            T.S[:, 16 * c + 15:16 * c + 16], None, A.is_gt),
-               r=["pc0", "pc1", "S0"] + zs, w=["f%d" % c])
-
-        def rowsum(c):
-            op("v", lambda: V.tensor_tensor_scan(T.rj[:, 112 * c:112 * c + 112], slot(c, 16 * (c + 1), 16 * (c + 8)),
-                                                 slot(c, 16 * (c + 8), 16 * (c + 15)), -16.0, A.add, A.add),
-               r=["f%d" % c], w=["rj%d" % c])
-
-        flags(0)
         for c in range(1, HB):
             flags(c)
             rowsum(c - 1)
@@ -293,33 +309,35 @@ def rank_program(g, core, T, topo):
         op("v", lambda: V.tensor_tensor_scan(T.fr[:], T.rs01[:], T.fa[:, 7:8 * C:8], 0.0, A.mult, A.add), r=["rs01", "fd0", "fd1"], w=["fr"])
 
         def colscan(i):
-            lo, hi = 7 * i, 7 * i + 6
-            r = ["f%d" % c for c in range(HB) if c + 1 <= hi and c + HB >= lo]
-            r += ["f%da" % c for c in range(HB, NB - 1) if c + 1 <= hi]
+            lo, hi = RUNS[i]
+            r = ["f%d" % c for c in range(HB) if c + 1 < hi and c + HB >= lo]
+            r += ["f%da" % c for c in range(HB, NB - 1) if c + 1 < hi]
             r += ["f%db" % c for c in range(HB + 1, NB) if c - HB - 1 >= lo]
-            op("v", lambda: V.tensor_tensor_scan(T.cum[:, CW * i + 8:CW * (i + 1)], T.fa[:, 8 * CH * i:8 * CH * (i + 1)],
-                                                 T.fb[:, 8 * CH * i:8 * CH * (i + 1)], 16.0, A.add, A.add),
-               r=r + zs + ["fd%d" % (i // 2)], w=["cum%d" % i])
+            op("v", lambda: V.tensor_tensor_scan(T.cum[:, CW * i + 8:CW * i + 8 + 128 * (hi - lo)], T.fa[:, 128 * lo:128 * hi],
+                                                 T.fb[:, 128 * lo:128 * hi], 16.0, A.add, A.add),
+               r=r + zs + ["fd0", "fd1"], w=["cum%d" % i])
 
         def coldiff(i):
-            op("v", lambda: V.tensor_tensor_scan(T.cs[:, 16 + CH * i:16 + CH * (i + 1)], T.cum[:, CW * i + 15:CW * (i + 1):8],
-                                                 T.cum[:, CW * i + 7:CW * (i + 1) - 8:8], 0.0, A.max, A.subtract),
+            lo, hi = RUNS[i]
+            end = CW * i + 8 + 128 * (hi - lo)
+            op("v", lambda: V.tensor_tensor_scan(T.cs[:, 16 + 16 * lo:16 + 16 * hi], T.cum[:, CW * i + 15:end:8],
+                                                 T.cum[:, CW * i + 7:end - 8:8], 0.0, A.max, A.subtract),
                r=["cum%d" % i, "cum_i"], w=["cs%d" % i])
 
-        colscan(2)
-        op("v", lambda: V.tensor_tensor(T.base[:, 0:HB], T.rj[:, 111:112 * HB:112], T.fr[:, 15:H:16], A.add),
+        colscan(0)
+        op("v", lambda: V.tensor_tensor(T.base[:, 0:HB], T.rj[:, 111:112 * HB:112], T.fr[:, 15:16 * HB:16], A.add),
            r=["fr"] + ["rj%d" % c for c in range(HB)], w=["base0"])
+        colscan(1)
+        coldiff(0)
+        op("v", lambda: V.tensor_tensor(T.rk[:, HB:NB], T.ra[:, 0:HB], T.fr[:, 16 * HB + 15:C:16], A.add),
+           r=["fr"] + ["ra%d" % c for c in range(HB, NB)], w=["rk"])
+        colscan(2)
+        coldiff(1)
         colscan(3)
         coldiff(2)
-        op("v", lambda: V.tensor_tensor(T.rk[:, HB:NB], T.ra[:, 0:HB], T.fr[:, H + 15:C:16], A.add),
-           r=["fr"] + ["ra%d" % c for c in range(HB, NB)], w=["rk"])
-        colscan(1)
         coldiff(3)
-        colscan(0)
-        coldiff(1)
         op("v", lambda: V.tensor_tensor(T.base[:, HB:NB], T.rk[:, HB:NB], T.rb[:, 0:HB], A.add),
            r=["rk"] + ["rb%d" % c for c in range(HB, NB)], w=["base1"])
-        coldiff(0)
         css = ["cs%d" % i for i in range(4)] + ["cs_a", "cs_b"]
         op("v", lambda: V.transpose(T.tt[:, 0:C], T.cs[:, 16:16 + C]), r=css, w=["tt0"])
         op("v", lambda: V.transpose(T.tt[:, C:928], T.cs[:, 0:480]), r=css, w=["tt1"])
@@ -328,21 +346,20 @@ def rank_program(g, core, T, topo):
         op("v", lambda: V.tensor_tensor(T.col[:, 1:NB:2], T.zz[:, 31:C:32], T.zz[:, C + 47:928:32], A.add), r=["zz"], w=["col1"])
         op("v", lambda: V.tensor_tensor(T.rk[:, 0:NB], T.base[:, 0:NB], T.col[:, 0:NB], A.subtract), r=["base0", "base1", "col0", "col1"], w=["rk"])
         op("v", lambda: V.tensor_scalar(T.oi[:, 0:NB], T.rk[:, 0:NB], T.pf[:, 2:3], None, A.add), r=["rk", "cr"], w=["oi"])
-        op("v", lambda: V.tensor_scalar(T.oi64[:, 0:NB], T.rk[:, 0:NB], T.pf[:, 2:3], float(K), A.add, A.add), r=["rk", "cr"], w=["oi64"])
 
         op("v", lambda: V.tensor_copy(T.o[:, 0:C].indirect(T.oi[:, 0:NB]), T.jc[:]), r=["oi", "jc"], w=["o"])
         op("v", lambda: V.tensor_tensor(T.t1[:], T.o[:, 0:K], T.m01[:, 0:K], A.mult), r=["o", "m01"], w=["t1"])
-        op("v", lambda: V.tensor_tensor(T.b1[:], T.o[:, C - K:C], T.m01[:, 0:K], A.mult), r=["o", "m01"], w=["b1"])
         op("v", lambda: V.tensor_tensor_scan(T.t2[:], T.rs01[:, 0:K], T.t1[:], 0.0, A.mult, A.add), r=["t1", "rs01"], w=["t2"])
-        op("v", lambda: V.tensor_tensor_scan(T.b2[:], T.rs01[:, 0:K], T.b1[:], 0.0, A.mult, A.add), r=["b1", "rs01"], w=["b2"])
         op("v", lambda: V.tensor_scalar(ls[:, 0:4], T.t2[:, 15:K:16], 256.0, None, A.add), r=["t2"], w=["ls%d" % t])
         send(ln[:, 0:4], ls[:, 0:4], "al%d" % t, ["ls%d" % t])
         wr["ln%d" % t] = ("al%d" % t, back)
         for b in range(4):
             op("a", lambda: S.activation(T.dall[:, C * b:C * b + C], bank(4 + b, C), F.Copy), x=["bk%d" % (4 + b)], w=["dall%d" % b])
 
-        op("v", lambda: V.tensor_tensor(T.e1[:], T.o[:].indirect(T.oi64[:, 0:NB]), T.m01[:], A.mult), r=["o", "o_x", "oi64", "m01"], w=["e1"])
+        op("v", lambda: V.tensor_tensor(T.e1[:], T.o[:, K:512].indirect(T.oi[:, 0:NB]), T.m01[:], A.mult), r=["o", "o_x", "oi", "m01"], w=["e1"])
+        op("v", lambda: V.tensor_tensor(T.b1[:], T.o[:, C - K:C], T.m01[:, 0:K], A.mult), r=["o", "m01"], w=["b1"])
         op("v", lambda: V.tensor_tensor_scan(T.e2[:], T.rs01[:], T.e1[:], 0.0, A.mult, A.add), r=["e1", "rs01"], w=["e2"])
+        op("v", lambda: V.tensor_tensor_scan(T.b2[:], T.rs01[:, 0:K], T.b1[:], 0.0, A.mult, A.add), r=["b1", "rs01"], w=["b2"])
         ys = ["Y%d%d" % (b, h) for b in range(4) for h in range(2)]
         for b in (2, 0, 3, 1):
             op("v", lambda: V.tensor_scalar(T.ox[:, NB * b:NB * b + NB], T.e2[:, 15:C:16], 4.0, 1024.0 + b, A.mult, A.add), r=["e2"], w=["ox%d" % b])
@@ -359,9 +376,6 @@ def rank_program(g, core, T, topo):
             op("v", lambda: V.tensor_scalar(T.ob[:, 4 * b:4 * b + 4], T.b2[:, 15:K:16], 4.0, 1024.0 + b, A.mult, A.add), r=["b2"], w=["ob%d" % b])
         if t == 0:
             op("v", lambda: V.quantize_mx(T.qv[:], T.sv[:], T.vt[:]), r=["vt"], w=["qv"])
-        if t == R - 1:
-            op("a", lambda: S.activation(T.of[:], T.o[:, 0:C], F.Identity, bias=256.0), r=["o"], w=["of"])
-            dma("s", T.ol[:], T.of[0:128:16, :], r=["of"])
         for b in (0, 2, 1, 3):
             out, src = T.dsel[:, K * b:K * b + K], T.dall[:, C * b:C * b + C].indirect(ln[:, 0:4])
             r = ["dall%d" % b, "ln%d" % t]
@@ -372,16 +386,20 @@ def rank_program(g, core, T, topo):
         op("v", lambda: V.tensor_copy(T.X[:].indirect(T.ob[:]), T.dsel[:]),
            r=["ds%d" % b for b in range(4)] + ["ob%d" % b for b in range(4)] + ["Xg%d" % b for b in range(4)], w=["Xs"])
 
+    op("a", lambda: S.activation(T.of[:], T.o[:, 0:C], F.Identity, bias=256.0), r=["o"], w=["of"])
+    dma("s", T.ol[:], T.of[0:128:16, :], r=["of"])
     quant_x(0)
     quant_x(1)
     for h in range(2):
-        mm(h, T.qv[:], T.sv[:], T.qx[:, H * h:H * h + H], T.sx[:, H * h:H * h + H], H, ["qv", "qx%d" % h])
+        lo, hi = PART[h]
+        mm(h, T.qv[:], T.sv[:], T.qx[:, lo:hi], T.sx[:, lo:hi], hi - lo, ["qv", "qx%d" % h])
+    op("a", lambda: S.activation(T.yo[:, l0:h0], bank(0, h0), F.Copy), x=["bk0"], w=["yo0"])
+    op("v", lambda: V.tensor_copy(T.yo[:, l1:h1], bank(1, h1 - l1)), x=["bk1"], w=["yo1"])
     dma("s", T.oc[:], T.qx[:].bitcast(u8), r=["qx0", "qx1"])
+    dma("a", T.y[:, l0:h0], T.yo[:, l0:h0], r=["yo0"])
+    dma("s", T.y[:, l1:h1], T.yo[:, l1:h1], r=["yo1"])
     for k in range(4):
         dma("a" if k < 2 else "s", T.osc[4 * k:4 * k + 4, :], T.sx[32 * k:32 * k + 4, :], r=["qx0", "qx1"])
-    for h in range(2):
-        op("v", lambda: V.tensor_copy(T.yo[:, H * h:H * h + H], bank(h, H)), x=["bk%d" % h], w=["yo%d" % h])
-    dma("a", T.y[:], T.yo[:], r=["yo0", "yo1"])
 
     for q in cnt:
         wait("g", (csem[q], cnt[q]))

@@ -4,6 +4,8 @@ C, K, R = 448, 64, 3
 PART = ((0, 288), (288, 448))
 NB = C // 16
 HB = NB // 2
+SB, SE = HB + 1, NB - 1
+W0, WN, WL = 256, 192, 208
 BIG = 2.0 ** 90
 RUNS = ((14, 21), (21, 28), (5, 14), (0, 5))
 CW = 8 * 144 + 8
@@ -23,16 +25,15 @@ SCRATCH = {
     "ui": ("sbuf", [128, 8], "int32"), "uo": ("sbuf", [128, 8], "uint16"),
     "rr": ("sbuf", [128, C], "float32"), "idn": ("sbuf", [128, 128], "float32"), "hh": ("sbuf", [128, 32], "float32"),
     "jc": ("sbuf", [128, C], "bfloat16"), "m01": ("sbuf", [128, C], "bfloat16"), "rs01": ("sbuf", [128, C], "bfloat16"),
-    "mpm": ("sbuf", [128, 288], "float32"), "mrs": ("sbuf", [128, 288], "float32"), "zm": ("sbuf", [128, 928], "bfloat16"),
-    "d1": ("sbuf", [128, C], "float32"), "S": ("sbuf", [128, C], "float32"), "pc": ("sbuf", [128, C + 208], "float32"),
+    "mpm": ("sbuf", [128, 288], "float32"), "mrs": ("sbuf", [128, 288], "float32"), "zm": ("sbuf", [128, 480], "bfloat16"),
+    "d1": ("sbuf", [128, C], "float32"), "S": ("sbuf", [128, C], "float32"), "pc": ("sbuf", [128, 2 * WN], "float32"),
     "fa": ("sbuf", [128, 8 * C], "bfloat16"), "fb": ("sbuf", [128, 8 * C], "bfloat16"),
-    "sg": ("sbuf", [128, HB * 208], "bfloat16"), "rj": ("sbuf", [128, HB * 112], "bfloat16"),
+    "sg": ("sbuf", [128, 12 * WL], "bfloat16"), "rj": ("sbuf", [128, 16 * 112], "bfloat16"),
     "fr": ("sbuf", [128, C], "bfloat16"), "ra": ("sbuf", [128, 16], "float32"), "rb": ("sbuf", [128, 16], "float32"),
     "cum": ("sbuf", [128, 4 * CW], "float16"), "cs": ("sbuf", [128, C + 32], "bfloat16"),
     "tt": ("sbuf", [128, 928], "bfloat16"), "zz": ("sbuf", [128, 928], "bfloat16"),
     "base": ("sbuf", [128, 32], "float32"), "col": ("sbuf", [128, 32], "float32"), "rk": ("sbuf", [128, 32], "float32"),
-    "oi": ("sbuf", [128, 32], "uint16"),
-    "o": ("sbuf", [128, 512], "bfloat16"),
+    "oi": ("sbuf", [128, 32], "uint16"), "o": ("sbuf", [128, 512], "bfloat16"),
     "t1": ("sbuf", [128, K], "bfloat16"), "t2": ("sbuf", [128, K], "bfloat16"),
     "b1": ("sbuf", [128, K], "bfloat16"), "b2": ("sbuf", [128, K], "bfloat16"),
     "e1": ("sbuf", [128, C], "bfloat16"), "e2": ("sbuf", [128, C], "bfloat16"),
@@ -48,7 +49,7 @@ for _t in range(R):
     SCRATCH["ls%d" % _t] = ("sbuf", [128, 8], "uint16")
     SCRATCH["ln%d" % _t] = ("sbuf", [128, 8], "uint16")
 
-SEMAPHORES = (["cv", "ca", "cp", "cg", "sent"] + ["d%d" % i for i in range(16)]
+SEMAPHORES = (["cv", "ca", "cp", "cg", "sent"] + ["d%d" % i for i in range(18)]
               + ["aq%d" % t for t in range(R)] + ["al%d" % t for t in range(R)])
 
 
@@ -114,8 +115,8 @@ def rank_program(g, core, T, topo):
     V, S = g.vector, g.scalar
     u8, u32 = dt.uint8, dt.uint32
 
-    def bank(b, m):
-        return T.ps[:, 512 * b:512 * b + m]
+    def bank(b, hi, lo=0):
+        return T.ps[:, 512 * b + lo:512 * b + hi]
 
     def slot(c, lo, hi):
         s = c % HB
@@ -157,8 +158,6 @@ def rank_program(g, core, T, topo):
     op("v", lambda: V.memset(T.cum[:, 7:4 * CW:CW], 16.0), w=["cum_i"])
     op("v", lambda: V.memset(T.cs[:, 0:16], 0.0), w=["cs_a"])
     op("v", lambda: V.memset(T.cs[:, C + 16:C + 32], 0.0), w=["cs_b"])
-    op("v", lambda: V.memset(T.ra[:], 0.0), w=["ra%d" % c for c in range(HB, NB)])
-    op("v", lambda: V.memset(T.rb[:], 0.0), w=["rb%d" % c for c in range(HB, NB)])
     op("v", lambda: V.memset(T.o[:, C:512], -256.0), w=["o_x"])
     op("v", lambda: V.tensor_copy(T.uo[:], T.ui[:]), r=["ui"], w=["uo"])
     op("v", lambda: V.tensor_scalar(T.zm[:, 0:32], T.hh[:], T.pf[:, 1:2], None, A.is_equal), r=["hh", "pf"], w=["zm"])
@@ -168,8 +167,8 @@ def rank_program(g, core, T, topo):
 
     def widen_zm():
         have = 32
-        while have < 928:
-            m = min(have, 928 - have)
+        while have < 480:
+            m = min(have, 480 - have)
             op("a", lambda: S.activation(T.zm[:, have:have + m], T.zm[:, 0:m], F.Copy), r=["zm"], w=["zm"])
             have += m
 
@@ -207,14 +206,17 @@ def rank_program(g, core, T, topo):
             op("v", lambda: V.quantize_mx(qy[:, lo:hi], sy[:, lo:hi], T.Y[:, 4 * lo:4 * hi]),
                r=["Y%d%d" % (b, h) for b in range(4)], w=["qy%d%d" % (t, h)])
 
-        def scores(h, b):
-            lo, hi = PART[h]
-            mm(b, T.qu2[:], T.su2[:], qy[:, lo:hi], sy[:, lo:hi], hi - lo, ["qu2", "su2", "qy%d%d" % (t, h)])
+        def scores(b, lo, hi):
+            mm(b, T.qu2[:], T.su2[:], qy[:, lo:hi], sy[:, lo:hi], hi - lo,
+               ["qu2", "su2", "qy%d0" % t] + (["qy%d1" % t] if hi > h0 else []))
+
+        def own(h):
+            return bank(h, PART[h][1], PART[h][0])
 
         def own_mask(h):
             lo, hi = PART[h]
-            op("v", lambda: V.tensor_tensor(T.d1[:, lo:hi], bank(2 * h, hi - lo), T.mpm[:, 0:hi - lo], A.max),
-               r=["mpm"], x=["bk%d" % (2 * h)], w=["d1%d" % h])
+            op("v", lambda: V.tensor_tensor(T.d1[:, lo:hi], own(h), T.mpm[:, 0:hi - lo], A.max),
+               r=["mpm"], x=["bk%d" % h], w=["d1%d" % h])
 
         def own_scan(h):
             lo, hi = PART[h]
@@ -223,8 +225,8 @@ def rank_program(g, core, T, topo):
 
         def diag(h):
             lo, hi = PART[h]
-            op("v", lambda: V.tensor_tensor(T.fa[:, 8 * lo + 7:8 * hi:8], bank(2 * h, hi - lo), T.S[:, lo:hi], A.is_gt),
-               r=["S%d" % h, "fz"], x=["bk%d" % (2 * h)], w=["fd%d" % h])
+            op("v", lambda: V.tensor_tensor(T.fa[:, 8 * lo + 7:8 * hi:8], own(h), T.S[:, lo:hi], A.is_gt),
+               r=["S%d" % h, "fz"], x=["bk%d" % h], w=["fd%d" % h])
 
         quant_x(0)
         quant_x(1)
@@ -238,22 +240,22 @@ def rank_program(g, core, T, topo):
             pick_u()
         to_y("v", 3, 0)
         quant_y(0)
-        scores(0, 0)
-        scores(0, 4)
+        scores(0, l0, h0)
+        scores(4, 0, WN)
         send(qn[:, l0:h0].bitcast(u8), qy[:, l0:h0].bitcast(u8), "aq%d" % t, ["qy%d0" % t])
         to_y("a", 0, 1)
         to_y("a", 1, 1)
         to_y("a", 2, 1)
         to_y("v", 3, 1)
         quant_y(1)
-        scores(1, 2)
+        scores(2, W0, C)
+        scores(1, 0, C)
         send(qn[:, l1:h1].bitcast(u8), qy[:, l1:h1].bitcast(u8), "aq%d" % t, ["qy%d1" % t])
         send(sn[:], sy[:], "aq%d" % t, [])
         if t == 0:
             count(T.jc[:], [[1, C]], -256, 0, "jc")
-        op("a", lambda: S.activation(T.pc[:, 0:h0], bank(4, h0), F.Copy), x=["bk4"], w=["pc0"])
-        op("a", lambda: S.activation(T.pc[:, l1:h1], bank(2, h1 - l1), F.Copy), x=["bk2"], w=["pc1"])
-        op("a", lambda: S.activation(T.pc[:, C:C + 208], bank(4, 208), F.Copy), x=["bk4"], w=["pcx"])
+        op("a", lambda: S.activation(T.pc[:, WN:2 * WN], bank(4, WN), F.Copy), x=["bk4"], w=["pcx"])
+        op("a", lambda: S.activation(T.pc[:, 0:WN], bank(2, WN), F.Copy), x=["bk2"], w=["pc1"])
         own_mask(0)
         own_scan(0)
         wr["qn%d" % t] = ("aq%d" % t, 3 * back)
@@ -262,57 +264,66 @@ def rank_program(g, core, T, topo):
 
         zs = ["fz", "fz2", "fz3", "fz4"]
 
+        def span(c):
+            return (0, WL) if c == SE else (16 * (c + 1), min(16 * (c + 15), C))
+
         def flags(c):
-            op("v", lambda: V.tensor_scalar(slot(c, 16 * (c + 1), 16 * (c + 15)), T.pc[:, 16 * (c + 1):16 * (c + 15)],
-                                            T.S[:, 16 * c + 15:16 * c + 16], None, A.is_gt),
-               r=["pc0", "S0"] + (["pc1"] if 16 * (c + 15) > h0 else []) + zs, w=["f%d" % c])
+            lo, hi = span(c)
+            op("v", lambda: V.tensor_scalar(slot(c, lo, hi), bank(1, hi, lo), T.S[:, 16 * c + 15:16 * c + 16], None,
+                                            A.is_ge if c == SE else A.is_gt),
+               r=["S1" if c == SE else "S0"] + zs, x=["bk1"], w=["f%d" % c])
 
         def rowsum(c):
-            op("v", lambda: V.tensor_tensor_scan(T.rj[:, 112 * c:112 * c + 112], slot(c, 16 * (c + 1), 16 * (c + 8)),
-                                                 slot(c, 16 * (c + 8), 16 * (c + 15)), -16.0, A.add, A.add),
-               r=["f%d" % c], w=["rj%d" % c])
+            lo, hi = span(c)
+            m, end = (hi - lo) // 2, 112 * min(c, SB) + 112
+            op("v", lambda: V.tensor_tensor_scan(T.rj[:, end - m:end], slot(c, lo, lo + m), slot(c, lo + m, hi),
+                                                 -16.0 if c < HB else 0.0, A.add, A.add), r=["f%d" % c], w=["rj%d" % c])
 
-        diag(0)
         own_mask(1)
-        flags(0)
+        diag(0)
         own_scan(1)
+        flags(0)
 
         def sign(c):
-            op("a", lambda: S.activation(T.sg[:, 208 * (c - HB):208 * (c - HB + 1)], T.pc[:, 16 * (c + 1):16 * (c + HB)], F.Sign,
+            op("a", lambda: S.activation(T.sg[:, WL * (c - SB):WL * (c - SB + 1)], T.pc[:, 16 * (c - SB):16 * (c - SB) + WL], F.Sign,
                                          bias=T.S[:, 16 * c + 15:16 * c + 16], scale=-1.0),
-               r=["pc0", "pc1", "pcx", "S0" if 16 * c < h0 else "S1"], w=["sg%d" % c])
+               r=["pc1", "pcx", "S0" if 16 * c < h0 else "S1"], w=["sg%d" % c])
 
         def later(c):
             m = C - 16 * (c + 1)
-            op("a", lambda: S.activation(slot(c, 16 * (c + 1), C), T.sg[:, 208 * (c - HB):208 * (c - HB) + m], F.Relu, scale=-1.0,
-                                         accum_out=T.ra[:, c - HB:c - HB + 1]), r=["sg%d" % c] + zs, w=["f%da" % c, "ra%d" % c])
+            op("a", lambda: S.activation(slot(c, 16 * (c + 1), C), T.sg[:, WL * (c - SB):WL * (c - SB) + m], F.Relu, scale=-1.0,
+                                         accum_out=T.ra[:, c - SB:c - SB + 1]), r=["sg%d" % c] + zs, w=["f%da" % c, "ra%d" % c])
 
         def earlier(c):
-            m = 16 * (c - HB)
-            op("a", lambda: S.activation(slot(c, 0, m), T.sg[:, 208 * (c - HB + 1) - m:208 * (c - HB + 1)], F.Sign, bias=1.0, scale=-1.0,
-                                         accum_out=T.rb[:, c - HB:c - HB + 1]), r=["sg%d" % c] + zs, w=["f%db" % c, "rb%d" % c])
+            m, end = 16 * (c - HB), WL * (c - SB + 1)
+            op("a", lambda: S.activation(slot(c, 0, m), T.sg[:, end - m:end], F.Sign, bias=1.0, scale=-1.0,
+                                         accum_out=T.rb[:, c - SB:c - SB + 1]), r=["sg%d" % c] + zs, w=["f%db" % c, "rb%d" % c])
 
-        sign(HB)
-        for c in range(HB, NB - 1):
-            sign(c + 1)
+        sign(SB)
+        for c in range(SB, SE):
+            if c + 1 < SE:
+                sign(c + 1)
             later(c)
-        for c in range(NB - 1, HB, -1):
+        for c in range(SE - 1, HB, -1):
             earlier(c)
         if t == 0:
             widen_zm()
+        for b in range(4):
+            op("a", lambda: S.activation(T.dall[:, C * b:C * b + C], bank(4 + b, C), F.Copy), x=["bk%d" % (4 + b)], w=["dall%d" % b])
 
-        for c in range(1, HB):
-            flags(c)
-            rowsum(c - 1)
+        mine = list(range(SB)) + [SE]
+        for k in range(1, len(mine)):
+            flags(mine[k])
+            rowsum(mine[k - 1])
         diag(1)
-        rowsum(HB - 1)
+        rowsum(SE)
         op("v", lambda: V.tensor_tensor_scan(T.fr[:], T.rs01[:], T.fa[:, 7:8 * C:8], 0.0, A.mult, A.add), r=["rs01", "fd0", "fd1"], w=["fr"])
 
         def colscan(i):
             lo, hi = RUNS[i]
-            r = ["f%d" % c for c in range(HB) if c + 1 < hi and c + HB >= lo]
-            r += ["f%da" % c for c in range(HB, NB - 1) if c + 1 < hi]
-            r += ["f%db" % c for c in range(HB + 1, NB) if c - HB - 1 >= lo]
+            r = ["f%d" % c for c in mine]
+            r += ["f%da" % c for c in range(SB, SE) if c + 1 < hi]
+            r += ["f%db" % c for c in range(SB, SE) if c - HB - 1 >= lo]
             op("v", lambda: V.tensor_tensor_scan(T.cum[:, CW * i + 8:CW * i + 8 + 128 * (hi - lo)], T.fa[:, 128 * lo:128 * hi],
                                                  T.fb[:, 128 * lo:128 * hi], 16.0, A.add, A.add),
                r=r + zs + ["fd0", "fd1"], w=["cum%d" % i])
@@ -325,55 +336,62 @@ def rank_program(g, core, T, topo):
                r=["cum%d" % i, "cum_i"], w=["cs%d" % i])
 
         colscan(0)
-        op("v", lambda: V.tensor_tensor(T.base[:, 0:HB], T.rj[:, 111:112 * HB:112], T.fr[:, 15:16 * HB:16], A.add),
-           r=["fr"] + ["rj%d" % c for c in range(HB)], w=["base0"])
+        op("v", lambda: V.tensor_tensor(T.base[:, 0:SB], T.rj[:, 111:112 * SB:112], T.fr[:, 15:16 * SB:16], A.add),
+           r=["fr"] + ["rj%d" % c for c in range(SB)], w=["base0"])
+        op("v", lambda: V.tensor_tensor(T.base[:, SE:NB], T.rj[:, 112 * SB + 111:112 * SB + 112], T.fr[:, C - 1:C], A.add),
+           r=["fr", "rj%d" % SE], w=["base2"])
         colscan(1)
         coldiff(0)
-        op("v", lambda: V.tensor_tensor(T.rk[:, HB:NB], T.ra[:, 0:HB], T.fr[:, 16 * HB + 15:C:16], A.add),
-           r=["fr"] + ["ra%d" % c for c in range(HB, NB)], w=["rk"])
+        op("v", lambda: V.tensor_tensor(T.rk[:, SB:SE], T.ra[:, 0:SE - SB], T.fr[:, 16 * SB + 15:16 * SE:16], A.add),
+           r=["fr"] + ["ra%d" % c for c in range(SB, SE)], w=["rk", "rk1"])
         colscan(2)
         coldiff(1)
         colscan(3)
         coldiff(2)
         coldiff(3)
-        op("v", lambda: V.tensor_tensor(T.base[:, HB:NB], T.rk[:, HB:NB], T.rb[:, 0:HB], A.add),
-           r=["rk"] + ["rb%d" % c for c in range(HB, NB)], w=["base1"])
+        op("v", lambda: V.tensor_tensor(T.base[:, SB:SE], T.rk[:, SB:SE], T.rb[:, 0:SE - SB], A.add),
+           r=["rk"] + ["rb%d" % c for c in range(SB, SE)], w=["base1"])
         css = ["cs%d" % i for i in range(4)] + ["cs_a", "cs_b"]
+        bs = ["base0", "base1", "base2"]
         op("v", lambda: V.transpose(T.tt[:, 0:C], T.cs[:, 16:16 + C]), r=css, w=["tt0"])
         op("v", lambda: V.transpose(T.tt[:, C:928], T.cs[:, 0:480]), r=css, w=["tt1"])
-        op("v", lambda: V.tensor_tensor_scan(T.zz[:], T.tt[:], T.zm[:], 0.0, A.add, A.mult), r=["tt0", "tt1", "zm"], w=["zz"])
-        op("v", lambda: V.tensor_tensor(T.col[:, 0:NB:2], T.zz[:, 15:C:32], T.zz[:, C + 31:C + 448:32], A.add), r=["zz"], w=["col0"])
-        op("v", lambda: V.tensor_tensor(T.col[:, 1:NB:2], T.zz[:, 31:C:32], T.zz[:, C + 47:928:32], A.add), r=["zz"], w=["col1"])
-        op("v", lambda: V.tensor_tensor(T.rk[:, 0:NB], T.base[:, 0:NB], T.col[:, 0:NB], A.subtract), r=["base0", "base1", "col0", "col1"], w=["rk"])
-        op("v", lambda: V.tensor_scalar(T.oi[:, 0:NB], T.rk[:, 0:NB], T.pf[:, 2:3], None, A.add), r=["rk", "cr"], w=["oi"])
+        op("v", lambda: V.tensor_tensor_scan(T.zz[:, 0:C], T.tt[:, 0:C], T.zm[:, 0:C], 0.0, A.add, A.mult), r=["tt0", "zm"], w=["zz0"])
+        op("v", lambda: V.tensor_tensor_scan(T.zz[:, C:928], T.tt[:, C:928], T.zm[:], 0.0, A.add, A.mult), r=["tt1", "zm"], w=["zz1"])
+        op("v", lambda: V.tensor_tensor(T.col[:, 0:NB:2], T.base[:, 0:NB:2], T.zz[:, 15:C:32], A.subtract), r=["zz0"] + bs, w=["col0"])
+        op("v", lambda: V.tensor_tensor(T.col[:, 1:NB:2], T.base[:, 1:NB:2], T.zz[:, 31:C:32], A.subtract), r=["zz0"] + bs, w=["col1"])
+        op("v", lambda: V.tensor_tensor(T.rk[:, 0:NB:2], T.col[:, 0:NB:2], T.zz[:, C + 31:C + 448:32], A.subtract), r=["zz1", "col0"], w=["rk"])
+        op("v", lambda: V.tensor_tensor(T.rk[:, 1:NB:2], T.col[:, 1:NB:2], T.zz[:, C + 47:928:32], A.subtract), r=["zz1", "col1", "base1"], w=["rk1"])
+        op("v", lambda: V.tensor_scalar(T.oi[:, 0:NB], T.rk[:, 0:NB], T.pf[:, 2:3], None, A.add), r=["rk", "rk1", "cr"], w=["oi"])
 
         op("v", lambda: V.tensor_copy(T.o[:, 0:C].indirect(T.oi[:, 0:NB]), T.jc[:]), r=["oi", "jc"], w=["o"])
         op("v", lambda: V.tensor_tensor(T.t1[:], T.o[:, 0:K], T.m01[:, 0:K], A.mult), r=["o", "m01"], w=["t1"])
+        op("v", lambda: V.tensor_tensor(T.b1[:], T.o[:, C - K:C], T.m01[:, 0:K], A.mult), r=["o", "m01"], w=["b1"])
         op("v", lambda: V.tensor_tensor_scan(T.t2[:], T.rs01[:, 0:K], T.t1[:], 0.0, A.mult, A.add), r=["t1", "rs01"], w=["t2"])
+        op("v", lambda: V.tensor_tensor_scan(T.b2[:], T.rs01[:, 0:K], T.b1[:], 0.0, A.mult, A.add), r=["b1", "rs01"], w=["b2"])
         op("v", lambda: V.tensor_scalar(ls[:, 0:4], T.t2[:, 15:K:16], 256.0, None, A.add), r=["t2"], w=["ls%d" % t])
         send(ln[:, 0:4], ls[:, 0:4], "al%d" % t, ["ls%d" % t])
         wr["ln%d" % t] = ("al%d" % t, back)
-        for b in range(4):
-            op("a", lambda: S.activation(T.dall[:, C * b:C * b + C], bank(4 + b, C), F.Copy), x=["bk%d" % (4 + b)], w=["dall%d" % b])
+
+        def places(b):
+            op("v", lambda: V.tensor_scalar(T.ob[:, 4 * b:4 * b + 4], T.b2[:, 15:K:16], 4.0, 1024.0 + b, A.mult, A.add), r=["b2"], w=["ob%d" % b])
 
         op("v", lambda: V.tensor_tensor(T.e1[:], T.o[:, K:512].indirect(T.oi[:, 0:NB]), T.m01[:], A.mult), r=["o", "o_x", "oi", "m01"], w=["e1"])
-        op("v", lambda: V.tensor_tensor(T.b1[:], T.o[:, C - K:C], T.m01[:, 0:K], A.mult), r=["o", "m01"], w=["b1"])
+        places(0)
         op("v", lambda: V.tensor_tensor_scan(T.e2[:], T.rs01[:], T.e1[:], 0.0, A.mult, A.add), r=["e1", "rs01"], w=["e2"])
-        op("v", lambda: V.tensor_tensor_scan(T.b2[:], T.rs01[:, 0:K], T.b1[:], 0.0, A.mult, A.add), r=["b1", "rs01"], w=["b2"])
+        places(1)
         ys = ["Y%d%d" % (b, h) for b in range(4) for h in range(2)]
         for b in (2, 0, 3, 1):
             op("v", lambda: V.tensor_scalar(T.ox[:, NB * b:NB * b + NB], T.e2[:, 15:C:16], 4.0, 1024.0 + b, A.mult, A.add), r=["e2"], w=["ox%d" % b])
+        order("v", (), ["X0", "X1", "Xs"], ())
+        order("a", (), ["X0", "X1", "Xs"], ())
         for b in range(4):
             out, src = T.X[:, b:4 * C:4], T.Y[:].indirect(T.ox[:, NB * b:NB * b + NB])
-            w = ["Xg%d" % b]
             if b < 2:
-                order("v", (), ["X0", "X1", "Xs"], ())
-                op("v", lambda: V.tensor_copy(out, src), r=ys + ["ox%d" % b], w=w)
+                op("v", lambda: V.tensor_copy(out, src), r=ys + ["ox%d" % b], w=["Xg%d" % b])
             else:
-                order("a", (), ["X0", "X1", "Xs"], ())
-                op("a", lambda: S.activation(out, src, F.Copy), r=ys + ["ox%d" % b], w=w)
-        for b in range(4):
-            op("v", lambda: V.tensor_scalar(T.ob[:, 4 * b:4 * b + 4], T.b2[:, 15:K:16], 4.0, 1024.0 + b, A.mult, A.add), r=["b2"], w=["ob%d" % b])
+                op("a", lambda: S.activation(out, src, F.Copy), r=ys + ["ox%d" % b], w=["Xg%d" % b])
+        places(2)
+        places(3)
         if t == 0:
             op("v", lambda: V.quantize_mx(T.qv[:], T.sv[:], T.vt[:]), r=["vt"], w=["qv"])
         for b in (0, 2, 1, 3):

@@ -1,18 +1,34 @@
 from concourse.mybir import dt, AluOpType as A, ActivationFunctionType as F
 
 C, K, R = 448, 64, 3
-PART = ((0, 288), (288, 448))
+PART = ((0, 128), (128, 288), (288, 448))
 NB = C // 16
 HB = NB // 2
-SB, SE = HB + 1, NB - 1
-W0, WN, WL = 256, 192, 208
+H = C // 2
+Q4 = C // 4
+FRONT = (
+    "x0 L0 e0 ya00 yv10 e1 e2 x1 ya20 ya30 L1 e3 c_ u_ q0 t0-128 P4:0-128 ya01 ya11 x2 ya21 m0 ya31 s0 L2 q1 P6:0-288 P5:0-288 "
+    "t128-288 ya02 yv12 ya22 yv32 m1 s1 q2 P4:224-448 P7:80-448 t288-448 T_ dA m2 rA s2 dB rB S_",
+    "x0 L0 x1 ya00 x2 yv10 ya20 yv30 L1 q0 t0-128 ya01 yv11 P4:0-128 ya21 ya31 m0 L2 s0 ya02 ya12 q1 P6:0-288 P5:0-288 "
+    "t128-288 yv22 yv32 q2 m1 P4:224-448 P7:80-448 t288-448 T_ s1 m2 dA s2 rA dB rB S_",
+)
+EARLY = (224,)
+OUT = ((0, 160), (160, 320), (320, 448))
+END = "x0 ya0 x1 cs01 ya1 x2 Ys01 cs2 yv2 Ya2 sa0 sa1 ss2 ss3"
+SROWS = ([0, 1, 2, 3, 14] + list(range(4, 14)),) * R
+VROWS = (list(range(15, 28)),) * R
+LAG = (2, 2, 2)
+STEP = 2
 BIG = 2.0 ** 90
-RUNS = ((14, 21), (21, 28), (5, 14), (0, 5))
-CW = 8 * 144 + 8
+UP, DOWN = 1024.0, -1600.0
+NP = HB + 1
+CUTS = (420, 366, 312, 258, 204, 150, 96, 56, 14)
+EV = 28
+MW = 192
 
 SCRATCH = {
     "ps": ("psum", [128, 4096], "float32"),
-    "X": ("sbuf", [128, 4 * C], "bfloat16"), "Y": ("sbuf", [128, 4 * C], "bfloat16"),
+    "X": ("sbuf", [128, 4 * C], "bfloat16"),
     "qx": ("sbuf", [128, C], "float8_e4m3fn_x4"), "sx": ("sbuf", [128, C], "uint8"),
     "qw": ("sbuf", [128, 512], "float8_e4m3fn_x4"), "sw": ("sbuf", [128, 512], "uint8"),
     "ut": ("sbuf", [128, 512], "bfloat16"), "vt": ("sbuf", [128, 512], "bfloat16"),
@@ -21,35 +37,39 @@ SCRATCH = {
     "qv": ("sbuf", [128, 128], "float8_e4m3fn_x4"), "sv": ("sbuf", [128, 128], "uint8"),
     "et": ("sbuf", [128, 516], "bfloat16"),
     "qe": ("sbuf", [128, 512], "float8_e4m3fn_x4"), "se": ("sbuf", [128, 512], "uint8"),
-    "pi": ("sbuf", [128, 8], "int32"), "pf": ("sbuf", [128, 8], "float32"),
+    "ct": ("sbuf", [128, 512], "bfloat16"),
+    "qc": ("sbuf", [128, 128], "float8_e4m3fn_x4"), "sc": ("sbuf", [128, 128], "uint8"),
+    "pi": ("sbuf", [128, 8], "int32"), "pf": ("sbuf", [128, 16], "float32"),
     "ui": ("sbuf", [128, 8], "int32"), "uo": ("sbuf", [128, 8], "uint16"),
-    "rr": ("sbuf", [128, C], "float32"), "idn": ("sbuf", [128, 128], "float32"), "hh": ("sbuf", [128, 32], "float32"),
-    "jc": ("sbuf", [128, C], "bfloat16"), "m01": ("sbuf", [128, C], "bfloat16"), "rs01": ("sbuf", [128, C], "bfloat16"),
-    "mpm": ("sbuf", [128, 288], "float32"), "mrs": ("sbuf", [128, 288], "float32"), "zm": ("sbuf", [128, 480], "bfloat16"),
-    "d1": ("sbuf", [128, C], "float32"), "S": ("sbuf", [128, C], "float32"), "pc": ("sbuf", [128, 2 * WN], "float32"),
-    "fa": ("sbuf", [128, 8 * C], "bfloat16"), "fb": ("sbuf", [128, 8 * C], "bfloat16"),
-    "sg": ("sbuf", [128, 12 * WL], "bfloat16"), "rj": ("sbuf", [128, 16 * 112], "bfloat16"),
-    "fr": ("sbuf", [128, C], "bfloat16"), "ra": ("sbuf", [128, 16], "float32"), "rb": ("sbuf", [128, 16], "float32"),
-    "cum": ("sbuf", [128, 4 * CW], "float16"), "cs": ("sbuf", [128, C + 32], "bfloat16"),
-    "tt": ("sbuf", [128, 928], "bfloat16"), "zz": ("sbuf", [128, 928], "bfloat16"),
-    "base": ("sbuf", [128, 32], "float32"), "col": ("sbuf", [128, 32], "float32"), "rk": ("sbuf", [128, 32], "float32"),
+    "rr": ("sbuf", [128, MW], "float32"), "idn": ("sbuf", [128, 128], "float32"),
+    "gq": ("sbuf", [128, 32], "float32"), "gm": ("sbuf", [128, 32], "float32"),
+    "i4": ("sbuf", [128, 4], "float32"), "ka": ("sbuf", [128, 12], "float32"),
+    "jc": ("sbuf", [128, C], "bfloat16"), "m01": ("sbuf", [128, MW], "float32"),
+    "mpm": ("sbuf", [128, MW], "float32"), "mrs": ("sbuf", [128, MW], "float32"),
+    "mh": ("sbuf", [128, C], "bfloat16"), "mz": ("sbuf", [128, Q4], "float32"), "rs": ("sbuf", [128, C], "bfloat16"),
+    "d1": ("sbuf", [128, C], "float32"), "S": ("sbuf", [128, C], "float32"),
+    "fl": ("sbuf", [128, NP * C + 64], "bfloat16"),
+    "qf": ("sbuf", [128, NP * Q4 + 16], "float8_e4m3fn_x4"), "sf": ("sbuf", [128, NP * Q4 + 16], "uint8"),
+    "rj": ("sbuf", [128, NB * Q4], "bfloat16"), "fr": ("sbuf", [128, C], "float16"), "ra": ("sbuf", [128, 32], "float32"),
+    "zz": ("sbuf", [128, Q4], "float32"),
     "oi": ("sbuf", [128, 32], "uint16"), "o": ("sbuf", [128, 512], "bfloat16"),
-    "t1": ("sbuf", [128, K], "bfloat16"), "t2": ("sbuf", [128, K], "bfloat16"),
-    "b1": ("sbuf", [128, K], "bfloat16"), "b2": ("sbuf", [128, K], "bfloat16"),
-    "e1": ("sbuf", [128, C], "bfloat16"), "e2": ("sbuf", [128, C], "bfloat16"),
-    "ox": ("sbuf", [128, 4 * NB], "uint16"), "ob": ("sbuf", [128, 16], "uint16"),
-    "dall": ("sbuf", [128, 4 * C], "bfloat16"), "dsel": ("sbuf", [128, 4 * K], "bfloat16"),
+    "t2": ("sbuf", [128, K], "float16"),
+    "e1": ("sbuf", [128, C], "bfloat16"), "e2": ("sbuf", [128, C], "float16"),
+    "ox": ("sbuf", [128, Q4], "uint16"),
+    "b2": ("sbuf", [128, K], "float16"), "ob": ("sbuf", [128, 16], "uint16"), "ds": ("sbuf", [128, 4 * K], "bfloat16"),
+    "dall": ("sbuf", [128, 4 * C], "bfloat16"),
     "of": ("sbuf", [128, C], "float32"), "yo": ("sbuf", [128, C], "float32"),
 }
 for _t in range(R):
+    SCRATCH["Y%d" % _t] = ("sbuf", [128, 4 * (C + K)], "bfloat16")
     SCRATCH["qy%d" % _t] = ("sbuf", [128, C], "float8_e4m3fn_x4")
     SCRATCH["sy%d" % _t] = ("sbuf", [128, C], "uint8")
     SCRATCH["qn%d" % _t] = ("sbuf", [128, C], "float8_e4m3fn_x4")
     SCRATCH["sn%d" % _t] = ("sbuf", [128, C], "uint8")
-    SCRATCH["ls%d" % _t] = ("sbuf", [128, 8], "uint16")
-    SCRATCH["ln%d" % _t] = ("sbuf", [128, 8], "uint16")
+    SCRATCH["ls%d" % _t] = ("sbuf", [128, 16], "uint16")
+    SCRATCH["ln%d" % _t] = ("sbuf", [128, 16], "uint16")
 
-SEMAPHORES = (["cv", "ca", "cp", "cg", "sent"] + ["d%d" % i for i in range(18)]
+SEMAPHORES = (["cv", "ca", "cp", "cg", "sent"] + ["d%d" % i for i in range(24)]
               + ["aq%d" % t for t in range(R)] + ["al%d" % t for t in range(R)])
 
 
@@ -81,10 +101,10 @@ def rank_program(g, core, T, topo):
         hs = [wr[k] for k in list(r) + list(w) + list(x) if k in wr]
         hs += [h for k in w for h in rd.get(k, [])]
         hs += [h for k in x for h in rd.get(k, []) if h[0] != csem.get(q)]
-        for s, c in hs:
-            need[s] = max(need.get(s, 0), c)
-        for s in need:
-            wait(q, (s, need[s]))
+        for sm, c in hs:
+            need[sm] = max(need.get(sm, 0), c)
+        for sm in need:
+            wait(q, (sm, need[sm]))
 
     def note(h, r, w, x):
         for k in list(r) + list(x):
@@ -93,11 +113,11 @@ def rank_program(g, core, T, topo):
             wr[k] = h
             rd[k] = []
 
-    def op(q, fn, r=(), w=(), x=()):
+    def op(q, fn, r=(), w=(), x=(), s=()):
         order(q, r, w, x)
         cnt[q] += 1
         fn().then_inc(T.sem[csem[q]], 1)
-        note((csem[q], cnt[q]), r, w, x)
+        note((csem[q], cnt[q]), r, list(w) + list(s), x)
 
     def dma(q, out, in_, r=(), w=()):
         order(q, r, w, ())
@@ -118,306 +138,360 @@ def rank_program(g, core, T, topo):
     def bank(b, hi, lo=0):
         return T.ps[:, 512 * b + lo:512 * b + hi]
 
-    def slot(c, lo, hi):
-        s = c % HB
-        buf = T.fa if s < 7 else T.fb
-        return buf[:, 8 * lo + s % 7:8 * hi:8]
+    def cell(c):
+        a = c % HB
+        s = 3 * HB + (NB - 1) * (HB - 1 - a)
+        return (s, HB) if c < HB else (s + HB, HB - 1)
 
-    (l0, h0), (l1, h1) = PART
+    NH = len(PART)
 
-    dma("s", T.X[:, 0:4 * h0], T.x[:, 0:4 * h0], w=["X0"])
+    def xk(lo, hi):
+        return ["X%d" % i for i in range(lo // 8, hi // 8)]
+
+    def parts(lo, hi):
+        return [i for i in range(NH) if PART[i][0] < hi and PART[i][1] > lo]
+
+    def load_x(q, h):
+        lo, hi = PART[h]
+        dma(q, T.X[:, 4 * lo:4 * hi], T.x[:, 4 * lo:4 * hi], w=xk(lo, hi))
+
+    load_x("s", 0)
     dma("a", T.sw[:], T.ws[:], w=["sw"])
     dma("a", T.qw[:, 0:256].bitcast(u8), T.wc[:, 0:1024], w=["w0", "w1"])
     dma("s", T.qw[:, 256:512].bitcast(u8), T.wc[:, 1024:2048], w=["w2", "w3"])
-    dma("a", T.X[:, 4 * h0:4 * C], T.x[:, 4 * h0:4 * C], w=["X1"])
+    load_x("a", 1)
     dma("s", T.ut[:], T.u[:], w=["ut"])
-    dma("s", T.vt[:], T.v[:], r=["ut"], w=["vt"])
+    if NH > 2:
+        load_x("s", 2)
+    dma("s", T.vt[:], T.v[:], r=xk(*PART[-1]), w=["vt"])
 
     def count(out, pattern, base, step, key):
         op("g", lambda: g.iota(out, pattern, base, step, allow_small_or_imprecise_dtypes=True), w=[key])
 
-    op("g", lambda: g.iota(T.pi[:, 0:1], [[1, 1]], 0, 1), w=["pi0"])
-    count(T.idn[:], [[1, 128]], 0, -1, "idn")
-    count(T.rr[:], [[0, NB], [1, 16]], 0, 0, "rr")
-    op("g", lambda: g.iota(T.ui[:], [[16, 8]], 0, 0), w=["ui"])
-    count(T.hh[:], [[1, 2], [0, 16]], 0, 0, "hh")
-    count(T.fa[:, 0:8 * 112], [[0, 8 * 112]], 0, 0, "fz")
-    count(T.fb[:, 8 * 112:8 * 224], [[0, 8 * 112]], 0, 0, "fz2")
-    op("v", lambda: V.memset(T.et[:], 0.0), w=["et"])
-    op("v", lambda: V.tensor_scalar(T.pi[:, 1:2], T.pi[:, 0:1], 15, None, A.bitwise_and), r=["pi0"], w=["pi1"])
-    op("v", lambda: V.tensor_scalar(T.pi[:, 2:3], T.pi[:, 0:1], 4, 1, A.logical_shift_right, A.bitwise_and), r=["pi0"], w=["pi2"])
-    op("v", lambda: V.memset(T.fb[:, 7:8 * 112:8], 0.0), w=["fz3"])
-    op("v", lambda: V.tensor_copy(T.pf[:, 0:2], T.pi[:, 1:3]), r=["pi1", "pi2"], w=["pf"])
-    op("v", lambda: V.tensor_scalar(T.et[:, 3:515:4], T.idn[:], 0.0, None, A.is_equal), r=["idn"], w=["et"])
-    op("v", lambda: V.memset(T.fb[:, 8 * 224 + 7:8 * C:8], 0.0), w=["fz4"])
-    op("v", lambda: V.tensor_scalar(T.pf[:, 2:3], T.pf[:, 0:1], 224.0, None, A.add), r=["pf"], w=["cr"])
-    for b in range(4):
-        op("v", lambda: V.quantize_mx(T.qe[:, 128 * b:128 * b + 128], T.se[:, 128 * b:128 * b + 128], T.et[:, 3 - b:515 - b]),
-           r=["et"], w=["e%d" % b])
-    op("v", lambda: V.tensor_scalar(T.m01[:], T.rr[:], T.pf[:, 0:1], None, A.is_equal), r=["rr", "pf"], w=["m01"])
-    op("v", lambda: V.memset(T.cum[:, 7:4 * CW:CW], 16.0), w=["cum_i"])
-    op("v", lambda: V.memset(T.cs[:, 0:16], 0.0), w=["cs_a"])
-    op("v", lambda: V.memset(T.cs[:, C + 16:C + 32], 0.0), w=["cs_b"])
-    op("v", lambda: V.memset(T.o[:, C:512], -256.0), w=["o_x"])
-    op("v", lambda: V.tensor_copy(T.uo[:], T.ui[:]), r=["ui"], w=["uo"])
-    op("v", lambda: V.tensor_scalar(T.zm[:, 0:32], T.hh[:], T.pf[:, 1:2], None, A.is_equal), r=["hh", "pf"], w=["zm"])
-    op("a", lambda: S.activation(T.mrs[:], T.rr[:, 0:h0], F.Identity, bias=BIG, scale=-2 * BIG), r=["rr"], w=["mrs"])
-    op("a", lambda: S.activation(T.mpm[:], T.m01[:, 0:h0], F.Identity, bias=BIG, scale=-2 * BIG), r=["m01"], w=["mpm"])
-    op("a", lambda: S.activation(T.rs01[:], T.rr[:], F.Sign), r=["rr"], w=["rs01"])
+    def ts(out, in0, s1, s2, o0, o1, r, w):
+        if o1 is None:
+            op("v", lambda: V.tensor_scalar(out, in0, s1, None, o0), r=r, w=w)
+        else:
+            op("v", lambda: V.tensor_scalar(out, in0, s1, s2, o0, o1), r=r, w=w)
 
-    def widen_zm():
-        have = 32
-        while have < 480:
-            m = min(have, 480 - have)
-            op("a", lambda: S.activation(T.zm[:, have:have + m], T.zm[:, 0:m], F.Copy), r=["zm"], w=["zm"])
-            have += m
+    op("g", lambda: g.iota(T.pi[:, 0:1], [[1, 1]], 0, 1), w=["pi0"])
+    count(T.i4[:], [[1, 4]], 0, 0, "i4")
+    op("g", lambda: g.iota(T.ui[:], [[16, 8]], 0, 0), w=["ui"])
+    count(T.rr[:], [[0, MW // 16], [1, 16]], 0, 0, "rr")
+    count(T.gq[:], [[1, 8], [0, 4]], 0, 0, "gq")
+    count(T.idn[:], [[1, 128]], 0, -1, "idn")
+    count(T.o[:, C:512], [[0 if EARLY else 1, K]], -256 if EARLY else C - 256, 0, "o_x")
+    count(T.jc[:], [[1, C]], -256, 0, "jc")
+    op("v", lambda: V.memset(T.fl[:, 0:512], 0.0), w=["fz0", "dgA", "dgB"])
+    op("v", lambda: V.memset(T.fl[:, (NP - 1) * C:NP * C + 64], 0.0), w=["fz1"])
+    ts(T.pi[:, 1:2], T.pi[:, 0:1], 15, None, A.bitwise_and, None, ["pi0"], ["pi1"])
+    ts(T.pi[:, 2:3], T.pi[:, 0:1], 2, 3, A.logical_shift_right, A.bitwise_and, ["pi0"], ["pi2"])
+    ts(T.pi[:, 3:4], T.pi[:, 0:1], 3, None, A.bitwise_and, None, ["pi0"], ["pi3"])
+    ts(T.pi[:, 4:5], T.pi[:, 0:1], 4, None, A.logical_shift_right, None, ["pi0"], ["pi4"])
+    op("v", lambda: V.quantize_mx(T.qf[:, 0:128], T.sf[:, 0:128], T.fl[:, 0:512]), r=["fz0", "dgA", "dgB"],
+       w=["qz0", "qf%d" % (len(CUTS) - 2), "qf%d" % (len(CUTS) - 3)])
+    op("v", lambda: V.tensor_copy(T.pf[:, 0:4], T.pi[:, 1:5]), r=["pi1", "pi2", "pi3", "pi4"], w=["pf"])
+    op("v", lambda: V.quantize_mx(T.qf[:, (NP - 1) * Q4:NP * Q4 + 16], T.sf[:, (NP - 1) * Q4:NP * Q4 + 16],
+                                  T.fl[:, (NP - 1) * C:NP * C + 64]), r=["fz1"], w=["qz1", "qf0"])
+    ts(T.ka[:, 0:4], T.i4[:], T.pf[:, 1:2], UP, A.is_equal, A.mult, ["i4", "pf"], ["ka0"])
+    op("v", lambda: V.memset(T.ct[:], 0.0), w=["ct"])
+    op("v", lambda: V.memset(T.rs[:], 4096.0), w=["rs"])
+    ts(T.ka[:, 4:7], T.ka[:, 1:4], DOWN / UP, None, A.mult, None, ["ka0"], ["ka1"])
+    ts(T.ka[:, 7:8], T.ka[:, 0:1], DOWN / UP, None, A.mult, None, ["ka0"], ["ka2"])
+    ts(T.m01[:], T.rr[:], T.pf[:, 0:1], None, A.is_equal, None, ["rr", "pf"], ["m01"])
+    op("v", lambda: V.tensor_tensor(T.ka[:, 8:12], T.ka[:, 0:4], T.ka[:, 4:8], A.add), r=["ka0", "ka1", "ka2"], w=["ka"])
+    ts(T.gm[:], T.gq[:], T.pf[:, 3:4], -1.0, A.is_equal, A.mult, ["gq", "pf"], ["gm"])
+    op("v", lambda: V.tensor_copy(T.uo[:], T.ui[:]), r=["ui"], w=["uo"])
+    ts(T.pf[:, 4:5], T.ka[:, 7:8], -1.0, H - UP, A.mult, A.add, ["ka2"], ["pf4"])
+    ts(T.pf[:, 5:6], T.ka[:, 7:8], -4.0, 4 * (256 - UP), A.mult, A.add, ["ka2"], ["pf5"])
+    ts(T.pf[:, 6:7], T.ka[:, 11:12], -16.0, None, A.add, None, ["ka"], ["pf6"])
+    op("v", lambda: V.memset(T.et[:], 0.0), w=["et"])
+    op("v", lambda: V.tensor_tensor(T.pf[:, 8:9], T.pf[:, 4:5], T.pf[:, 0:1], A.add), r=["pf", "pf4"], w=["cr"])
+    op("v", lambda: V.tensor_tensor(T.pf[:, 9:10], T.pf[:, 5:6], T.pf[:, 2:3], A.add), r=["pf", "pf5"], w=["cx"])
+    ts(T.et[:, 3:515:4], T.idn[:], 0.0, None, A.is_equal, None, ["idn"], ["et"])
+
+    op("a", lambda: S.activation(T.mrs[:], T.rr[:], F.Identity, bias=BIG, scale=-2 * BIG), r=["rr"], w=["mrs"])
+    op("a", lambda: S.activation(T.mpm[:], T.m01[:], F.Identity, bias=BIG, scale=-2 * BIG), r=["m01"], w=["mpm"])
+    for i in range(4):
+        op("a", lambda: S.activation(T.ct[:, 5 * i:512:16], T.gm[:], F.Copy), r=["gm", "ct"], w=["ct%d" % i])
+    for i in range(4):
+        op("a", lambda: S.activation(T.mh[:, i:C:4], T.rr[:, 0:Q4], F.Identity, bias=T.ka[:, 8 + i:9 + i], scale=0.0),
+           r=["rr", "ka"], w=["mh%d" % i])
+    mh = ["mh%d" % i for i in range(4)]
+    mz = ["mz%d" % i for i in range(4)]
+    op("a", lambda: S.activation(T.rs[:, 0:H:16], T.rr[:, 0:HB], F.Identity, bias=T.pf[:, 6:7], scale=0.0), r=["rr", "rs", "pf6"], w=["rsA"])
+    op("a", lambda: S.activation(T.rs[:, H:C:16], T.rr[:, 0:HB], F.Identity, bias=T.ka[:, 11:12], scale=0.0), r=["rr", "rs", "ka"], w=["rsB"])
+    op("a", lambda: S.activation(T.mz[:], T.mh[:, 0:Q4], F.Copy), r=mh, w=mz)
+
+    def unit(i):
+        op("v", lambda: V.quantize_mx(T.qe[:, 128 * i:128 * i + 128], T.se[:, 128 * i:128 * i + 128], T.et[:, 3 - i:515 - i]),
+           r=["et"], w=["e%d" % i])
 
     def pick_u():
         op("v", lambda: V.quantize_mx(T.qu[:], T.su[:], T.ut[:]), r=["ut"], w=["qu"])
         op("v", lambda: V.tensor_copy(T.qu2[:].bitcast(u32), T.qu[:].bitcast(u32).indirect(T.uo[:])), r=["qu", "uo"], w=["qu2"])
         op("a", lambda: S.activation(T.su2[:], T.su[:].indirect(T.uo[:]), F.Copy), r=["qu", "uo"], w=["su2"])
 
-    def quant_x(h):
-        lo, hi = PART[h]
-        op("v", lambda: V.quantize_mx(T.qx[:, lo:hi], T.sx[:, lo:hi], T.X[:, 4 * lo:4 * hi]),
-           r=["X%d" % h, "Xs"] + ["Xg%d" % b for b in range(4)], w=["qx%d" % h])
+    def quant_x(lo, hi, key):
+        op("v", lambda: V.quantize_mx(T.qx[:, lo:hi], T.sx[:, lo:hi], T.X[:, 4 * lo:4 * hi]), r=xk(lo, hi), w=[key])
 
     def mm(b, lq, ls, rq, rs, m, r):
         op("p", lambda: g.tensor.matmul_mx(bank(b, m), lq, ls, rq, rs, True, True), r=r, w=["bk%d" % b])
 
+    def pick(q, out, src, r, w):
+        if q == "v":
+            op("v", lambda: V.tensor_copy(out, src), r=r, w=w)
+        else:
+            op("a", lambda: S.activation(out, src, F.Copy), r=r, w=w)
+
+    def gather(t, q, lo, hi):
+        pick(q, T.X[:, 4 * lo:4 * hi], T["Y%d" % t][:, 0:4 * (C if EARLY else C + K)].indirect(T.ox[:, lo // 4:hi // 4]),
+             ["Y%d%d%d" % (t, b, i) for b in range(4) for i in range(NH)] + ([] if EARLY else ["ds0", "ds1"]) + ["ox"], xk(lo, hi))
+
     for t in range(R):
-        qy, sy, qn, sn, ls, ln = (T[k + str(t)] for k in ("qy", "sy", "qn", "sn", "ls", "ln"))
+        Y, qy, sy, qn, sn, ls, ln = (T[k + str(t)] for k in ("Y", "qy", "sy", "qn", "sn", "ls", "ln"))
+        front = FRONT[min(t, 1)]
 
         def layer(b, h):
             lo, hi = PART[h]
-            mm(2 * b + h, T.qw[:, 128 * b:128 * b + 128], T.sw[:, 128 * b:128 * b + 128],
+            mm(b, T.qw[:, 128 * b:128 * b + 128], T.sw[:, 128 * b:128 * b + 128],
                T.qx[:, lo:hi], T.sx[:, lo:hi], hi - lo, ["w%d" % b, "sw", "qx%d" % h])
 
         def to_y(q, b, h):
             lo, hi = PART[h]
-            out, src = T.Y[:, 4 * lo + b:4 * hi:4], bank(2 * b + h, hi - lo)
+            out, src = Y[:, 4 * lo + b:4 * hi:4], bank(b, hi - lo)
             if q == "a":
-                op("a", lambda: S.activation(out, src, F.Copy, scale=0.03125), x=["bk%d" % (2 * b + h)], w=["Y%d%d" % (b, h)])
+                op("a", lambda: S.activation(out, src, F.Copy, scale=0.03125), x=["bk%d" % b], w=["Y%d%d%d" % (t, b, h)])
             else:
-                op("v", lambda: V.tensor_scalar(out, src, 0.03125, None, A.mult), x=["bk%d" % (2 * b + h)], w=["Y%d%d" % (b, h)])
+                op("v", lambda: V.tensor_scalar(out, src, 0.03125, None, A.mult), x=["bk%d" % b], w=["Y%d%d%d" % (t, b, h)])
 
         def quant_y(h):
             lo, hi = PART[h]
-            op("v", lambda: V.quantize_mx(qy[:, lo:hi], sy[:, lo:hi], T.Y[:, 4 * lo:4 * hi]),
-               r=["Y%d%d" % (b, h) for b in range(4)], w=["qy%d%d" % (t, h)])
+            op("v", lambda: V.quantize_mx(qy[:, lo:hi], sy[:, lo:hi], Y[:, 4 * lo:4 * hi]),
+               r=["Y%d%d%d" % (t, b, h) for b in range(4)], w=["qy%d%d" % (t, h)])
+
+        base = {}
 
         def scores(b, lo, hi):
-            mm(b, T.qu2[:], T.su2[:], qy[:, lo:hi], sy[:, lo:hi], hi - lo,
-               ["qu2", "su2", "qy%d0" % t] + (["qy%d1" % t] if hi > h0 else []))
+            base[b] = (lo, hi)
+            mm(b, T.qu2[:], T.su2[:], qy[:, lo:hi], sy[:, lo:hi], hi - lo, ["qu2", "su2"] + ["qy%d%d" % (t, i) for i in parts(lo, hi)])
 
-        def own(h):
-            return bank(h, PART[h][1], PART[h][0])
+        def sco(banks, lo, hi):
+            b = [i for i in banks if i in base and base[i][0] <= lo and hi <= base[i][1]][0]
+            return b, bank(b, hi - base[b][0], lo - base[b][0])
 
         def own_mask(h):
             lo, hi = PART[h]
-            op("v", lambda: V.tensor_tensor(T.d1[:, lo:hi], own(h), T.mpm[:, 0:hi - lo], A.max),
-               r=["mpm"], x=["bk%d" % h], w=["d1%d" % h])
+            b, p = sco((4, 5), lo, hi)
+            op("v", lambda: V.tensor_tensor(T.d1[:, lo:hi], p, T.mpm[:, 0:hi - lo], A.max), r=["mpm"], x=["bk%d" % b], w=["d1%d" % h])
 
         def own_scan(h):
             lo, hi = PART[h]
             op("v", lambda: V.tensor_tensor_scan(T.S[:, lo:hi], T.mrs[:, 0:hi - lo], T.d1[:, lo:hi], BIG, A.max, A.min),
                r=["mrs", "d1%d" % h], w=["S%d" % h])
 
-        def diag(h):
-            lo, hi = PART[h]
-            op("v", lambda: V.tensor_tensor(T.fa[:, 8 * lo + 7:8 * hi:8], own(h), T.S[:, lo:hi], A.is_gt),
-               r=["S%d" % h, "fz"], x=["bk%d" % h], w=["fd%d" % h])
+        def diag(k):
+            lo, at = (0, C) if k == "A" else (H, H)
+            b, p = sco((4, 5), lo, lo + H)
+            op("v", lambda: V.tensor_tensor(T.fl[:, at:at + H], p, T.S[:, lo:lo + H], A.is_gt),
+               r=["S%d" % i for i in parts(lo, lo + H)], x=["bk%d" % b], w=["dg" + k])
 
-        quant_x(0)
-        quant_x(1)
-        for h in range(2):
-            for b in range(4):
-                layer(b, h)
-        to_y("a", 0, 0)
-        to_y("v", 1, 0)
-        to_y("a", 2, 0)
-        if t == 0:
-            pick_u()
-        to_y("v", 3, 0)
-        quant_y(0)
-        scores(0, l0, h0)
-        scores(4, 0, WN)
-        send(qn[:, l0:h0].bitcast(u8), qy[:, l0:h0].bitcast(u8), "aq%d" % t, ["qy%d0" % t])
-        to_y("a", 0, 1)
-        to_y("a", 1, 1)
-        to_y("a", 2, 1)
-        to_y("v", 3, 1)
-        quant_y(1)
-        scores(2, W0, C)
-        scores(1, 0, C)
-        send(qn[:, l1:h1].bitcast(u8), qy[:, l1:h1].bitcast(u8), "aq%d" % t, ["qy%d1" % t])
-        send(sn[:], sy[:], "aq%d" % t, [])
-        if t == 0:
-            count(T.jc[:], [[1, C]], -256, 0, "jc")
-        op("a", lambda: S.activation(T.pc[:, WN:2 * WN], bank(4, WN), F.Copy), x=["bk4"], w=["pcx"])
-        op("a", lambda: S.activation(T.pc[:, 0:WN], bank(2, WN), F.Copy), x=["bk2"], w=["pc1"])
-        own_mask(0)
-        own_scan(0)
-        wr["qn%d" % t] = ("aq%d" % t, 3 * back)
-        for b in range(4):
-            mm(4 + b, T.qe[:, 128 * b:128 * b + 128], T.se[:, 128 * b:128 * b + 128], qn[:], sn[:], C, ["e%d" % b, "qn%d" % t])
+        def diag_rows(k):
+            lo, at = (0, C) if k == "A" else (H, H)
+            op("v", lambda: V.tensor_tensor_scan(T.fr[:, lo:lo + H], T.rs[:, lo:lo + H], T.fl[:, at:at + H], 4096.0, A.min, A.add),
+               r=["rs" + k, "dg" + k], w=["fr" + k])
 
-        zs = ["fz", "fz2", "fz3", "fz4"]
+        def skey(c):
+            return "S%d" % parts(16 * c, 16 * c + 16)[0]
 
-        def span(c):
-            return (0, WL) if c == SE else (16 * (c + 1), min(16 * (c + 15), C))
-
-        def flags(c):
-            lo, hi = span(c)
-            op("v", lambda: V.tensor_scalar(slot(c, lo, hi), bank(1, hi, lo), T.S[:, 16 * c + 15:16 * c + 16], None,
-                                            A.is_ge if c == SE else A.is_gt),
-               r=["S1" if c == SE else "S0"] + zs, x=["bk1"], w=["f%d" % c])
+        def flags(c, side):
+            s, m = cell(c)
+            lat = min(m, NB - 1 - c)
+            lo, hi, at = (c + 1, c + 1 + lat, s) if side == 0 else (0, m - lat, s + lat)
+            if hi > lo:
+                b, p = sco((4, 5), 16 * lo, 16 * hi)
+                op("v", lambda: V.tensor_scalar(T.fl[:, 16 * at:16 * (at + hi - lo)], p, T.S[:, 16 * c + 15:16 * c + 16],
+                                                None, A.is_ge if side else A.is_gt),
+                   r=[skey(c), "qz0", "qz1"], x=["bk%d" % b], w=["f%d_%d" % (c, side)])
 
         def rowsum(c):
-            lo, hi = span(c)
-            m, end = (hi - lo) // 2, 112 * min(c, SB) + 112
-            op("v", lambda: V.tensor_tensor_scan(T.rj[:, end - m:end], slot(c, lo, lo + m), slot(c, lo + m, hi),
-                                                 -16.0 if c < HB else 0.0, A.add, A.add), r=["f%d" % c], w=["rj%d" % c])
-
-        own_mask(1)
-        diag(0)
-        own_scan(1)
-        flags(0)
+            s, m = cell(c)
+            op("v", lambda: V.tensor_tensor_scan(T.rj[:, Q4 * (c + 1) - 8 * m:Q4 * (c + 1)], T.fl[:, 16 * s:16 * s + 8 * m],
+                                                 T.fl[:, 16 * s + 8 * m:16 * (s + m)], 0.0, A.add, A.add),
+               r=["f%d_0" % c, "f%d_1" % c], w=["rj%d" % c])
 
         def sign(c):
-            op("a", lambda: S.activation(T.sg[:, WL * (c - SB):WL * (c - SB + 1)], T.pc[:, 16 * (c - SB):16 * (c - SB) + WL], F.Sign,
-                                         bias=T.S[:, 16 * c + 15:16 * c + 16], scale=-1.0),
-               r=["pc1", "pcx", "S0" if 16 * c < h0 else "S1"], w=["sg%d" % c])
+            s, m = cell(c)
+            lo = 16 * ((c + 1) % NB)
+            b, p = sco((6, 7), lo, lo + 16 * m)
+            op("a", lambda: S.activation(T.fl[:, 16 * s:16 * (s + m)], p, F.Sign, bias=T.S[:, 16 * c + 15:16 * c + 16], scale=-1.0),
+               r=[skey(c), "qz0", "qz1"], x=["bk%d" % b], w=["f%d_0" % c])
 
-        def later(c):
-            m = C - 16 * (c + 1)
-            op("a", lambda: S.activation(slot(c, 16 * (c + 1), C), T.sg[:, WL * (c - SB):WL * (c - SB) + m], F.Relu, scale=-1.0,
-                                         accum_out=T.ra[:, c - SB:c - SB + 1]), r=["sg%d" % c] + zs, w=["f%da" % c, "ra%d" % c])
+        def step(c):
+            s, m = cell(c)
+            v = T.fl[:, 16 * s:16 * (s + m)]
+            if c == NB - 1:
+                op("a", lambda: S.activation(v, v, F.Sign, bias=1.0, scale=-1.0, accum_out=T.ra[:, c:c + 1]), w=["f%d_0" % c, "ra%d" % c])
+            else:
+                op("a", lambda: S.activation(v, v, F.Relu, scale=-1.0, accum_out=T.ra[:, c:c + 1]), w=["f%d_0" % c, "ra%d" % c])
 
-        def earlier(c):
-            m, end = 16 * (c - HB), WL * (c - SB + 1)
-            op("a", lambda: S.activation(slot(c, 0, m), T.sg[:, end - m:end], F.Sign, bias=1.0, scale=-1.0,
-                                         accum_out=T.rb[:, c - SB:c - SB + 1]), r=["sg%d" % c] + zs, w=["f%db" % c, "rb%d" % c])
+        done = [0]
 
-        sign(SB)
-        for c in range(SB, SE):
-            if c + 1 < SE:
-                sign(c + 1)
-            later(c)
-        for c in range(SE - 1, HB, -1):
-            earlier(c)
-        if t == 0:
-            widen_zm()
+        def inside(i):
+            return [c for c in range(NB) if cell(c)[0] < CUTS[i] and sum(cell(c)) > CUTS[i + 1]]
+
+        def columns(i):
+            hi, lo = CUTS[i], CUTS[i + 1]
+            r = ["f%d_%d" % (c, k) for c in inside(i) for k in range(2)] + (["dgA", "dgB"] if lo < 3 * HB else [])
+            op("v", lambda: V.quantize_mx(T.qf[:, 4 * lo:4 * hi], T.sf[:, 4 * lo:4 * hi], T.fl[:, 16 * lo:16 * hi]), r=r, w=["qf%d" % i])
+            while done[0] < NP and (NB * (NP - 1 - done[0]) >= lo or i == len(CUTS) - 2):
+                s = NP - 1 - done[0]
+                done[0] += 1
+                op("p", lambda: g.tensor.matmul_mx(bank(0, 128), T.qc[:], T.sc[:], T.qf[:, Q4 * s:Q4 * s + 128], T.sf[:, Q4 * s:Q4 * s + 128],
+                                                   s == NP - 1, s == 0),
+                   r=["qc", "qz0", "qz1"] + ["qf%d" % k for k in range(max(i - 1, 0), i + 1)],
+                   w=["bk0"] if s == NP - 1 else [], s=["bk0"])
+
+        def rows(lo, hi, src, r, key):
+            op("v", lambda: V.tensor_tensor(T.mz[:, 4 * lo + 3:4 * hi:4], src, T.fr[:, 16 * lo + 15:16 * hi:16], A.add), r=r, w=[key])
+
+        for word in front.split():
+            k, q, z = word[0], word[1], word[2:]
+            if k == "g":
+                gather(t - 1, q, *(int(i) for i in z.split("-")))
+            elif k == "x":
+                quant_x(*PART[int(q)], "qx" + q)
+            elif k == "L":
+                for b in range(4):
+                    layer(b, int(q))
+            elif k == "l":
+                layer(int(q), int(z))
+            elif k == "y":
+                to_y(q, int(z[0]), int(z[1]))
+            elif k == "q":
+                quant_y(int(q))
+            elif k == "P":
+                scores(int(q), *(int(i) for i in z[1:].split("-")))
+            elif k == "m":
+                own_mask(int(q))
+            elif k == "s":
+                own_scan(int(q))
+            elif k == "d":
+                diag(q)
+            elif k == "r":
+                diag_rows(q)
+            elif k == "u":
+                pick_u()
+            elif k == "e":
+                unit(int(q))
+            elif k == "c":
+                op("v", lambda: V.quantize_mx(T.qc[:], T.sc[:], T.ct[:]), r=["ct%d" % i for i in range(4)], w=["qc"])
+            elif k == "f":
+                flags(int(q), 0)
+            elif k == "F":
+                rowsum(int(q))
+            elif k == "t":
+                lo, hi = (int(i) for i in (q + z).split("-"))
+                send(qn[:, lo:hi].bitcast(u8), qy[:, lo:hi].bitcast(u8), "aq%d" % t, ["qy%d%d" % (t, i) for i in parts(0, hi)])
+            elif k == "T":
+                send(sn[:], sy[:], "aq%d" % t, [])
+            elif k == "S":
+                his = SROWS[t]
+                sign(his[0])
+                for i, c in enumerate(his):
+                    if i + 1 < len(his):
+                        sign(his[i + 1])
+                    step(c)
+
+        mine = VROWS[t]
+        piece = 0
+        for i, c in enumerate(mine):
+            flags(c, 0)
+            flags(c, 1)
+            if i > 0:
+                rowsum(mine[i - 1])
+            if piece < len(CUTS) - 3 and not set(mine[i:]).intersection(inside(piece)) and i >= LAG[t] + STEP * piece:
+                columns(piece)
+                piece += 1
+        while piece < len(CUTS) - 3:
+            columns(piece)
+            piece += 1
+        rowsum(mine[-1])
+        columns(piece)
+        runs = []
+        for c in range(NB):
+            if runs and (c in SROWS[t]) == (c - 1 in SROWS[t]):
+                runs[-1][1] = c + 1
+            else:
+                runs.append([c, c + 1])
+        order("v", (), mz, ())
+        for i, (lo, hi) in enumerate(runs):
+            if lo not in SROWS[t]:
+                rows(lo, hi, T.rj[:, Q4 * (lo + 1) - 1:Q4 * hi:Q4], ["frA", "frB"] + ["rj%d" % c for c in range(lo, hi)], mz[i])
+        columns(piece + 1)
+        for i, (lo, hi) in enumerate(runs):
+            if lo in SROWS[t]:
+                rows(lo, hi, T.ra[:, lo:hi], ["frA", "frB"] + ["ra%d" % c for c in range(lo, hi)], mz[i])
+        wr["qn%d" % t] = ("aq%d" % t, front.lower().count("t") * back)
         for b in range(4):
-            op("a", lambda: S.activation(T.dall[:, C * b:C * b + C], bank(4 + b, C), F.Copy), x=["bk%d" % (4 + b)], w=["dall%d" % b])
-
-        mine = list(range(SB)) + [SE]
-        for k in range(1, len(mine)):
-            flags(mine[k])
-            rowsum(mine[k - 1])
-        diag(1)
-        rowsum(SE)
-        op("v", lambda: V.tensor_tensor_scan(T.fr[:], T.rs01[:], T.fa[:, 7:8 * C:8], 0.0, A.mult, A.add), r=["rs01", "fd0", "fd1"], w=["fr"])
-
-        def colscan(i):
-            lo, hi = RUNS[i]
-            r = ["f%d" % c for c in mine]
-            r += ["f%da" % c for c in range(SB, SE) if c + 1 < hi]
-            r += ["f%db" % c for c in range(SB, SE) if c - HB - 1 >= lo]
-            op("v", lambda: V.tensor_tensor_scan(T.cum[:, CW * i + 8:CW * i + 8 + 128 * (hi - lo)], T.fa[:, 128 * lo:128 * hi],
-                                                 T.fb[:, 128 * lo:128 * hi], 16.0, A.add, A.add),
-               r=r + zs + ["fd0", "fd1"], w=["cum%d" % i])
-
-        def coldiff(i):
-            lo, hi = RUNS[i]
-            end = CW * i + 8 + 128 * (hi - lo)
-            op("v", lambda: V.tensor_tensor_scan(T.cs[:, 16 + 16 * lo:16 + 16 * hi], T.cum[:, CW * i + 15:end:8],
-                                                 T.cum[:, CW * i + 7:end - 8:8], 0.0, A.max, A.subtract),
-               r=["cum%d" % i, "cum_i"], w=["cs%d" % i])
-
-        colscan(0)
-        op("v", lambda: V.tensor_tensor(T.base[:, 0:SB], T.rj[:, 111:112 * SB:112], T.fr[:, 15:16 * SB:16], A.add),
-           r=["fr"] + ["rj%d" % c for c in range(SB)], w=["base0"])
-        op("v", lambda: V.tensor_tensor(T.base[:, SE:NB], T.rj[:, 112 * SB + 111:112 * SB + 112], T.fr[:, C - 1:C], A.add),
-           r=["fr", "rj%d" % SE], w=["base2"])
-        colscan(1)
-        coldiff(0)
-        op("v", lambda: V.tensor_tensor(T.rk[:, SB:SE], T.ra[:, 0:SE - SB], T.fr[:, 16 * SB + 15:16 * SE:16], A.add),
-           r=["fr"] + ["ra%d" % c for c in range(SB, SE)], w=["rk", "rk1"])
-        colscan(2)
-        coldiff(1)
-        colscan(3)
-        coldiff(2)
-        coldiff(3)
-        op("v", lambda: V.tensor_tensor(T.base[:, SB:SE], T.rk[:, SB:SE], T.rb[:, 0:SE - SB], A.add),
-           r=["rk"] + ["rb%d" % c for c in range(SB, SE)], w=["base1"])
-        css = ["cs%d" % i for i in range(4)] + ["cs_a", "cs_b"]
-        bs = ["base0", "base1", "base2"]
-        op("v", lambda: V.transpose(T.tt[:, 0:C], T.cs[:, 16:16 + C]), r=css, w=["tt0"])
-        op("v", lambda: V.transpose(T.tt[:, C:928], T.cs[:, 0:480]), r=css, w=["tt1"])
-        op("v", lambda: V.tensor_tensor_scan(T.zz[:, 0:C], T.tt[:, 0:C], T.zm[:, 0:C], 0.0, A.add, A.mult), r=["tt0", "zm"], w=["zz0"])
-        op("v", lambda: V.tensor_tensor_scan(T.zz[:, C:928], T.tt[:, C:928], T.zm[:], 0.0, A.add, A.mult), r=["tt1", "zm"], w=["zz1"])
-        op("v", lambda: V.tensor_tensor(T.col[:, 0:NB:2], T.base[:, 0:NB:2], T.zz[:, 15:C:32], A.subtract), r=["zz0"] + bs, w=["col0"])
-        op("v", lambda: V.tensor_tensor(T.col[:, 1:NB:2], T.base[:, 1:NB:2], T.zz[:, 31:C:32], A.subtract), r=["zz0"] + bs, w=["col1"])
-        op("v", lambda: V.tensor_tensor(T.rk[:, 0:NB:2], T.col[:, 0:NB:2], T.zz[:, C + 31:C + 448:32], A.subtract), r=["zz1", "col0"], w=["rk"])
-        op("v", lambda: V.tensor_tensor(T.rk[:, 1:NB:2], T.col[:, 1:NB:2], T.zz[:, C + 47:928:32], A.subtract), r=["zz1", "col1", "base1"], w=["rk1"])
-        op("v", lambda: V.tensor_scalar(T.oi[:, 0:NB], T.rk[:, 0:NB], T.pf[:, 2:3], None, A.add), r=["rk", "rk1", "cr"], w=["oi"])
+            mm(4 + b, T.qe[:, 128 * b:128 * b + 128], T.se[:, 128 * b:128 * b + 128], qn[:], sn[:], C, ["e%d" % b, "qn%d" % t])
+        for b in range(4):
+            op("a", lambda: S.activation(T.dall[:, b:4 * C:4], bank(4 + b, C), F.Copy), x=["bk%d" % (4 + b)], w=["dall%d" % b])
+        op("v", lambda: V.tensor_tensor_scan(T.zz[:], bank(0, Q4), T.mz[:], DOWN, A.max, A.add), r=mz, x=["bk0"], w=["zz"])
+        ts(T.oi[:, 0:NB], T.zz[:, 3:Q4:4], T.pf[:, 8:9], None, A.add, None, ["zz", "cr"], ["oi"])
 
         op("v", lambda: V.tensor_copy(T.o[:, 0:C].indirect(T.oi[:, 0:NB]), T.jc[:]), r=["oi", "jc"], w=["o"])
-        op("v", lambda: V.tensor_tensor(T.t1[:], T.o[:, 0:K], T.m01[:, 0:K], A.mult), r=["o", "m01"], w=["t1"])
-        op("v", lambda: V.tensor_tensor(T.b1[:], T.o[:, C - K:C], T.m01[:, 0:K], A.mult), r=["o", "m01"], w=["b1"])
-        op("v", lambda: V.tensor_tensor_scan(T.t2[:], T.rs01[:, 0:K], T.t1[:], 0.0, A.mult, A.add), r=["t1", "rs01"], w=["t2"])
-        op("v", lambda: V.tensor_tensor_scan(T.b2[:], T.rs01[:, 0:K], T.b1[:], 0.0, A.mult, A.add), r=["b1", "rs01"], w=["b2"])
-        op("v", lambda: V.tensor_scalar(ls[:, 0:4], T.t2[:, 15:K:16], 256.0, None, A.add), r=["t2"], w=["ls%d" % t])
-        send(ln[:, 0:4], ls[:, 0:4], "al%d" % t, ["ls%d" % t])
+        op("v", lambda: V.tensor_tensor_scan(T.t2[:], T.o[:, 0:K], T.mh[:, 0:K], DOWN, A.max, A.add), r=["o"] + mh, w=["t2"])
+        if EARLY:
+            op("v", lambda: V.tensor_tensor_scan(T.b2[:], T.o[:, C - K:C], T.mh[:, 0:K], DOWN, A.max, A.add), r=["o"] + mh, w=["b2"])
+        ts(ls[:], T.t2[:, 3:K:4], 4.0, T.pf[:, 9:10], A.mult, A.add, ["t2", "cx"], ["ls%d" % t])
+        send(ln[:], ls[:], "al%d" % t, ["ls%d" % t])
         wr["ln%d" % t] = ("al%d" % t, back)
 
-        def places(b):
-            op("v", lambda: V.tensor_scalar(T.ob[:, 4 * b:4 * b + 4], T.b2[:, 15:K:16], 4.0, 1024.0 + b, A.mult, A.add), r=["b2"], w=["ob%d" % b])
-
-        op("v", lambda: V.tensor_tensor(T.e1[:], T.o[:, K:512].indirect(T.oi[:, 0:NB]), T.m01[:], A.mult), r=["o", "o_x", "oi", "m01"], w=["e1"])
-        places(0)
-        op("v", lambda: V.tensor_tensor_scan(T.e2[:], T.rs01[:], T.e1[:], 0.0, A.mult, A.add), r=["e1", "rs01"], w=["e2"])
-        places(1)
-        ys = ["Y%d%d" % (b, h) for b in range(4) for h in range(2)]
-        for b in (2, 0, 3, 1):
-            op("v", lambda: V.tensor_scalar(T.ox[:, NB * b:NB * b + NB], T.e2[:, 15:C:16], 4.0, 1024.0 + b, A.mult, A.add), r=["e2"], w=["ox%d" % b])
-        order("v", (), ["X0", "X1", "Xs"], ())
-        order("a", (), ["X0", "X1", "Xs"], ())
-        for b in range(4):
-            out, src = T.X[:, b:4 * C:4], T.Y[:].indirect(T.ox[:, NB * b:NB * b + NB])
-            if b < 2:
-                op("v", lambda: V.tensor_copy(out, src), r=ys + ["ox%d" % b], w=["Xg%d" % b])
-            else:
-                op("a", lambda: S.activation(out, src, F.Copy), r=ys + ["ox%d" % b], w=["Xg%d" % b])
-        places(2)
-        places(3)
+        pick("v", T.e1[:, 0:16 * EV], T.o[:, K:512].indirect(T.oi[:, 0:EV]), ["o", "o_x", "oi"], ["e1a"])
+        if EV < NB:
+            pick("a", T.e1[:, 16 * EV:C], T.o[:, K:512].indirect(T.oi[:, EV:NB]), ["o", "o_x", "oi"], ["e1b"])
+        if t == R - 1:
+            op("a", lambda: S.activation(T.of[:], T.o[:, 0:C], F.Identity, bias=256.0), r=["o"], w=["of"])
+            dma("s", T.ol[:], T.of[0:128:16, :], r=["of"])
+        if EARLY:
+            ts(T.ob[:], T.b2[:, 3:K:4], 4.0, T.pf[:, 9:10], A.mult, A.add, ["b2", "cx"], ["ob"])
+        op("v", lambda: V.tensor_tensor_scan(T.e2[:], T.e1[:], T.mh[:], DOWN, A.max, A.add), r=["e1a", "e1b"] + mh, w=["e2"])
         if t == 0:
             op("v", lambda: V.quantize_mx(T.qv[:], T.sv[:], T.vt[:]), r=["vt"], w=["qv"])
-        for b in (0, 2, 1, 3):
-            out, src = T.dsel[:, K * b:K * b + K], T.dall[:, C * b:C * b + C].indirect(ln[:, 0:4])
-            r = ["dall%d" % b, "ln%d" % t]
-            if b < 2:
-                op("v", lambda: V.tensor_copy(out, src), r=r, w=["ds%d" % b])
-            else:
-                op("a", lambda: S.activation(out, src, F.Copy), r=r, w=["ds%d" % b])
-        op("v", lambda: V.tensor_copy(T.X[:].indirect(T.ob[:]), T.dsel[:]),
-           r=["ds%d" % b for b in range(4)] + ["ob%d" % b for b in range(4)] + ["Xg%d" % b for b in range(4)], w=["Xs"])
+        ts(T.ox[:], T.e2[:, 3:C:4], 4.0, T.pf[:, 9:10], A.mult, A.add, ["e2", "cx"], ["ox"])
+        if EARLY:
+            gather(t, "a", 0, EARLY[0])
+            gather(t, "v", EARLY[0], C)
+        for i, q in enumerate("va"):
+            out = T.ds[:, 128 * i:128 * i + 128] if EARLY else Y[:, 4 * C + 128 * i:4 * C + 128 * i + 128]
+            pick(q, out, T.dall[:].indirect(ln[:, 8 * i:8 * i + 8]), ["dall%d" % b for b in range(4)] + ["ln%d" % t], ["ds%d" % i])
+        if EARLY:
+            op("v", lambda: V.tensor_copy(T.X[:].indirect(T.ob[:]), T.ds[:]), r=["ds0", "ds1", "ob"], w=xk(0, C))
 
-    op("a", lambda: S.activation(T.of[:], T.o[:, 0:C], F.Identity, bias=256.0), r=["o"], w=["of"])
-    dma("s", T.ol[:], T.of[0:128:16, :], r=["of"])
-    quant_x(0)
-    quant_x(1)
-    for h in range(2):
-        lo, hi = PART[h]
-        mm(h, T.qv[:], T.sv[:], T.qx[:, lo:hi], T.sx[:, lo:hi], hi - lo, ["qv", "qx%d" % h])
-    op("a", lambda: S.activation(T.yo[:, l0:h0], bank(0, h0), F.Copy), x=["bk0"], w=["yo0"])
-    op("v", lambda: V.tensor_copy(T.yo[:, l1:h1], bank(1, h1 - l1)), x=["bk1"], w=["yo1"])
-    dma("s", T.oc[:], T.qx[:].bitcast(u8), r=["qx0", "qx1"])
-    dma("a", T.y[:, l0:h0], T.yo[:, l0:h0], r=["yo0"])
-    dma("s", T.y[:, l1:h1], T.yo[:, l1:h1], r=["yo1"])
-    for k in range(4):
-        dma("a" if k < 2 else "s", T.osc[4 * k:4 * k + 4, :], T.sx[32 * k:32 * k + 4, :], r=["qx0", "qx1"])
+    order("v", (), ["qx%d" % h for h in range(NH)], ())
+    for word in END.split():
+        k, q, z = word[0], word[1], word[2:]
+        if k == "g":
+            gather(R - 1, q, *(int(i) for i in z.split("-")))
+        elif k == "x":
+            quant_x(*OUT[int(q)], "qo" + q)
+        elif k == "y":
+            h = int(z)
+            lo, hi = OUT[h]
+            mm(h, T.qv[:], T.sv[:], T.qx[:, lo:hi], T.sx[:, lo:hi], hi - lo, ["qv", "qo" + z])
+            if q == "a":
+                op("a", lambda: S.activation(T.yo[:, lo:hi], bank(h, hi - lo), F.Copy), x=["bk" + z], w=["yo" + z])
+            else:
+                op("v", lambda: V.tensor_copy(T.yo[:, lo:hi], bank(h, hi - lo)), x=["bk" + z], w=["yo" + z])
+        elif k == "s":
+            dma(q, T.osc[4 * int(z):4 * int(z) + 4, :], T.sx[32 * int(z):32 * int(z) + 4, :], r=["qo%d" % h for h in range(len(OUT))])
+        else:
+            lo, hi = OUT[int(z[0])][0], OUT[int(z[-1])][1]
+            if k == "c":
+                dma(q, T.oc[:, 4 * lo:4 * hi], T.qx[:, lo:hi].bitcast(u8), r=["qo" + h for h in z])
+            else:
+                dma(q, T.y[:, lo:hi], T.yo[:, lo:hi], r=["yo" + h for h in z])
 
     for q in cnt:
         wait("g", (csem[q], cnt[q]))

@@ -6,68 +6,40 @@ NB = C // 16
 HB = NB // 2
 H = C // 2
 Q4 = C // 4
+RANKS = (" m128-288 s128-288 P4:224-448 P7:80-448 m288-448 d0-224 s288-448 rA "
+         "n000 n010 N000 n020 N010 n030 N020 n040 N030 n050 N040 n060 N050 n070 N060 n080 N070 n090 N080 n100 N090 n110 N100 n120 N110 "
+         "n271 N120 n130 N271 N130 f161 d224-448 f140 rB f160 f170 f180 f151 f150 f191 f181 f190 f200 f171 F19 Q0 F14 F17 F15 F16 F18 "
+         "f220 Q1 Q2 f210 f240 f230 f251 f201 f221 f260 F20 f250 f231 f241 f211 f261 Q3 F22 Q4 F25 F23 F21 Q5 Q6 Q7 F24 F26 "
+         "M0-14 M27-28 M14-27")
 FRONT = (
-    "x0 L0 e0 ya00 yv10 e1 e2 x1 ya20 ya30 L1 e3 c_ u_ q0 t0-128 P4:0-128 ya01 ya11 x2 ya21 m0 ya31 s0 L2 q1 P6:0-288 P5:0-288 "
-    "t128-288 ya02 yv12 ya22 yv32 m1 s1 q2 P4:224-448 P7:80-448 t288-448 T_ dA m2 rA s2 dB rB S_",
-    "x0 L0 x1 ya00 x2 yv10 ya20 yv30 L1 q0 t0-128 ya01 yv11 P4:0-128 ya21 ya31 m0 L2 s0 ya02 ya12 q1 P6:0-288 P5:0-288 "
-    "t128-288 yv22 yv32 q2 m1 P4:224-448 P7:80-448 t288-448 T_ s1 m2 dA s2 rA dB rB S_",
+    "j_ x0 l10 l20 l00 l30 e3 e0 e2 e1 yv10 ya00 yv30 x1 ya20 J_ l31 l01 l21 l11 q0 u_ t0-128 P4:0-128 ya11 ya01 ya21 yv31 x2 "
+    "l02 l22 l12 l32 m0-128 q1 t128-288 P6:0-288 P5:0-288 ya02 ya22 ya32 s0-128 yv12 c_ q2 t288-448 T_ i_" + RANKS,
+    "p_ x0 l00 l10 l20 l30 x1 yv00 yv20 ya10 ya30 l01 l11 l21 l31 x2 q0 t0-128 ya01 ya11 P4:0-128 yv21 ya31 m0-128 q1 t128-288 "
+    "l02 l22 l32 l12 ya02 yv32 s0-128 ya22 ya12 P6:0-288 P5:0-288 q2 t288-448 T_" + RANKS,
 )
-EARLY = (224,)
-OUT = ((0, 160), (160, 320), (320, 448))
-END = "x0 ya0 x1 cs01 ya1 x2 Ys01 cs2 yv2 Ya2 sa0 sa1 ss2 ss3"
-SROWS = ([0, 1, 2, 3, 14] + list(range(4, 14)),) * R
-VROWS = (list(range(15, 28)),) * R
-LAG = (2, 2, 2)
-STEP = 2
+SHARE = 216
+EV = 16
+OUT = ((0, 256), (256, 448))
 BIG = 2.0 ** 90
 UP, DOWN = 1024.0, -1600.0
 NP = HB + 1
-CUTS = (420, 366, 312, 258, 204, 150, 96, 56, 14)
-EV = 28
-MW = 192
+PIECES = ((366, 420), (312, 366), (258, 312), (204, 258), (150, 204), (96, 150), (56, 96), (14, 56))
+MW = 160
 
-SCRATCH = {
-    "ps": ("psum", [128, 4096], "float32"),
-    "X": ("sbuf", [128, 4 * C], "bfloat16"),
-    "qx": ("sbuf", [128, C], "float8_e4m3fn_x4"), "sx": ("sbuf", [128, C], "uint8"),
-    "qw": ("sbuf", [128, 512], "float8_e4m3fn_x4"), "sw": ("sbuf", [128, 512], "uint8"),
-    "ut": ("sbuf", [128, 512], "bfloat16"), "vt": ("sbuf", [128, 512], "bfloat16"),
-    "qu": ("sbuf", [128, 128], "float8_e4m3fn_x4"), "su": ("sbuf", [128, 128], "uint8"),
-    "qu2": ("sbuf", [128, 128], "float8_e4m3fn_x4"), "su2": ("sbuf", [128, 128], "uint8"),
-    "qv": ("sbuf", [128, 128], "float8_e4m3fn_x4"), "sv": ("sbuf", [128, 128], "uint8"),
-    "et": ("sbuf", [128, 516], "bfloat16"),
-    "qe": ("sbuf", [128, 512], "float8_e4m3fn_x4"), "se": ("sbuf", [128, 512], "uint8"),
-    "ct": ("sbuf", [128, 512], "bfloat16"),
-    "qc": ("sbuf", [128, 128], "float8_e4m3fn_x4"), "sc": ("sbuf", [128, 128], "uint8"),
-    "pi": ("sbuf", [128, 8], "int32"), "pf": ("sbuf", [128, 16], "float32"),
-    "ui": ("sbuf", [128, 8], "int32"), "uo": ("sbuf", [128, 8], "uint16"),
-    "rr": ("sbuf", [128, MW], "float32"), "idn": ("sbuf", [128, 128], "float32"),
-    "gq": ("sbuf", [128, 32], "float32"), "gm": ("sbuf", [128, 32], "float32"),
-    "i4": ("sbuf", [128, 4], "float32"), "ka": ("sbuf", [128, 12], "float32"),
-    "jc": ("sbuf", [128, C], "bfloat16"), "m01": ("sbuf", [128, MW], "float32"),
-    "mpm": ("sbuf", [128, MW], "float32"), "mrs": ("sbuf", [128, MW], "float32"),
-    "mh": ("sbuf", [128, C], "bfloat16"), "mz": ("sbuf", [128, Q4], "float32"), "rs": ("sbuf", [128, C], "bfloat16"),
-    "d1": ("sbuf", [128, C], "float32"), "S": ("sbuf", [128, C], "float32"),
-    "fl": ("sbuf", [128, NP * C + 64], "bfloat16"),
-    "qf": ("sbuf", [128, NP * Q4 + 16], "float8_e4m3fn_x4"), "sf": ("sbuf", [128, NP * Q4 + 16], "uint8"),
-    "rj": ("sbuf", [128, NB * Q4], "bfloat16"), "fr": ("sbuf", [128, C], "float16"), "ra": ("sbuf", [128, 32], "float32"),
-    "zz": ("sbuf", [128, Q4], "float32"),
-    "oi": ("sbuf", [128, 32], "uint16"), "o": ("sbuf", [128, 512], "bfloat16"),
-    "t2": ("sbuf", [128, K], "float16"),
-    "e1": ("sbuf", [128, C], "bfloat16"), "e2": ("sbuf", [128, C], "float16"),
-    "ox": ("sbuf", [128, Q4], "uint16"),
-    "b2": ("sbuf", [128, K], "float16"), "ob": ("sbuf", [128, 16], "uint16"), "ds": ("sbuf", [128, 4 * K], "bfloat16"),
-    "dall": ("sbuf", [128, 4 * C], "bfloat16"),
-    "of": ("sbuf", [128, C], "float32"), "yo": ("sbuf", [128, C], "float32"),
-}
-for _t in range(R):
-    SCRATCH["Y%d" % _t] = ("sbuf", [128, 4 * (C + K)], "bfloat16")
-    SCRATCH["qy%d" % _t] = ("sbuf", [128, C], "float8_e4m3fn_x4")
-    SCRATCH["sy%d" % _t] = ("sbuf", [128, C], "uint8")
-    SCRATCH["qn%d" % _t] = ("sbuf", [128, C], "float8_e4m3fn_x4")
-    SCRATCH["sn%d" % _t] = ("sbuf", [128, C], "uint8")
-    SCRATCH["ls%d" % _t] = ("sbuf", [128, 16], "uint16")
-    SCRATCH["ln%d" % _t] = ("sbuf", [128, 16], "uint16")
+SCRATCH = {"ps": ("psum", [128, 4096], "float32")}
+for _d, _l in (
+        ("bfloat16", dict(X=4 * C, ut=512, vt=512, et=516, ct=512, jc=C, mh=C, rs=C, fl=NP * C, rj=NB * Q4, o=512, e1=C,
+                          dall=4 * C, ds=4 * K, Y0=4 * C, Y1=4 * C, Y2=4 * C)),
+        ("float8_e4m3fn_x4", dict(qx=C, qw=512, qu=128, qu2=128, qv=128, qe=512, qc=128, qf=NP * Q4 + 16,
+                                  qy0=C, qy1=C, qy2=C, qn0=C, qn1=C, qn2=C)),
+        ("uint8", dict(sx=C, sw=512, su=128, su2=128, sv=128, se=512, sc=128, sf=NP * Q4 + 16, sy0=C, sy1=C, sy2=C, sn0=C, sn1=C, sn2=C)),
+        ("float32", dict(pf=16, rr=MW, idn=128, gq=32, gm=32, i4=8, ka=16, ng=Q4, m01=MW, mpm=MW, mrs=MW, mz=Q4, d1=C, S=C,
+                         ra=32, zz=Q4, of=C, yo=C)),
+        ("float16", dict(fr=C, t2=K, e2=C, b2=K)),
+        ("int32", dict(pi=8, ui=8)),
+        ("uint16", dict(uo=8, oi=32, ox=Q4, ob=16, ls0=16, ls1=16, ls2=16, ln0=16, ln1=16, ln2=16))):
+    for _k, _n in _l.items():
+        SCRATCH[_k] = ("sbuf", [128, _n], _d)
 
 SEMAPHORES = (["cv", "ca", "cp", "cg", "sent"] + ["d%d" % i for i in range(24)]
               + ["aq%d" % t for t in range(R)] + ["al%d" % t for t in range(R)])
@@ -89,6 +61,7 @@ def rank_program(g, core, T, topo):
     cnt = {"v": 0, "a": 0, "p": 0, "g": 0}
     waited = {q: {} for q in Q}
     wr, rd = {}, {}
+    born, now, holds = {}, [0], {}
     ndma, dmas, sent = [0], [], [0]
 
     def wait(q, h):
@@ -97,6 +70,8 @@ def rank_program(g, core, T, topo):
             waited[q][h[0]] = h[1]
 
     def order(q, r, w, x):
+        for k in r:
+            assert born[k] in (-1, now[0]), k
         need = {}
         hs = [wr[k] for k in list(r) + list(w) + list(x) if k in wr]
         hs += [h for k in w for h in rd.get(k, [])]
@@ -112,6 +87,11 @@ def rank_program(g, core, T, topo):
         for k in w:
             wr[k] = h
             rd[k] = []
+            born[k] = now[0]
+
+    def stay(*keys):
+        for k in keys:
+            born[k] = -1
 
     def op(q, fn, r=(), w=(), x=(), s=()):
         order(q, r, w, x)
@@ -143,6 +123,11 @@ def rank_program(g, core, T, topo):
         s = 3 * HB + (NB - 1) * (HB - 1 - a)
         return (s, HB) if c < HB else (s + HB, HB - 1)
 
+    def side(c, k):
+        s, m = cell(c)
+        lat = min(m, NB - 1 - c)
+        return (c + 1, c + 1 + lat, s) if k == 0 else (0, m - lat, s + lat)
+
     NH = len(PART)
 
     def xk(lo, hi):
@@ -150,6 +135,9 @@ def rank_program(g, core, T, topo):
 
     def parts(lo, hi):
         return [i for i in range(NH) if PART[i][0] < hi and PART[i][1] > lo]
+
+    def span(z):
+        return tuple(int(i) for i in z.split("-"))
 
     def load_x(q, h):
         lo, hi = PART[h]
@@ -161,12 +149,11 @@ def rank_program(g, core, T, topo):
     dma("s", T.qw[:, 256:512].bitcast(u8), T.wc[:, 1024:2048], w=["w2", "w3"])
     load_x("a", 1)
     dma("s", T.ut[:], T.u[:], w=["ut"])
-    if NH > 2:
-        load_x("s", 2)
+    load_x("s", 2)
     dma("s", T.vt[:], T.v[:], r=xk(*PART[-1]), w=["vt"])
 
-    def count(out, pattern, base, step, key):
-        op("g", lambda: g.iota(out, pattern, base, step, allow_small_or_imprecise_dtypes=True), w=[key])
+    def count(out, pattern, base, step, *key):
+        op("g", lambda: g.iota(out, pattern, base, step, allow_small_or_imprecise_dtypes=True), w=key)
 
     def ts(out, in0, s1, s2, o0, o1, r, w):
         if o1 is None:
@@ -174,324 +161,270 @@ def rank_program(g, core, T, topo):
         else:
             op("v", lambda: V.tensor_scalar(out, in0, s1, s2, o0, o1), r=r, w=w)
 
+    def tt(out, a, b, o, r, w, x=()):
+        op("v", lambda: V.tensor_tensor(out, a, b, o), r=r, w=w, x=x)
+
+    def scan(out, a, b, init, o0, o1, r, w, x=()):
+        op("v", lambda: V.tensor_tensor_scan(out, a, b, init, o0, o1), r=r, w=w, x=x)
+
+    def act(out, in_, f, r, w, x=(), **kw):
+        op("a", lambda: S.activation(out, in_, f, **kw), r=r, w=w, x=x)
+
+    def quant(q, s, lo, hi, src, r, w):
+        op("v", lambda: V.quantize_mx(q[:, lo:hi], s[:, lo:hi], src), r=r, w=w)
+
+    def copy(q, out, src, r, w, x=()):
+        if q == "v":
+            op("v", lambda: V.tensor_copy(out, src), r=r, w=w, x=x)
+        else:
+            act(out, src, F.Copy, r, w, x)
+
+    def qfk(lo, hi):
+        return ["qf%d" % k for k in range(lo, hi)]
+
     op("g", lambda: g.iota(T.pi[:, 0:1], [[1, 1]], 0, 1), w=["pi0"])
-    count(T.i4[:], [[1, 4]], 0, 0, "i4")
-    op("g", lambda: g.iota(T.ui[:], [[16, 8]], 0, 0), w=["ui"])
+    count(T.i4[:], [[0, 2], [1, 4]], 0, 0, "i4")
+    count(T.idn[:], [[1, 128]], 0, -1, "idn")
     count(T.rr[:], [[0, MW // 16], [1, 16]], 0, 0, "rr")
     count(T.gq[:], [[1, 8], [0, 4]], 0, 0, "gq")
-    count(T.idn[:], [[1, 128]], 0, -1, "idn")
-    count(T.o[:, C:512], [[0 if EARLY else 1, K]], -256 if EARLY else C - 256, 0, "o_x")
-    count(T.jc[:], [[1, C]], -256, 0, "jc")
-    op("v", lambda: V.memset(T.fl[:, 0:512], 0.0), w=["fz0", "dgA", "dgB"])
-    op("v", lambda: V.memset(T.fl[:, (NP - 1) * C:NP * C + 64], 0.0), w=["fz1"])
+    op("g", lambda: g.iota(T.ui[:], [[16, 8]], 0, 0), w=["ui"])
+    count(T.ng[:], [[0, Q4]], int(DOWN) // 64, 0, "ng")
+    count(T.ct[:], [[0, 512]], 0, 0, "ct")
+    count(T.rs[:], [[0, C]], 4096, 0, "rs")
+    op("v", lambda: V.memset(T.et[:], 0.0), w=["et"])
     ts(T.pi[:, 1:2], T.pi[:, 0:1], 15, None, A.bitwise_and, None, ["pi0"], ["pi1"])
     ts(T.pi[:, 2:3], T.pi[:, 0:1], 2, 3, A.logical_shift_right, A.bitwise_and, ["pi0"], ["pi2"])
     ts(T.pi[:, 3:4], T.pi[:, 0:1], 3, None, A.bitwise_and, None, ["pi0"], ["pi3"])
     ts(T.pi[:, 4:5], T.pi[:, 0:1], 4, None, A.logical_shift_right, None, ["pi0"], ["pi4"])
-    op("v", lambda: V.quantize_mx(T.qf[:, 0:128], T.sf[:, 0:128], T.fl[:, 0:512]), r=["fz0", "dgA", "dgB"],
-       w=["qz0", "qf%d" % (len(CUTS) - 2), "qf%d" % (len(CUTS) - 3)])
-    op("v", lambda: V.tensor_copy(T.pf[:, 0:4], T.pi[:, 1:5]), r=["pi1", "pi2", "pi3", "pi4"], w=["pf"])
-    op("v", lambda: V.quantize_mx(T.qf[:, (NP - 1) * Q4:NP * Q4 + 16], T.sf[:, (NP - 1) * Q4:NP * Q4 + 16],
-                                  T.fl[:, (NP - 1) * C:NP * C + 64]), r=["fz1"], w=["qz1", "qf0"])
-    ts(T.ka[:, 0:4], T.i4[:], T.pf[:, 1:2], UP, A.is_equal, A.mult, ["i4", "pf"], ["ka0"])
-    op("v", lambda: V.memset(T.ct[:], 0.0), w=["ct"])
-    op("v", lambda: V.memset(T.rs[:], 4096.0), w=["rs"])
-    ts(T.ka[:, 4:7], T.ka[:, 1:4], DOWN / UP, None, A.mult, None, ["ka0"], ["ka1"])
-    ts(T.ka[:, 7:8], T.ka[:, 0:1], DOWN / UP, None, A.mult, None, ["ka0"], ["ka2"])
-    ts(T.m01[:], T.rr[:], T.pf[:, 0:1], None, A.is_equal, None, ["rr", "pf"], ["m01"])
-    op("v", lambda: V.tensor_tensor(T.ka[:, 8:12], T.ka[:, 0:4], T.ka[:, 4:8], A.add), r=["ka0", "ka1", "ka2"], w=["ka"])
-    ts(T.gm[:], T.gq[:], T.pf[:, 3:4], -1.0, A.is_equal, A.mult, ["gq", "pf"], ["gm"])
-    op("v", lambda: V.tensor_copy(T.uo[:], T.ui[:]), r=["ui"], w=["uo"])
-    ts(T.pf[:, 4:5], T.ka[:, 7:8], -1.0, H - UP, A.mult, A.add, ["ka2"], ["pf4"])
-    ts(T.pf[:, 5:6], T.ka[:, 7:8], -4.0, 4 * (256 - UP), A.mult, A.add, ["ka2"], ["pf5"])
-    ts(T.pf[:, 6:7], T.ka[:, 11:12], -16.0, None, A.add, None, ["ka"], ["pf6"])
-    op("v", lambda: V.memset(T.et[:], 0.0), w=["et"])
-    op("v", lambda: V.tensor_tensor(T.pf[:, 8:9], T.pf[:, 4:5], T.pf[:, 0:1], A.add), r=["pf", "pf4"], w=["cr"])
-    op("v", lambda: V.tensor_tensor(T.pf[:, 9:10], T.pf[:, 5:6], T.pf[:, 2:3], A.add), r=["pf", "pf5"], w=["cx"])
+    quant(T.qf, T.sf, 0, 128, T.et[:, 0:512], ["et"], qfk(0, 32))
+    copy("v", T.pf[:, 0:4], T.pi[:, 1:5], ["pi1", "pi2", "pi3", "pi4"], ["pf"])
+    quant(T.qf, T.sf, (NP - 1) * Q4, NP * Q4 + 16, T.et[:, 0:512], ["et"], qfk(NB * (NP - 1), NB * NP + 4))
+    ts(T.ka[:, 0:8], T.i4[:], T.pf[:, 1:2], UP, A.is_equal, A.mult, ["i4", "pf"], ["ka0"])
+    ts(T.ka[:, 8:16], T.i4[:], T.pf[:, 1:2], 64.0, A.is_equal, A.mult, ["i4", "pf"], ["ka1"])
     ts(T.et[:, 3:515:4], T.idn[:], 0.0, None, A.is_equal, None, ["idn"], ["et"])
+    ts(T.m01[:], T.rr[:], T.pf[:, 0:1], None, A.is_equal, None, ["rr", "pf"], ["m01"])
+    ts(T.gm[:], T.gq[:], T.pf[:, 3:4], -1.0, A.is_equal, A.mult, ["gq", "pf"], ["gm"])
+    copy("v", T.uo[:], T.ui[:], ["ui"], ["uo"])
 
-    op("a", lambda: S.activation(T.mrs[:], T.rr[:], F.Identity, bias=BIG, scale=-2 * BIG), r=["rr"], w=["mrs"])
-    op("a", lambda: S.activation(T.mpm[:], T.m01[:], F.Identity, bias=BIG, scale=-2 * BIG), r=["m01"], w=["mpm"])
-    for i in range(4):
-        op("a", lambda: S.activation(T.ct[:, 5 * i:512:16], T.gm[:], F.Copy), r=["gm", "ct"], w=["ct%d" % i])
-    for i in range(4):
-        op("a", lambda: S.activation(T.mh[:, i:C:4], T.rr[:, 0:Q4], F.Identity, bias=T.ka[:, 8 + i:9 + i], scale=0.0),
-           r=["rr", "ka"], w=["mh%d" % i])
+    I = F.Identity
     mh = ["mh%d" % i for i in range(4)]
-    mz = ["mz%d" % i for i in range(4)]
-    op("a", lambda: S.activation(T.rs[:, 0:H:16], T.rr[:, 0:HB], F.Identity, bias=T.pf[:, 6:7], scale=0.0), r=["rr", "rs", "pf6"], w=["rsA"])
-    op("a", lambda: S.activation(T.rs[:, H:C:16], T.rr[:, 0:HB], F.Identity, bias=T.ka[:, 11:12], scale=0.0), r=["rr", "rs", "ka"], w=["rsB"])
-    op("a", lambda: S.activation(T.mz[:], T.mh[:, 0:Q4], F.Copy), r=mh, w=mz)
-
-    def unit(i):
-        op("v", lambda: V.quantize_mx(T.qe[:, 128 * i:128 * i + 128], T.se[:, 128 * i:128 * i + 128], T.et[:, 3 - i:515 - i]),
-           r=["et"], w=["e%d" % i])
-
-    def pick_u():
-        op("v", lambda: V.quantize_mx(T.qu[:], T.su[:], T.ut[:]), r=["ut"], w=["qu"])
-        op("v", lambda: V.tensor_copy(T.qu2[:].bitcast(u32), T.qu[:].bitcast(u32).indirect(T.uo[:])), r=["qu", "uo"], w=["qu2"])
-        op("a", lambda: S.activation(T.su2[:], T.su[:].indirect(T.uo[:]), F.Copy), r=["qu", "uo"], w=["su2"])
+    mz = ["mz%d" % i for i in range(NB)]
+    act(T.pf[:, 4:5], T.pf[:, 0:1], I, ["pf"], ["pf4"], bias=H - UP)
+    act(T.pf[:, 5:6], T.pf[:, 2:3], I, ["pf"], ["pf5"], bias=4 * (256 - UP))
+    act(T.mrs[:], T.rr[:], I, ["rr"], ["mrs"], bias=BIG, scale=-2 * BIG)
+    act(T.pf[:, 8:9], T.ka[:, 0:1], I, ["ka0", "pf4"], ["cr"], bias=T.pf[:, 4:5], scale=-DOWN / UP)
+    act(T.pf[:, 9:10], T.ka[:, 0:1], I, ["ka0", "pf5"], ["cx"], bias=T.pf[:, 5:6], scale=-4 * DOWN / UP)
+    act(T.mpm[:], T.m01[:], I, ["m01"], ["mpm"], bias=BIG, scale=-2 * BIG)
+    for i in range(4):
+        act(T.mh[:, i:C:4], T.ng[:], I, ["ng", "ka0", "ka1"], [mh[i]], bias=T.ka[:, i:i + 1], scale=T.ka[:, 9 + i:10 + i])
+    act(T.pf[:, 6:7], T.mh[:, 3:4], I, mh, ["pf6"], bias=-16.0)
+    stay(*[k for k in born if k[0] != "X"])
 
     def quant_x(lo, hi, key):
-        op("v", lambda: V.quantize_mx(T.qx[:, lo:hi], T.sx[:, lo:hi], T.X[:, 4 * lo:4 * hi]), r=xk(lo, hi), w=[key])
+        quant(T.qx, T.sx, lo, hi, T.X[:, 4 * lo:4 * hi], xk(lo, hi) + (["pt"] if now[0] else []), [key])
 
     def mm(b, lq, ls, rq, rs, m, r):
+        holds[b] = r[-1]
         op("p", lambda: g.tensor.matmul_mx(bank(b, m), lq, ls, rq, rs, True, True), r=r, w=["bk%d" % b])
 
-    def pick(q, out, src, r, w):
-        if q == "v":
-            op("v", lambda: V.tensor_copy(out, src), r=r, w=w)
-        else:
-            op("a", lambda: S.activation(out, src, F.Copy), r=r, w=w)
+    def patch():
+        copy("v", T.X[:].indirect(T.ob[:]), T.ds[:], ["ds0", "ds1", "ob"], xk(0, C) + ["pt"])
 
-    def gather(t, q, lo, hi):
-        pick(q, T.X[:, 4 * lo:4 * hi], T["Y%d" % t][:, 0:4 * (C if EARLY else C + K)].indirect(T.ox[:, lo // 4:hi // 4]),
-             ["Y%d%d%d" % (t, b, i) for b in range(4) for i in range(NH)] + ([] if EARLY else ["ds0", "ds1"]) + ["ox"], xk(lo, hi))
+    def pick(out, src, lo, hi, r, w):
+        scan(out, src, T.mh[:, lo:hi], DOWN, A.max, A.add, r + mh, w)
+
+    def offsets(out, src, r, w):
+        ts(out, src, 4.0, T.pf[:, 9:10], A.mult, A.add, r + ["cx"], w)
 
     for t in range(R):
         Y, qy, sy, qn, sn, ls, ln = (T[k + str(t)] for k in ("Y", "qy", "sy", "qn", "sn", "ls", "ln"))
-        front = FRONT[min(t, 1)]
-
-        def layer(b, h):
-            lo, hi = PART[h]
-            mm(b, T.qw[:, 128 * b:128 * b + 128], T.sw[:, 128 * b:128 * b + 128],
-               T.qx[:, lo:hi], T.sx[:, lo:hi], hi - lo, ["w%d" % b, "sw", "qx%d" % h])
-
-        def to_y(q, b, h):
-            lo, hi = PART[h]
-            out, src = Y[:, 4 * lo + b:4 * hi:4], bank(b, hi - lo)
-            if q == "a":
-                op("a", lambda: S.activation(out, src, F.Copy, scale=0.03125), x=["bk%d" % b], w=["Y%d%d%d" % (t, b, h)])
-            else:
-                op("v", lambda: V.tensor_scalar(out, src, 0.03125, None, A.mult), x=["bk%d" % b], w=["Y%d%d%d" % (t, b, h)])
-
-        def quant_y(h):
-            lo, hi = PART[h]
-            op("v", lambda: V.quantize_mx(qy[:, lo:hi], sy[:, lo:hi], Y[:, 4 * lo:4 * hi]),
-               r=["Y%d%d%d" % (t, b, h) for b in range(4)], w=["qy%d%d" % (t, h)])
-
+        words = FRONT[min(t, len(FRONT) - 1)].split()
+        his = [int(w[1:3]) for w in words if w[0] == "n"]
         base = {}
+        dgs = [w for w in words if w[0] == "d"]
+        todo, whole = list(range(NP - 1, -1, -1)), set(range(HB)) | set(range(NB * NP, NB * NP + 4))
 
-        def scores(b, lo, hi):
-            base[b] = (lo, hi)
-            mm(b, T.qu2[:], T.su2[:], qy[:, lo:hi], sy[:, lo:hi], hi - lo, ["qu2", "su2"] + ["qy%d%d" % (t, i) for i in parts(lo, hi)])
+        def qyk(lo, hi):
+            return ["qy%d%d" % (t, i) for i in parts(lo, hi)]
 
         def sco(banks, lo, hi):
             b = [i for i in banks if i in base and base[i][0] <= lo and hi <= base[i][1]][0]
-            return b, bank(b, hi - base[b][0], lo - base[b][0])
+            return bank(b, hi - base[b][0], lo - base[b][0]), ["bk%d" % b]
 
-        def own_mask(h):
-            lo, hi = PART[h]
-            b, p = sco((4, 5), lo, hi)
-            op("v", lambda: V.tensor_tensor(T.d1[:, lo:hi], p, T.mpm[:, 0:hi - lo], A.max), r=["mpm"], x=["bk%d" % b], w=["d1%d" % h])
+        def sk(lo, hi):
+            return ["S%d" % i for i in range(lo // 16, hi // 16)]
 
-        def own_scan(h):
-            lo, hi = PART[h]
-            op("v", lambda: V.tensor_tensor_scan(T.S[:, lo:hi], T.mrs[:, 0:hi - lo], T.d1[:, lo:hi], BIG, A.max, A.min),
-               r=["mrs", "d1%d" % h], w=["S%d" % h])
+        def fk(c):
+            return [("h%d_%d" if c in his else "f%d_%d") % (c, k) for k in range(2) if side(c, k)[1] > side(c, k)[0]]
 
-        def diag(k):
-            lo, at = (0, C) if k == "A" else (H, H)
-            b, p = sco((4, 5), lo, lo + H)
-            op("v", lambda: V.tensor_tensor(T.fl[:, at:at + H], p, T.S[:, lo:lo + H], A.is_gt),
-               r=["S%d" % i for i in parts(lo, lo + H)], x=["bk%d" % b], w=["dg" + k])
+        def unpack(b):
+            act(T.dall[:, b:4 * C:4], bank(4 + b, C), F.Copy, [], ["dall%d" % b], ["bk%d" % (4 + b)])
 
-        def diag_rows(k):
-            lo, at = (0, C) if k == "A" else (H, H)
-            op("v", lambda: V.tensor_tensor_scan(T.fr[:, lo:lo + H], T.rs[:, lo:lo + H], T.fl[:, at:at + H], 4096.0, A.min, A.add),
-               r=["rs" + k, "dg" + k], w=["fr" + k])
+        def gather(q, lo, hi):
+            copy(q, T.X[:, 4 * lo:4 * hi], Y[:].indirect(T.ox[:, lo // 4:hi // 4]),
+                 ["Y%d%d%d" % (t, b, i) for b in range(4) for i in range(NH)] + ["ox"], xk(lo, hi))
 
-        def skey(c):
-            return "S%d" % parts(16 * c, 16 * c + 16)[0]
-
-        def flags(c, side):
-            s, m = cell(c)
-            lat = min(m, NB - 1 - c)
-            lo, hi, at = (c + 1, c + 1 + lat, s) if side == 0 else (0, m - lat, s + lat)
-            if hi > lo:
-                b, p = sco((4, 5), 16 * lo, 16 * hi)
-                op("v", lambda: V.tensor_scalar(T.fl[:, 16 * at:16 * (at + hi - lo)], p, T.S[:, 16 * c + 15:16 * c + 16],
-                                                None, A.is_ge if side else A.is_gt),
-                   r=[skey(c), "qz0", "qz1"], x=["bk%d" % b], w=["f%d_%d" % (c, side)])
-
-        def rowsum(c):
-            s, m = cell(c)
-            op("v", lambda: V.tensor_tensor_scan(T.rj[:, Q4 * (c + 1) - 8 * m:Q4 * (c + 1)], T.fl[:, 16 * s:16 * s + 8 * m],
-                                                 T.fl[:, 16 * s + 8 * m:16 * (s + m)], 0.0, A.add, A.add),
-               r=["f%d_0" % c, "f%d_1" % c], w=["rj%d" % c])
-
-        def sign(c):
-            s, m = cell(c)
-            lo = 16 * ((c + 1) % NB)
-            b, p = sco((6, 7), lo, lo + 16 * m)
-            op("a", lambda: S.activation(T.fl[:, 16 * s:16 * (s + m)], p, F.Sign, bias=T.S[:, 16 * c + 15:16 * c + 16], scale=-1.0),
-               r=[skey(c), "qz0", "qz1"], x=["bk%d" % b], w=["f%d_0" % c])
-
-        def step(c):
-            s, m = cell(c)
-            v = T.fl[:, 16 * s:16 * (s + m)]
-            if c == NB - 1:
-                op("a", lambda: S.activation(v, v, F.Sign, bias=1.0, scale=-1.0, accum_out=T.ra[:, c:c + 1]), w=["f%d_0" % c, "ra%d" % c])
-            else:
-                op("a", lambda: S.activation(v, v, F.Relu, scale=-1.0, accum_out=T.ra[:, c:c + 1]), w=["f%d_0" % c, "ra%d" % c])
-
-        done = [0]
-
-        def inside(i):
-            return [c for c in range(NB) if cell(c)[0] < CUTS[i] and sum(cell(c)) > CUTS[i + 1]]
-
-        def columns(i):
-            hi, lo = CUTS[i], CUTS[i + 1]
-            r = ["f%d_%d" % (c, k) for c in inside(i) for k in range(2)] + (["dgA", "dgB"] if lo < 3 * HB else [])
-            op("v", lambda: V.quantize_mx(T.qf[:, 4 * lo:4 * hi], T.sf[:, 4 * lo:4 * hi], T.fl[:, 16 * lo:16 * hi]), r=r, w=["qf%d" % i])
-            while done[0] < NP and (NB * (NP - 1 - done[0]) >= lo or i == len(CUTS) - 2):
-                s = NP - 1 - done[0]
-                done[0] += 1
-                op("p", lambda: g.tensor.matmul_mx(bank(0, 128), T.qc[:], T.sc[:], T.qf[:, Q4 * s:Q4 * s + 128], T.sf[:, Q4 * s:Q4 * s + 128],
-                                                   s == NP - 1, s == 0),
-                   r=["qc", "qz0", "qz1"] + ["qf%d" % k for k in range(max(i - 1, 0), i + 1)],
-                   w=["bk0"] if s == NP - 1 else [], s=["bk0"])
-
-        def rows(lo, hi, src, r, key):
-            op("v", lambda: V.tensor_tensor(T.mz[:, 4 * lo + 3:4 * hi:4], src, T.fr[:, 16 * lo + 15:16 * hi:16], A.add), r=r, w=[key])
-
-        for word in front.split():
+        for word in words:
             k, q, z = word[0], word[1], word[2:]
-            if k == "g":
-                gather(t - 1, q, *(int(i) for i in z.split("-")))
+            if k == "p":
+                patch()
             elif k == "x":
                 quant_x(*PART[int(q)], "qx" + q)
-            elif k == "L":
-                for b in range(4):
-                    layer(b, int(q))
             elif k == "l":
-                layer(int(q), int(z))
+                b, (lo, hi) = int(q), PART[int(z)]
+                mm(b, T.qw[:, 128 * b:128 * b + 128], T.sw[:, 128 * b:128 * b + 128],
+                   T.qx[:, lo:hi], T.sx[:, lo:hi], hi - lo, ["w" + q, "sw", "qx" + z])
             elif k == "y":
-                to_y(q, int(z[0]), int(z[1]))
+                b, (lo, hi) = int(z[0]), PART[int(z[1])]
+                assert holds[b] == "qx" + z[1] and born["bk" + z[0]] == now[0]
+                out, src, key = Y[:, 4 * lo + b:4 * hi:4], bank(b, hi - lo), "Y%d%s" % (t, z)
+                if q == "a":
+                    act(out, src, F.Copy, [], [key], ["bk" + z[0]], scale=0.03125)
+                else:
+                    op("v", lambda: V.tensor_scalar(out, src, 0.03125, None, A.mult), x=["bk" + z[0]], w=[key])
+                stay(key)
             elif k == "q":
-                quant_y(int(q))
+                lo, hi = PART[int(q)]
+                quant(qy, sy, lo, hi, Y[:, 4 * lo:4 * hi], ["Y%d%d%s" % (t, b, q) for b in range(4)], ["qy%d%s" % (t, q)])
             elif k == "P":
-                scores(int(q), *(int(i) for i in z[1:].split("-")))
+                lo, hi = base[int(q)] = span(z[1:])
+                mm(int(q), T.qu2[:], T.su2[:], qy[:, lo:hi], sy[:, lo:hi], hi - lo, ["qu2", "su2"] + qyk(lo, hi))
             elif k == "m":
-                own_mask(int(q))
+                lo, hi = span(q + z)
+                p, x = sco((4, 5), lo, hi)
+                tt(T.d1[:, lo:hi], p, T.mpm[:, 0:hi - lo], A.max, ["mpm"], ["d1%d" % lo], x)
             elif k == "s":
-                own_scan(int(q))
+                lo, hi = span(q + z)
+                scan(T.S[:, lo:hi], T.mrs[:, 0:hi - lo], T.d1[:, lo:hi], BIG, A.max, A.min, ["mrs", "d1%d" % lo], sk(lo, hi))
             elif k == "d":
-                diag(q)
+                lo, hi = span(q + z)
+                at = lo + (C if lo < H else 0)
+                p, x = sco((4, 5), lo, hi)
+                tt(T.fl[:, at:at + hi - lo], p, T.S[:, lo:hi], A.is_gt, sk(lo, hi), [word], x)
             elif k == "r":
-                diag_rows(q)
+                lo, at = (0, C) if q == "A" else (H, H)
+                scan(T.fr[:, lo:lo + H], T.rs[:, lo:lo + H], T.fl[:, at:at + H], 4096.0, A.min, A.add,
+                     ["rs" + q] + [d for d in dgs if (span(d[1:])[0] < H) == (q == "A")], ["fr" + q])
             elif k == "u":
-                pick_u()
+                quant(T.qu, T.su, 0, 128, T.ut[:], ["ut"], ["qu"])
+                copy("v", T.qu2[:].bitcast(u32), T.qu[:].bitcast(u32).indirect(T.uo[:]), ["qu", "uo"], ["qu2"])
+                copy("a", T.su2[:], T.su[:].indirect(T.uo[:]), ["qu", "uo"], ["su2"])
+                stay("qu2", "su2")
+            elif k == "i":
+                count(T.jc[:], [[1, C]], -256, 0, "jc")
+                count(T.o[:, C:512], [[0, K]], -256, 0, "o_x")
+                stay("jc", "o_x")
+            elif k == "j":
+                for i in range(4):
+                    act(T.ct[:, 5 * i:512:16], T.gm[:], F.Copy, ["gm", "ct"], ["ct%d" % i])
+            elif k == "J":
+                act(T.rs[:, 0:H:16], T.rr[:, 0:HB], I, ["rr", "rs", "pf6"], ["rsA"], bias=T.pf[:, 6:7], scale=0.0)
+                act(T.rs[:, H:C:16], T.rr[:, 0:HB], I, ["rr", "rs"] + mh, ["rsB"], bias=T.mh[:, 3:4], scale=0.0)
+                act(T.mz[:], T.mh[:, 0:Q4], F.Copy, mh, mz)
+                stay("rsA", "rsB")
             elif k == "e":
-                unit(int(q))
+                i = int(q)
+                quant(T.qe, T.se, 128 * i, 128 * i + 128, T.et[:, 3 - i:515 - i], ["et"], [word])
+                stay(word)
             elif k == "c":
-                op("v", lambda: V.quantize_mx(T.qc[:], T.sc[:], T.ct[:]), r=["ct%d" % i for i in range(4)], w=["qc"])
-            elif k == "f":
-                flags(int(q), 0)
+                quant(T.qc, T.sc, 0, 128, T.ct[:], ["ct%d" % i for i in range(4)], ["qc"])
+                stay("qc")
+            elif k in "fnN":
+                c, e = int(word[1:3]), int(word[3])
+                lo, hi, at = side(c, e)
+                v, own = T.fl[:, 16 * at:16 * (at + hi - lo)], T.S[:, 16 * c + 15:16 * c + 16]
+                w = ["f%d_%d" % (c, e), "h%d_%d" % (c, e)]
+                if k == "N" and e:
+                    act(v, v, F.Sign, w[:1], w + ["ra%d" % c], bias=1.0, scale=-1.0, accum_out=T.ra[:, c:c + 1])
+                elif k == "N":
+                    act(v, v, F.Relu, w[:1], w + ["ra%d" % c], scale=-1.0, accum_out=T.ra[:, c:c + 1])
+                elif k == "n":
+                    p, x = sco((6, 7), 16 * lo, 16 * hi)
+                    act(v, p, F.Sign, ["S%d" % c], w, x, bias=own, scale=-1.0)
+                    born[w[1]] = -2
+                else:
+                    p, x = sco((4, 5), 16 * lo, 16 * hi)
+                    op("v", lambda: V.tensor_scalar(v, p, own, None, A.is_ge if e else A.is_gt), r=["S%d" % c], w=w, x=x)
             elif k == "F":
-                rowsum(int(q))
+                c = int(q + z)
+                s, m = cell(c)
+                scan(T.rj[:, Q4 * (c + 1) - 8 * m:Q4 * (c + 1)], T.fl[:, 16 * s:16 * s + 8 * m], T.fl[:, 16 * s + 8 * m:16 * (s + m)],
+                     0.0, A.add, A.add, fk(c), ["rj%d" % c])
+            elif k == "Q":
+                lo, hi = PIECES[int(q + z)]
+                r = [i for c in range(NB) for e in range(2) for i in fk(c)
+                     if i[-1] == str(e) and side(c, e)[2] < hi and side(c, e)[2] + side(c, e)[1] - side(c, e)[0] > lo]
+                quant(T.qf, T.sf, 4 * lo, 4 * hi, T.fl[:, 16 * lo:16 * hi], r + (dgs if lo < 3 * HB else []), qfk(lo, hi))
+                stay(*qfk(lo, hi))
+                whole.update(range(lo, hi))
+                for s in [s for s in todo if whole.issuperset(range(NB * s, NB * s + 32))]:
+                    first = len(todo) == NP
+                    assert not first or all(born.get("Y%d0%d" % (t, h)) == -1 for h in range(NH))
+                    todo.remove(s)
+                    op("p", lambda: g.tensor.matmul_mx(bank(0, 128), T.qc[:], T.sc[:], T.qf[:, Q4 * s:Q4 * s + 128], T.sf[:, Q4 * s:Q4 * s + 128],
+                                                       first, not todo),
+                       r=["qc"] + qfk(NB * s, NB * s + 32), w=["bk0"] if first else [], s=["bk0"])
+            elif k == "M":
+                lo, hi = span(q + z)
+                fr = ["frA"] * (lo < HB) + ["frB"] * (hi > HB)
+                src, key = (T.ra[:, lo:hi], "ra%d") if lo in his else (T.rj[:, Q4 * (lo + 1) - 1:Q4 * hi:Q4], "rj%d")
+                tt(T.mz[:, 4 * lo + 3:4 * hi:4], src, T.fr[:, 16 * lo + 15:16 * hi:16], A.add, fr + [key % c for c in range(lo, hi)], mz[lo:hi])
             elif k == "t":
-                lo, hi = (int(i) for i in (q + z).split("-"))
-                send(qn[:, lo:hi].bitcast(u8), qy[:, lo:hi].bitcast(u8), "aq%d" % t, ["qy%d%d" % (t, i) for i in parts(0, hi)])
+                lo, hi = span(q + z)
+                send(qn[:, lo:hi].bitcast(u8), qy[:, lo:hi].bitcast(u8), "aq%d" % t, qyk(lo, hi))
             elif k == "T":
-                send(sn[:], sy[:], "aq%d" % t, [])
-            elif k == "S":
-                his = SROWS[t]
-                sign(his[0])
-                for i, c in enumerate(his):
-                    if i + 1 < len(his):
-                        sign(his[i + 1])
-                    step(c)
+                send(sn[:], sy[:], "aq%d" % t, qyk(0, C))
+        assert not todo
 
-        mine = VROWS[t]
-        piece = 0
-        for i, c in enumerate(mine):
-            flags(c, 0)
-            flags(c, 1)
-            if i > 0:
-                rowsum(mine[i - 1])
-            if piece < len(CUTS) - 3 and not set(mine[i:]).intersection(inside(piece)) and i >= LAG[t] + STEP * piece:
-                columns(piece)
-                piece += 1
-        while piece < len(CUTS) - 3:
-            columns(piece)
-            piece += 1
-        rowsum(mine[-1])
-        columns(piece)
-        runs = []
-        for c in range(NB):
-            if runs and (c in SROWS[t]) == (c - 1 in SROWS[t]):
-                runs[-1][1] = c + 1
-            else:
-                runs.append([c, c + 1])
-        order("v", (), mz, ())
-        for i, (lo, hi) in enumerate(runs):
-            if lo not in SROWS[t]:
-                rows(lo, hi, T.rj[:, Q4 * (lo + 1) - 1:Q4 * hi:Q4], ["frA", "frB"] + ["rj%d" % c for c in range(lo, hi)], mz[i])
-        columns(piece + 1)
-        for i, (lo, hi) in enumerate(runs):
-            if lo in SROWS[t]:
-                rows(lo, hi, T.ra[:, lo:hi], ["frA", "frB"] + ["ra%d" % c for c in range(lo, hi)], mz[i])
-        wr["qn%d" % t] = ("aq%d" % t, front.lower().count("t") * back)
+        wr["qn%d" % t], born["qn%d" % t] = ("aq%d" % t, len([w for w in words if w[0] in "tT"]) * back), -1
         for b in range(4):
             mm(4 + b, T.qe[:, 128 * b:128 * b + 128], T.se[:, 128 * b:128 * b + 128], qn[:], sn[:], C, ["e%d" % b, "qn%d" % t])
-        for b in range(4):
-            op("a", lambda: S.activation(T.dall[:, b:4 * C:4], bank(4 + b, C), F.Copy), x=["bk%d" % (4 + b)], w=["dall%d" % b])
-        op("v", lambda: V.tensor_tensor_scan(T.zz[:], bank(0, Q4), T.mz[:], DOWN, A.max, A.add), r=mz, x=["bk0"], w=["zz"])
+        for b in range(3):
+            unpack(b)
+        scan(T.zz[:], bank(0, Q4), T.mz[:], DOWN, A.max, A.add, mz, ["zz"], ["bk0"])
         ts(T.oi[:, 0:NB], T.zz[:, 3:Q4:4], T.pf[:, 8:9], None, A.add, None, ["zz", "cr"], ["oi"])
 
-        op("v", lambda: V.tensor_copy(T.o[:, 0:C].indirect(T.oi[:, 0:NB]), T.jc[:]), r=["oi", "jc"], w=["o"])
-        op("v", lambda: V.tensor_tensor_scan(T.t2[:], T.o[:, 0:K], T.mh[:, 0:K], DOWN, A.max, A.add), r=["o"] + mh, w=["t2"])
-        if EARLY:
-            op("v", lambda: V.tensor_tensor_scan(T.b2[:], T.o[:, C - K:C], T.mh[:, 0:K], DOWN, A.max, A.add), r=["o"] + mh, w=["b2"])
-        ts(ls[:], T.t2[:, 3:K:4], 4.0, T.pf[:, 9:10], A.mult, A.add, ["t2", "cx"], ["ls%d" % t])
+        copy("v", T.o[:, 0:C].indirect(T.oi[:, 0:NB]), T.jc[:], ["oi", "jc"], ["o"])
+        pick(T.t2[:], T.o[:, 0:K], 0, K, ["o"], ["t2"])
+        pick(T.b2[:], T.o[:, C - K:C], 0, K, ["o"], ["b2"])
+        offsets(ls[:], T.t2[:, 3:K:4], ["t2"], ["ls%d" % t])
         send(ln[:], ls[:], "al%d" % t, ["ls%d" % t])
-        wr["ln%d" % t] = ("al%d" % t, back)
+        wr["ln%d" % t], born["ln%d" % t] = ("al%d" % t, back), -1
 
-        pick("v", T.e1[:, 0:16 * EV], T.o[:, K:512].indirect(T.oi[:, 0:EV]), ["o", "o_x", "oi"], ["e1a"])
-        if EV < NB:
-            pick("a", T.e1[:, 16 * EV:C], T.o[:, K:512].indirect(T.oi[:, EV:NB]), ["o", "o_x", "oi"], ["e1b"])
+        copy("v", T.e1[:, 0:16 * EV], T.o[:, K:512].indirect(T.oi[:, 0:EV]), ["o", "o_x", "oi"], ["e1a"])
+        copy("a", T.e1[:, 16 * EV:C], T.o[:, K:512].indirect(T.oi[:, EV:NB]), ["o", "o_x", "oi"], ["e1b"])
+        unpack(3)
         if t == R - 1:
-            op("a", lambda: S.activation(T.of[:], T.o[:, 0:C], F.Identity, bias=256.0), r=["o"], w=["of"])
+            act(T.of[:], T.o[:, 0:C], I, ["o"], ["of"], bias=256.0)
             dma("s", T.ol[:], T.of[0:128:16, :], r=["of"])
-        if EARLY:
-            ts(T.ob[:], T.b2[:, 3:K:4], 4.0, T.pf[:, 9:10], A.mult, A.add, ["b2", "cx"], ["ob"])
-        op("v", lambda: V.tensor_tensor_scan(T.e2[:], T.e1[:], T.mh[:], DOWN, A.max, A.add), r=["e1a", "e1b"] + mh, w=["e2"])
+        stay("b2", "dall0", "dall1", "dall2", "dall3", "e1a", "e1b")
+        now[0] += 1
+        offsets(T.ob[:], T.b2[:, 3:K:4], ["b2"], ["ob"])
+        pick(T.e2[:], T.e1[:], 0, C, ["e1a", "e1b"], ["e2"])
         if t == 0:
-            op("v", lambda: V.quantize_mx(T.qv[:], T.sv[:], T.vt[:]), r=["vt"], w=["qv"])
-        ts(T.ox[:], T.e2[:, 3:C:4], 4.0, T.pf[:, 9:10], A.mult, A.add, ["e2", "cx"], ["ox"])
-        if EARLY:
-            gather(t, "a", 0, EARLY[0])
-            gather(t, "v", EARLY[0], C)
+            quant(T.qv, T.sv, 0, 128, T.vt[:], ["vt"], ["qv"])
+            stay("qv")
+        offsets(T.ox[:], T.e2[:, 3:C:4], ["e2"], ["ox"])
+        gather("a", 0, SHARE)
+        gather("v", SHARE, C)
         for i, q in enumerate("va"):
-            out = T.ds[:, 128 * i:128 * i + 128] if EARLY else Y[:, 4 * C + 128 * i:4 * C + 128 * i + 128]
-            pick(q, out, T.dall[:].indirect(ln[:, 8 * i:8 * i + 8]), ["dall%d" % b for b in range(4)] + ["ln%d" % t], ["ds%d" % i])
-        if EARLY:
-            op("v", lambda: V.tensor_copy(T.X[:].indirect(T.ob[:]), T.ds[:]), r=["ds0", "ds1", "ob"], w=xk(0, C))
+            copy(q, T.ds[:, 128 * i:128 * i + 128], T.dall[:].indirect(ln[:, 8 * i:8 * i + 8]),
+                 ["dall%d" % b for b in range(4)] + ["ln%d" % t], ["ds%d" % i])
 
     order("v", (), ["qx%d" % h for h in range(NH)], ())
-    for word in END.split():
-        k, q, z = word[0], word[1], word[2:]
-        if k == "g":
-            gather(R - 1, q, *(int(i) for i in z.split("-")))
-        elif k == "x":
-            quant_x(*OUT[int(q)], "qo" + q)
-        elif k == "y":
-            h = int(z)
-            lo, hi = OUT[h]
-            mm(h, T.qv[:], T.sv[:], T.qx[:, lo:hi], T.sx[:, lo:hi], hi - lo, ["qv", "qo" + z])
-            if q == "a":
-                op("a", lambda: S.activation(T.yo[:, lo:hi], bank(h, hi - lo), F.Copy), x=["bk" + z], w=["yo" + z])
-            else:
-                op("v", lambda: V.tensor_copy(T.yo[:, lo:hi], bank(h, hi - lo)), x=["bk" + z], w=["yo" + z])
-        elif k == "s":
-            dma(q, T.osc[4 * int(z):4 * int(z) + 4, :], T.sx[32 * int(z):32 * int(z) + 4, :], r=["qo%d" % h for h in range(len(OUT))])
-        else:
-            lo, hi = OUT[int(z[0])][0], OUT[int(z[-1])][1]
-            if k == "c":
-                dma(q, T.oc[:, 4 * lo:4 * hi], T.qx[:, lo:hi].bitcast(u8), r=["qo" + h for h in z])
-            else:
-                dma(q, T.y[:, lo:hi], T.yo[:, lo:hi], r=["yo" + h for h in z])
+    patch()
+    for h, q in enumerate("av"):
+        lo, hi = OUT[h]
+        quant_x(lo, hi, "qo%d" % h)
+        mm(h, T.qv[:], T.sv[:], T.qx[:, lo:hi], T.sx[:, lo:hi], hi - lo, ["qv", "qo%d" % h])
+        if h:
+            dma("s", T.oc[:], T.qx[:].bitcast(u8), r=["qo0", "qo1"])
+        copy(q, T.yo[:, lo:hi], bank(h, hi - lo), [], ["yo%d" % h], ["bk%d" % h])
+    for h, q in enumerate("as"):
+        lo, hi = OUT[h]
+        dma(q, T.y[:, lo:hi], T.yo[:, lo:hi], r=["yo%d" % h])
+    for k in range(4):
+        dma("a" if k < 2 else "s", T.osc[4 * k:4 * k + 4, :], T.sx[32 * k:32 * k + 4, :], r=["qo0", "qo1"])
 
     for q in cnt:
         wait("g", (csem[q], cnt[q]))

from concourse.mybir import dt, AluOpType as A, ActivationFunctionType as F

C, K, R = 448, 64, 3
PART = ((0, 128), (128, 288), (288, 448))
NB = C // 16
HB = NB // 2
H = C // 2
Q4 = C // 4
RANKS = (" m128-288 s128-288 P4:224-448 P7:80-448 m288-448 d0-224 s288-448 rA "
         "n000 n010 N000 n020 N010 n030 N020 n040 N030 n050 N040 n060 N050 n070 N060 n080 N070 n090 N080 n100 N090 n110 N100 n120 N110 "
         "n271 N120 n130 N271 N130 f161 d224-448 f140 rB f160 f170 f180 f151 f150 f191 f181 f190 f200 f171 F19 Q0 F14 F17 F15 F16 F18 "
         "f220 Q1 Q2 f210 f240 f230 f251 f201 f221 f260 F20 f250 f231 f241 f211 f261 Q3 F22 Q4 F25 F23 F21 Q5 Q6 Q7 F24 F26 "
         "M0-14 M27-28 M14-27")
FRONT = (
    "j_ x0 l10 l20 l00 l30 e3 e0 e2 e1 yv10 ya00 yv30 x1 ya20 J_ l31 l01 l21 l11 q0 u_ t0-128 P4:0-128 ya11 ya01 ya21 yv31 x2 "
    "l02 l22 l12 l32 m0-128 q1 t128-288 P6:0-288 P5:0-288 ya02 ya22 ya32 s0-128 yv12 c_ q2 t288-448 T_ i_" + RANKS,
    "p_ x0 l00 l10 l20 l30 x1 yv00 yv20 ya10 ya30 l01 l11 l21 l31 x2 q0 t0-128 ya01 ya11 P4:0-128 yv21 ya31 m0-128 q1 t128-288 "
    "l02 l22 l32 l12 ya02 yv32 s0-128 ya22 ya12 P6:0-288 P5:0-288 q2 t288-448 T_" + RANKS,
)
SHARE = 216
EV = 16
OUT = ((0, 256), (256, 448))
BIG = 2.0 ** 90
UP, DOWN = 1024.0, -1600.0
NP = HB + 1
PIECES = ((366, 420), (312, 366), (258, 312), (204, 258), (150, 204), (96, 150), (56, 96), (14, 56))
MW = 160

SCRATCH = {"ps": ("psum", [128, 4096], "float32")}
for _d, _l in (
        ("bfloat16", dict(X=4 * C, ut=512, vt=512, et=516, ct=512, jc=C, mh=C, rs=C, fl=NP * C, rj=NB * Q4, o=512, e1=C,
                          dall=4 * C, ds=4 * K, Y0=4 * C, Y1=4 * C, Y2=4 * C)),
        ("float8_e4m3fn_x4", dict(qx=C, qw=512, qu=128, qu2=128, qv=128, qe=512, qc=128, qf=NP * Q4 + 16,
                                  qy0=C, qy1=C, qy2=C, qn0=C, qn1=C, qn2=C)),
        ("uint8", dict(sx=C, sw=512, su=128, su2=128, sv=128, se=512, sc=128, sf=NP * Q4 + 16, sy0=C, sy1=C, sy2=C, sn0=C, sn1=C, sn2=C)),
        ("float32", dict(pf=16, rr=MW, idn=128, gq=32, gm=32, i4=8, ka=16, ng=Q4, m01=MW, mpm=MW, mrs=MW, mz=Q4, d1=C, S=C,
                         ra=32, zz=Q4, of=C, yo=C)),
        ("float16", dict(fr=C, t2=K, e2=C, b2=K)),
        ("int32", dict(pi=8, ui=8)),
        ("uint16", dict(uo=8, oi=32, ox=Q4, ob=16, ls0=16, ls1=16, ls2=16, ln0=16, ln1=16, ln2=16))):
    for _k, _n in _l.items():
        SCRATCH[_k] = ("sbuf", [128, _n], _d)

SEMAPHORES = (["cv", "ca", "cp", "cg", "sent"] + ["d%d" % i for i in range(24)]
              + ["aq%d" % t for t in range(R)] + ["al%d" % t for t in range(R)])


def rank_program(g, core, T, topo):
    rank = T.rank_of(core)
    if rank is None:
        return
    n = len(T.cores)
    dst = T.cores[(rank - 1) % n]
    rid, pid, _se = topo.addr(dst)
    mask = topo.mask(core, dst)
    neng = len(topo.engines(core, dst))
    back = len(topo.engines(T.cores[(rank + 1) % n], core))

    Q = {"v": g.vector, "a": g.scalar, "p": g.tensor, "g": g, "s": g.sync}
    csem = {"v": "cv", "a": "ca", "p": "cp", "g": "cg"}
    cnt = {"v": 0, "a": 0, "p": 0, "g": 0}
    waited = {q: {} for q in Q}
    wr, rd = {}, {}
    born, now, holds = {}, [0], {}
    ndma, dmas, sent = [0], [], [0]

    def wait(q, h):
        if waited[q].get(h[0], 0) < h[1]:
            Q[q].wait_ge(T.sem[h[0]], h[1])
            waited[q][h[0]] = h[1]

    def order(q, r, w, x):
        for k in r:
            assert born[k] in (-1, now[0]), k
        need = {}
        hs = [wr[k] for k in list(r) + list(w) + list(x) if k in wr]
        hs += [h for k in w for h in rd.get(k, [])]
        hs += [h for k in x for h in rd.get(k, []) if h[0] != csem.get(q)]
        for sm, c in hs:
            need[sm] = max(need.get(sm, 0), c)
        for sm in need:
            wait(q, (sm, need[sm]))

    def note(h, r, w, x):
        for k in list(r) + list(x):
            rd.setdefault(k, []).append(h)
        for k in w:
            wr[k] = h
            rd[k] = []
            born[k] = now[0]

    def stay(*keys):
        for k in keys:
            born[k] = -1

    def op(q, fn, r=(), w=(), x=(), s=()):
        order(q, r, w, x)
        cnt[q] += 1
        fn().then_inc(T.sem[csem[q]], 1)
        note((csem[q], cnt[q]), r, list(w) + list(s), x)

    def dma(q, out, in_, r=(), w=()):
        order(q, r, w, ())
        s = "d%d" % ndma[0]
        ndma[0] += 1
        Q[q].dma_start(out, in_).then_inc(T.sem[s], 16)
        dmas.append((s, 16))
        note((s, 16), r, w, ())

    def send(out, in_, sem, r):
        order("g", r, (), ())
        g.remote_dma(out, in_, T.sem[sem], T.sem.sent, pid, rid, mask)
        sent[0] += neng

    V, S = g.vector, g.scalar
    u8, u32 = dt.uint8, dt.uint32

    def bank(b, hi, lo=0):
        return T.ps[:, 512 * b + lo:512 * b + hi]

    def cell(c):
        a = c % HB
        s = 3 * HB + (NB - 1) * (HB - 1 - a)
        return (s, HB) if c < HB else (s + HB, HB - 1)

    def side(c, k):
        s, m = cell(c)
        lat = min(m, NB - 1 - c)
        return (c + 1, c + 1 + lat, s) if k == 0 else (0, m - lat, s + lat)

    NH = len(PART)

    def xk(lo, hi):
        return ["X%d" % i for i in range(lo // 8, hi // 8)]

    def parts(lo, hi):
        return [i for i in range(NH) if PART[i][0] < hi and PART[i][1] > lo]

    def span(z):
        return tuple(int(i) for i in z.split("-"))

    def load_x(q, h):
        lo, hi = PART[h]
        dma(q, T.X[:, 4 * lo:4 * hi], T.x[:, 4 * lo:4 * hi], w=xk(lo, hi))

    load_x("s", 0)
    dma("a", T.sw[:], T.ws[:], w=["sw"])
    dma("a", T.qw[:, 0:256].bitcast(u8), T.wc[:, 0:1024], w=["w0", "w1"])
    dma("s", T.qw[:, 256:512].bitcast(u8), T.wc[:, 1024:2048], w=["w2", "w3"])
    load_x("a", 1)
    dma("s", T.ut[:], T.u[:], w=["ut"])
    load_x("s", 2)
    dma("s", T.vt[:], T.v[:], r=xk(*PART[-1]), w=["vt"])

    def count(out, pattern, base, step, *key):
        op("g", lambda: g.iota(out, pattern, base, step, allow_small_or_imprecise_dtypes=True), w=key)

    def ts(out, in0, s1, s2, o0, o1, r, w):
        if o1 is None:
            op("v", lambda: V.tensor_scalar(out, in0, s1, None, o0), r=r, w=w)
        else:
            op("v", lambda: V.tensor_scalar(out, in0, s1, s2, o0, o1), r=r, w=w)

    def tt(out, a, b, o, r, w, x=()):
        op("v", lambda: V.tensor_tensor(out, a, b, o), r=r, w=w, x=x)

    def scan(out, a, b, init, o0, o1, r, w, x=()):
        op("v", lambda: V.tensor_tensor_scan(out, a, b, init, o0, o1), r=r, w=w, x=x)

    def act(out, in_, f, r, w, x=(), **kw):
        op("a", lambda: S.activation(out, in_, f, **kw), r=r, w=w, x=x)

    def quant(q, s, lo, hi, src, r, w):
        op("v", lambda: V.quantize_mx(q[:, lo:hi], s[:, lo:hi], src), r=r, w=w)

    def copy(q, out, src, r, w, x=()):
        if q == "v":
            op("v", lambda: V.tensor_copy(out, src), r=r, w=w, x=x)
        else:
            act(out, src, F.Copy, r, w, x)

    def qfk(lo, hi):
        return ["qf%d" % k for k in range(lo, hi)]

    op("g", lambda: g.iota(T.pi[:, 0:1], [[1, 1]], 0, 1), w=["pi0"])
    count(T.i4[:], [[0, 2], [1, 4]], 0, 0, "i4")
    count(T.idn[:], [[1, 128]], 0, -1, "idn")
    count(T.rr[:], [[0, MW // 16], [1, 16]], 0, 0, "rr")
    count(T.gq[:], [[1, 8], [0, 4]], 0, 0, "gq")
    op("g", lambda: g.iota(T.ui[:], [[16, 8]], 0, 0), w=["ui"])
    count(T.ng[:], [[0, Q4]], int(DOWN) // 64, 0, "ng")
    count(T.ct[:], [[0, 512]], 0, 0, "ct")
    count(T.rs[:], [[0, C]], 4096, 0, "rs")
    op("v", lambda: V.memset(T.et[:], 0.0), w=["et"])
    ts(T.pi[:, 1:2], T.pi[:, 0:1], 15, None, A.bitwise_and, None, ["pi0"], ["pi1"])
    ts(T.pi[:, 2:3], T.pi[:, 0:1], 2, 3, A.logical_shift_right, A.bitwise_and, ["pi0"], ["pi2"])
    ts(T.pi[:, 3:4], T.pi[:, 0:1], 3, None, A.bitwise_and, None, ["pi0"], ["pi3"])
    ts(T.pi[:, 4:5], T.pi[:, 0:1], 4, None, A.logical_shift_right, None, ["pi0"], ["pi4"])
    quant(T.qf, T.sf, 0, 128, T.et[:, 0:512], ["et"], qfk(0, 32))
    copy("v", T.pf[:, 0:4], T.pi[:, 1:5], ["pi1", "pi2", "pi3", "pi4"], ["pf"])
    quant(T.qf, T.sf, (NP - 1) * Q4, NP * Q4 + 16, T.et[:, 0:512], ["et"], qfk(NB * (NP - 1), NB * NP + 4))
    ts(T.ka[:, 0:8], T.i4[:], T.pf[:, 1:2], UP, A.is_equal, A.mult, ["i4", "pf"], ["ka0"])
    ts(T.ka[:, 8:16], T.i4[:], T.pf[:, 1:2], 64.0, A.is_equal, A.mult, ["i4", "pf"], ["ka1"])
    ts(T.et[:, 3:515:4], T.idn[:], 0.0, None, A.is_equal, None, ["idn"], ["et"])
    ts(T.m01[:], T.rr[:], T.pf[:, 0:1], None, A.is_equal, None, ["rr", "pf"], ["m01"])
    ts(T.gm[:], T.gq[:], T.pf[:, 3:4], -1.0, A.is_equal, A.mult, ["gq", "pf"], ["gm"])
    copy("v", T.uo[:], T.ui[:], ["ui"], ["uo"])

    I = F.Identity
    mh = ["mh%d" % i for i in range(4)]
    mz = ["mz%d" % i for i in range(NB)]
    act(T.pf[:, 4:5], T.pf[:, 0:1], I, ["pf"], ["pf4"], bias=H - UP)
    act(T.pf[:, 5:6], T.pf[:, 2:3], I, ["pf"], ["pf5"], bias=4 * (256 - UP))
    act(T.mrs[:], T.rr[:], I, ["rr"], ["mrs"], bias=BIG, scale=-2 * BIG)
    act(T.pf[:, 8:9], T.ka[:, 0:1], I, ["ka0", "pf4"], ["cr"], bias=T.pf[:, 4:5], scale=-DOWN / UP)
    act(T.pf[:, 9:10], T.ka[:, 0:1], I, ["ka0", "pf5"], ["cx"], bias=T.pf[:, 5:6], scale=-4 * DOWN / UP)
    act(T.mpm[:], T.m01[:], I, ["m01"], ["mpm"], bias=BIG, scale=-2 * BIG)
    for i in range(4):
        act(T.mh[:, i:C:4], T.ng[:], I, ["ng", "ka0", "ka1"], [mh[i]], bias=T.ka[:, i:i + 1], scale=T.ka[:, 9 + i:10 + i])
    act(T.pf[:, 6:7], T.mh[:, 3:4], I, mh, ["pf6"], bias=-16.0)
    stay(*[k for k in born if k[0] != "X"])

    def quant_x(lo, hi, key):
        quant(T.qx, T.sx, lo, hi, T.X[:, 4 * lo:4 * hi], xk(lo, hi) + (["pt"] if now[0] else []), [key])

    def mm(b, lq, ls, rq, rs, m, r):
        holds[b] = r[-1]
        op("p", lambda: g.tensor.matmul_mx(bank(b, m), lq, ls, rq, rs, True, True), r=r, w=["bk%d" % b])

    def patch():
        copy("v", T.X[:].indirect(T.ob[:]), T.ds[:], ["ds0", "ds1", "ob"], xk(0, C) + ["pt"])

    def pick(out, src, lo, hi, r, w):
        scan(out, src, T.mh[:, lo:hi], DOWN, A.max, A.add, r + mh, w)

    def offsets(out, src, r, w):
        ts(out, src, 4.0, T.pf[:, 9:10], A.mult, A.add, r + ["cx"], w)

    for t in range(R):
        Y, qy, sy, qn, sn, ls, ln = (T[k + str(t)] for k in ("Y", "qy", "sy", "qn", "sn", "ls", "ln"))
        words = FRONT[min(t, len(FRONT) - 1)].split()
        his = [int(w[1:3]) for w in words if w[0] == "n"]
        base = {}
        dgs = [w for w in words if w[0] == "d"]
        todo, whole = list(range(NP - 1, -1, -1)), set(range(HB)) | set(range(NB * NP, NB * NP + 4))

        def qyk(lo, hi):
            return ["qy%d%d" % (t, i) for i in parts(lo, hi)]

        def sco(banks, lo, hi):
            b = [i for i in banks if i in base and base[i][0] <= lo and hi <= base[i][1]][0]
            return bank(b, hi - base[b][0], lo - base[b][0]), ["bk%d" % b]

        def sk(lo, hi):
            return ["S%d" % i for i in range(lo // 16, hi // 16)]

        def fk(c):
            return [("h%d_%d" if c in his else "f%d_%d") % (c, k) for k in range(2) if side(c, k)[1] > side(c, k)[0]]

        def unpack(b):
            act(T.dall[:, b:4 * C:4], bank(4 + b, C), F.Copy, [], ["dall%d" % b], ["bk%d" % (4 + b)])

        def gather(q, lo, hi):
            copy(q, T.X[:, 4 * lo:4 * hi], Y[:].indirect(T.ox[:, lo // 4:hi // 4]),
                 ["Y%d%d%d" % (t, b, i) for b in range(4) for i in range(NH)] + ["ox"], xk(lo, hi))

        for word in words:
            k, q, z = word[0], word[1], word[2:]
            if k == "p":
                patch()
            elif k == "x":
                quant_x(*PART[int(q)], "qx" + q)
            elif k == "l":
                b, (lo, hi) = int(q), PART[int(z)]
                mm(b, T.qw[:, 128 * b:128 * b + 128], T.sw[:, 128 * b:128 * b + 128],
                   T.qx[:, lo:hi], T.sx[:, lo:hi], hi - lo, ["w" + q, "sw", "qx" + z])
            elif k == "y":
                b, (lo, hi) = int(z[0]), PART[int(z[1])]
                assert holds[b] == "qx" + z[1] and born["bk" + z[0]] == now[0]
                out, src, key = Y[:, 4 * lo + b:4 * hi:4], bank(b, hi - lo), "Y%d%s" % (t, z)
                if q == "a":
                    act(out, src, F.Copy, [], [key], ["bk" + z[0]], scale=0.03125)
                else:
                    op("v", lambda: V.tensor_scalar(out, src, 0.03125, None, A.mult), x=["bk" + z[0]], w=[key])
                stay(key)
            elif k == "q":
                lo, hi = PART[int(q)]
                quant(qy, sy, lo, hi, Y[:, 4 * lo:4 * hi], ["Y%d%d%s" % (t, b, q) for b in range(4)], ["qy%d%s" % (t, q)])
            elif k == "P":
                lo, hi = base[int(q)] = span(z[1:])
                mm(int(q), T.qu2[:], T.su2[:], qy[:, lo:hi], sy[:, lo:hi], hi - lo, ["qu2", "su2"] + qyk(lo, hi))
            elif k == "m":
                lo, hi = span(q + z)
                p, x = sco((4, 5), lo, hi)
                tt(T.d1[:, lo:hi], p, T.mpm[:, 0:hi - lo], A.max, ["mpm"], ["d1%d" % lo], x)
            elif k == "s":
                lo, hi = span(q + z)
                scan(T.S[:, lo:hi], T.mrs[:, 0:hi - lo], T.d1[:, lo:hi], BIG, A.max, A.min, ["mrs", "d1%d" % lo], sk(lo, hi))
            elif k == "d":
                lo, hi = span(q + z)
                at = lo + (C if lo < H else 0)
                p, x = sco((4, 5), lo, hi)
                tt(T.fl[:, at:at + hi - lo], p, T.S[:, lo:hi], A.is_gt, sk(lo, hi), [word], x)
            elif k == "r":
                lo, at = (0, C) if q == "A" else (H, H)
                scan(T.fr[:, lo:lo + H], T.rs[:, lo:lo + H], T.fl[:, at:at + H], 4096.0, A.min, A.add,
                     ["rs" + q] + [d for d in dgs if (span(d[1:])[0] < H) == (q == "A")], ["fr" + q])
            elif k == "u":
                quant(T.qu, T.su, 0, 128, T.ut[:], ["ut"], ["qu"])
                copy("v", T.qu2[:].bitcast(u32), T.qu[:].bitcast(u32).indirect(T.uo[:]), ["qu", "uo"], ["qu2"])
                copy("a", T.su2[:], T.su[:].indirect(T.uo[:]), ["qu", "uo"], ["su2"])
                stay("qu2", "su2")
            elif k == "i":
                count(T.jc[:], [[1, C]], -256, 0, "jc")
                count(T.o[:, C:512], [[0, K]], -256, 0, "o_x")
                stay("jc", "o_x")
            elif k == "j":
                for i in range(4):
                    act(T.ct[:, 5 * i:512:16], T.gm[:], F.Copy, ["gm", "ct"], ["ct%d" % i])
            elif k == "J":
                act(T.rs[:, 0:H:16], T.rr[:, 0:HB], I, ["rr", "rs", "pf6"], ["rsA"], bias=T.pf[:, 6:7], scale=0.0)
                act(T.rs[:, H:C:16], T.rr[:, 0:HB], I, ["rr", "rs"] + mh, ["rsB"], bias=T.mh[:, 3:4], scale=0.0)
                act(T.mz[:], T.mh[:, 0:Q4], F.Copy, mh, mz)
                stay("rsA", "rsB")
            elif k == "e":
                i = int(q)
                quant(T.qe, T.se, 128 * i, 128 * i + 128, T.et[:, 3 - i:515 - i], ["et"], [word])
                stay(word)
            elif k == "c":
                quant(T.qc, T.sc, 0, 128, T.ct[:], ["ct%d" % i for i in range(4)], ["qc"])
                stay("qc")
            elif k in "fnN":
                c, e = int(word[1:3]), int(word[3])
                lo, hi, at = side(c, e)
                v, own = T.fl[:, 16 * at:16 * (at + hi - lo)], T.S[:, 16 * c + 15:16 * c + 16]
                w = ["f%d_%d" % (c, e), "h%d_%d" % (c, e)]
                if k == "N" and e:
                    act(v, v, F.Sign, w[:1], w + ["ra%d" % c], bias=1.0, scale=-1.0, accum_out=T.ra[:, c:c + 1])
                elif k == "N":
                    act(v, v, F.Relu, w[:1], w + ["ra%d" % c], scale=-1.0, accum_out=T.ra[:, c:c + 1])
                elif k == "n":
                    p, x = sco((6, 7), 16 * lo, 16 * hi)
                    act(v, p, F.Sign, ["S%d" % c], w, x, bias=own, scale=-1.0)
                    born[w[1]] = -2
                else:
                    p, x = sco((4, 5), 16 * lo, 16 * hi)
                    op("v", lambda: V.tensor_scalar(v, p, own, None, A.is_ge if e else A.is_gt), r=["S%d" % c], w=w, x=x)
            elif k == "F":
                c = int(q + z)
                s, m = cell(c)
                scan(T.rj[:, Q4 * (c + 1) - 8 * m:Q4 * (c + 1)], T.fl[:, 16 * s:16 * s + 8 * m], T.fl[:, 16 * s + 8 * m:16 * (s + m)],
                     0.0, A.add, A.add, fk(c), ["rj%d" % c])
            elif k == "Q":
                lo, hi = PIECES[int(q + z)]
                r = [i for c in range(NB) for e in range(2) for i in fk(c)
                     if i[-1] == str(e) and side(c, e)[2] < hi and side(c, e)[2] + side(c, e)[1] - side(c, e)[0] > lo]
                quant(T.qf, T.sf, 4 * lo, 4 * hi, T.fl[:, 16 * lo:16 * hi], r + (dgs if lo < 3 * HB else []), qfk(lo, hi))
                stay(*qfk(lo, hi))
                whole.update(range(lo, hi))
                for s in [s for s in todo if whole.issuperset(range(NB * s, NB * s + 32))]:
                    first = len(todo) == NP
                    assert not first or all(born.get("Y%d0%d" % (t, h)) == -1 for h in range(NH))
                    todo.remove(s)
                    op("p", lambda: g.tensor.matmul_mx(bank(0, 128), T.qc[:], T.sc[:], T.qf[:, Q4 * s:Q4 * s + 128], T.sf[:, Q4 * s:Q4 * s + 128],
                                                       first, not todo),
                       r=["qc"] + qfk(NB * s, NB * s + 32), w=["bk0"] if first else [], s=["bk0"])
            elif k == "M":
                lo, hi = span(q + z)
                fr = ["frA"] * (lo < HB) + ["frB"] * (hi > HB)
                src, key = (T.ra[:, lo:hi], "ra%d") if lo in his else (T.rj[:, Q4 * (lo + 1) - 1:Q4 * hi:Q4], "rj%d")
                tt(T.mz[:, 4 * lo + 3:4 * hi:4], src, T.fr[:, 16 * lo + 15:16 * hi:16], A.add, fr + [key % c for c in range(lo, hi)], mz[lo:hi])
            elif k == "t":
                lo, hi = span(q + z)
                send(qn[:, lo:hi].bitcast(u8), qy[:, lo:hi].bitcast(u8), "aq%d" % t, qyk(lo, hi))
            elif k == "T":
                send(sn[:], sy[:], "aq%d" % t, qyk(0, C))
        assert not todo

        wr["qn%d" % t], born["qn%d" % t] = ("aq%d" % t, len([w for w in words if w[0] in "tT"]) * back), -1
        for b in range(4):
            mm(4 + b, T.qe[:, 128 * b:128 * b + 128], T.se[:, 128 * b:128 * b + 128], qn[:], sn[:], C, ["e%d" % b, "qn%d" % t])
        for b in range(3):
            unpack(b)
        scan(T.zz[:], bank(0, Q4), T.mz[:], DOWN, A.max, A.add, mz, ["zz"], ["bk0"])
        ts(T.oi[:, 0:NB], T.zz[:, 3:Q4:4], T.pf[:, 8:9], None, A.add, None, ["zz", "cr"], ["oi"])

        copy("v", T.o[:, 0:C].indirect(T.oi[:, 0:NB]), T.jc[:], ["oi", "jc"], ["o"])
        pick(T.t2[:], T.o[:, 0:K], 0, K, ["o"], ["t2"])
        pick(T.b2[:], T.o[:, C - K:C], 0, K, ["o"], ["b2"])
        offsets(ls[:], T.t2[:, 3:K:4], ["t2"], ["ls%d" % t])
        send(ln[:], ls[:], "al%d" % t, ["ls%d" % t])
        wr["ln%d" % t], born["ln%d" % t] = ("al%d" % t, back), -1

        copy("v", T.e1[:, 0:16 * EV], T.o[:, K:512].indirect(T.oi[:, 0:EV]), ["o", "o_x", "oi"], ["e1a"])
        copy("a", T.e1[:, 16 * EV:C], T.o[:, K:512].indirect(T.oi[:, EV:NB]), ["o", "o_x", "oi"], ["e1b"])
        unpack(3)
        if t == R - 1:
            act(T.of[:], T.o[:, 0:C], I, ["o"], ["of"], bias=256.0)
            dma("s", T.ol[:], T.of[0:128:16, :], r=["of"])
        stay("b2", "dall0", "dall1", "dall2", "dall3", "e1a", "e1b")
        now[0] += 1
        offsets(T.ob[:], T.b2[:, 3:K:4], ["b2"], ["ob"])
        pick(T.e2[:], T.e1[:], 0, C, ["e1a", "e1b"], ["e2"])
        if t == 0:
            quant(T.qv, T.sv, 0, 128, T.vt[:], ["vt"], ["qv"])
            stay("qv")
        offsets(T.ox[:], T.e2[:, 3:C:4], ["e2"], ["ox"])
        gather("a", 0, SHARE)
        gather("v", SHARE, C)
        for i, q in enumerate("va"):
            copy(q, T.ds[:, 128 * i:128 * i + 128], T.dall[:].indirect(ln[:, 8 * i:8 * i + 8]),
                 ["dall%d" % b for b in range(4)] + ["ln%d" % t], ["ds%d" % i])

    order("v", (), ["qx%d" % h for h in range(NH)], ())
    patch()
    for h, q in enumerate("av"):
        lo, hi = OUT[h]
        quant_x(lo, hi, "qo%d" % h)
        mm(h, T.qv[:], T.sv[:], T.qx[:, lo:hi], T.sx[:, lo:hi], hi - lo, ["qv", "qo%d" % h])
        if h:
            dma("s", T.oc[:], T.qx[:].bitcast(u8), r=["qo0", "qo1"])
        copy(q, T.yo[:, lo:hi], bank(h, hi - lo), [], ["yo%d" % h], ["bk%d" % h])
    for h, q in enumerate("as"):
        lo, hi = OUT[h]
        dma(q, T.y[:, lo:hi], T.yo[:, lo:hi], r=["yo%d" % h])
    for k in range(4):
        dma("a" if k < 2 else "s", T.osc[4 * k:4 * k + 4, :], T.sx[32 * k:32 * k + 4, :], r=["qo0", "qo1"])

    for q in cnt:
        wait("g", (csem[q], cnt[q]))
    for h in dmas:
        wait("g", h)
    wait("g", ("sent", sent[0]))
